import numpy as np, ml_dtypes
CORES = [25,29,65,69,153,157,193,197]
N = 8
BF = ml_dtypes.bfloat16
T0, L, M, RO, KILL, HOPS, TILE = 1024, 256, 3, 5, 200, [1, 4, 1, 4], [0, 1, 2, 1, 2]
NS, GB, W = L * M, T0 + L * RO, T0 + L * (2 * RO - 1)
LAST = NS - M + max(TILE)
R4 = np.arange(N).reshape(N, 1, 1, 1); G4 = np.arange(8).reshape(1, 8, 1, 1); R3 = R4[..., 0]; G3 = G4[..., 0]
def members(rng, of, cl, k):
    tab = np.argsort(of, axis=-1, kind="stable").reshape(N, 8, 32, -1)
    return tab[R4, G4, cl[:, :, None, :], rng.integers(0, tab.shape[3], (N, 8, k, cl.shape[2]))]
def around(rng, cen, cl):
    n = cl.shape[2]; w = rng.choice(np.array([2, 6, 10]), (N, 8, n, 1))
    p = cen[R3, G3, cl] + np.rint(w * (2 * rng.random((N, 8, n, 16)) - 1)).astype(np.int64)
    return np.ascontiguousarray(np.clip(p, 0, 63).transpose(0, 1, 3, 2))
def parts(rng):
    cen = np.where(rng.random((N, 8, 32, 1)) < 0.7, rng.integers(0, 64, (1, 8, 32, 16)), rng.integers(0, 64, (N, 8, 32, 16)))
    cv = np.argsort(rng.random((N, 8, T0)), axis=-1) % 32; cz = np.argsort(rng.random((N, 8, NS)), axis=-1) % 32
    two = rng.permutation(8)[:2]; cz[:, two] = np.repeat(np.argsort(rng.random((2, L)), axis=-1) % 32, M, axis=1)
    V = around(rng, cen, cv); Z = around(rng, cen, cz)
    stray = rng.choice(np.array([0.0, 0.1, 0.1, 0.5, 0.5]), (N, 8, 1, NS))
    S = np.where(rng.random((N, 8, 16, NS)) < stray, rng.integers(0, T0, (N, 8, 16, NS)), members(rng, cv, cz, 16))
    Q = np.where(rng.random((N, 8, 16, T0)) < 0.4, rng.integers(0, NS, (N, 8, 16, T0)), members(rng, cz, cv, 16))
    Q[R4, G4, np.arange(5).reshape(1, 1, 5, 1), S[:, :, :5]] = np.arange(NS)
    u = rng.random((N, 8, T0))
    kid = np.where(u < 0.15, np.arange(T0), np.where(u < 0.4, rng.integers(0, T0, (N, 8, T0)), members(rng, cv, cv, 1)[:, :, 0]))
    u = rng.random((N, 8, NS)); best = np.take_along_axis(S, rng.integers(0, 16, (N, 8, 1, NS)), 2)[:, :, 0]
    best = np.where(u < 0.07, -1, np.where(u < 0.2, rng.integers(0, T0, (N, 8, NS)), best))
    return V, Z, S, Q, kid, best
def pack(V, Z, S, Q, kid, best):
    def p(x): return np.ascontiguousarray(x).reshape(N, 128, -1)
    return {"vn": p(V).astype(np.float32).astype(BF), "zs": p(Z).astype(np.float32).astype(BF), "sn": p(S).astype(np.int32), "nq": p(Q).astype(np.int32),
            "kid": np.ascontiguousarray(kid).astype(np.int32), "bst": np.ascontiguousarray(best).astype(np.int32)}
def setup_inputs(rng):
    return pack(*parts(rng))
def setup_inputs_spread(rng):
    def pts(n):
        x = np.minimum((np.exp2(6 * rng.random((N, 8, 1, n))) * rng.random((N, 8, 16, n))).astype(np.int64), 63)
        return np.where(rng.random((N, 8, 1, n)) < 0.5, x, 63 - x)
    def lst(n, k, hi):
        return np.minimum((hi * rng.random((N, 8, k, n)) ** rng.choice(np.array([1.0, 2.0, 6.0]), (N, 8, 1, n))).astype(np.int64), hi - 1)
    return pack(pts(T0), pts(NS), lst(NS, 16, T0), lst(T0, 16, NS), lst(T0, 1, T0)[:, :, 0], lst(NS, 1, T0 + 1)[:, :, 0] - 1)
def edge(rng, shape, lo, hi, by):
    m = rng.choice(np.array([0.0, 0.5, 0.5, 1.0]), shape[:-2] + (1, shape[-1]))
    return np.where(rng.random(by) < 0.2, rng.integers(lo, hi + 1, shape), np.where(rng.random(shape) < m, hi, lo))
def setup_inputs_ends(rng):
    V = edge(rng, (N, 8, 16, T0), 0, 63, (N, 8, 1, T0)); Z = edge(rng, (N, 8, 16, NS), 0, 63, (N, 8, 1, NS))
    S = edge(rng, (N, 8, 16, NS), 0, T0 - 1, (N, 8, 16, NS)); Q = edge(rng, (N, 8, 16, T0), 0, NS - 1, (N, 8, 16, T0))
    kid = edge(rng, (N, 8, 1, T0), 0, T0 - 1, (N, 8, 1, T0))[:, :, 0]; best = edge(rng, (N, 8, 1, NS), -1, T0 - 1, (N, 8, 1, NS))[:, :, 0]
    for q in range(N):
        for g in range(8):
            hi = 63 if g % 2 == 0 else 0; own = (g // 2) % 2 == 1
            V[q, g, :, 0] = 63 - hi; V[q, g, :, [3, 8, T0 - 1]] = hi
            kid[q, g, 0] = 0 if own else T0 - 1; kid[q, g, T0 - 1] = T0 - 1 if own else 0; kid[q, g, 3] = 3; kid[q, g, 8] = 8
            Z[q, g, :, LAST] = hi; S[q, g, :, LAST] = 0; S[q, g, 4, LAST] = 3; S[q, g, 9, LAST] = 8; S[q, g, 15, LAST] = T0 - 1
            Z[q, g, :, LAST - 1] = 63 - hi; S[q, g, :, LAST - 1] = T0 - 1; Z[q, g, :, 0] = hi; S[q, g, :, 0] = 0
            Q[q, g, :, 3] = LAST; Q[q, g, :, T0 - 1] = LAST - 1
    return pack(V, Z, S, Q, kid, best)
def setup_inputs_corners(rng):
    V, Z, S, Q, kid, best = parts(rng); sh = int(rng.integers(0, 8))
    for q in range(N):
        for g in range(8):
            c = (g + q + sh) % 8
            if c == 0:
                kid[q, g] = np.arange(T0); best[q, g] = -1
            elif c == 1:
                kid[q, g] = 0; best[q, g] = 0; S[q, g, :, ::3] = 0
            elif c == 2:
                kid[q, g] = T0 - 1; best[q, g] = T0 - 1; S[q, g, :, 1::3] = T0 - 1
            elif c == 3:
                kid[q, g] = (np.arange(T0) + 1) % T0
            elif c == 4:
                o = rng.permutation(T0)[:6]; kid[q, g, o] = o; Z[q, g] = 0
                for j in range(6):
                    s = KILL - 1 + j // 2; x = np.full(16, s // 16); x[rng.permutation(16)[:s % 16]] += 1; V[q, g, :, o[j]] = x
                typ = rng.integers(0, 5, NS); s = o[rng.integers(0, 2, (16, NS))]
                s = np.where((np.arange(16)[:, None] == rng.integers(0, 16, NS)) & (typ == 1), o[2], s); s = np.where(typ == 2, o[3], s)
                s = np.where(typ == 3, o[rng.integers(0, 6, (16, NS))], s); S[q, g] = np.where(typ == 4, S[q, g], s)
            elif c == 5:
                S[q, g] = np.arange(NS); Q[q, g] = np.arange(T0) % NS; kid[q, g, ::2] = np.arange(0, T0, 2)
            elif c == 6:
                V[q, g] = rng.choice(np.array([0, 1, 62, 63]), (16, T0)); Z[q, g] = rng.choice(np.array([0, 63]), (16, NS))
                S[q, g, :, ::2] = rng.choice(np.array([0, T0 - 1]), (16, (NS + 1) // 2))
                o = rng.permutation(T0)[:10]; kid[q, g, o] = o; kid[q, g, o[8]] = o[7]; flip = (q + g) % 2 == 1
                for j in range(10):
                    x = 63 - (rng.permutation(16) < 8 - j); V[q, g, :, o[j]] = 63 - x if flip else x
                far = (np.arange(NS) // M) % 2 == 1; least = (np.arange(NS) // (2 * M)) % 10
                Z[q, g] = np.where(far, 63 if flip else 0, Z[q, g]); S[q, g] = np.where(far, o[rng.integers(least, 10, (16, NS))], S[q, g])
            else:
                Q[q, g] = rng.choice(np.array([0, NS - 1]), (16, T0)); best[q, g] = rng.choice(np.array([-1, 0, T0 - 1]), NS)
    return pack(V, Z, S, Q, kid, best)
def setup_inputs_crowd(rng):
    V, Z, S, Q, kid, best = parts(rng); sh = int(rng.integers(0, 8)); e = NS - M
    for q in range(N):
        for g in range(8):
            c = (g + sh) % 8; p = T0 - 1 if (q + g) % 2 else int(rng.integers(1, T0 - 1)); o = (p + 1) % T0
            kid[q, g, p] = p; kid[q, g, o] = o; V[q, g, :, p] = 0
            if c in (0, 1, 5):
                Z[q, g] = np.maximum(Z[q, g], 20); S[q, g] = p
            if c == 1: S[q, g, :, e:] = o
            if c in (2, 3):
                Z[q, g] = rng.integers(0, 4, (16, NS)); S[q, g] = p
            if c == 2: Z[q, g, :, e:] = 63
            if c == 4: S[q, g] = rng.choice(np.array([p, o, (p + 2) % T0]), (16, NS))
            if c == 5:
                Q[q, g, :, p] = NS - 1; best[q, g, NS - 1] = p
            if c >= 6:
                V[q, g, :, p] = 31; S[q, g] = p
                Z[q, g] = np.where(rng.random((1, NS)) < 0.5, rng.integers(50, 64, (16, NS)), rng.integers(0, 13, (16, NS))); Z[q, g, :, NS - 1] = 63; Z[q, g, :, 0] = 0
                best[q, g, 0] = p; best[q, g, NS - 1] = p; Q[q, g, :, p] = NS - 1; Q[q, g, (15 if c == 6 else 8):, p] = 0
            if c == 7:
                Z[q, g, :, 1] = 31
                if q % 4 == 3: Q[q, g, 0, p] = 1
                else: Q[q, g, 16 - q % 4:, p] = 1
    return pack(V, Z, S, Q, kid, best)
def setup_inputs_ties(rng):
    V, Z, S, Q, kid, best = parts(rng)
    pts = rng.integers(0, 64, (8, 48, 16)); pts[1::2] = 20 + 25 * (pts[1::2] % 2)
    few = rng.choice(np.array([3, 6, 16, 48]), (N, 8, 1))
    V = pts[G3, rng.integers(0, 48, (N, 8, T0)) % few].transpose(0, 1, 3, 2); Z = pts[G3, rng.integers(0, 48, (N, 8, NS))].transpose(0, 1, 3, 2)
    return pack(V, Z, S, Q, kid, best)
def check_inputs(d):
    bad = []
    for k, lo, hi in (("vn", 0, 63), ("zs", 0, 63), ("sn", 0, T0 - 1), ("nq", 0, NS - 1), ("kid", 0, T0 - 1), ("bst", -1, T0 - 1)):
        x = np.asarray(d[k]).astype(np.float64)
        if not (np.min(x) >= lo and np.max(x) <= hi and np.all(x == np.floor(x))): bad.append("range of " + k)
    return bad
def columns(x):
    return np.ascontiguousarray(x.astype(np.float32).astype(np.int32).reshape(N, 8, 16, -1).transpose(0, 1, 3, 2))
def rows(x):
    return np.ascontiguousarray(x.transpose(0, 1, 3, 2)).reshape(N, 128, -1)
def dist(a, b):
    return np.add.reduce(np.abs(a - b), axis=-1)
def reference(vn, zs, sn, nq, kid, bst):
    V = np.zeros((N, 8, W, 16), np.int32); V[:, :, :T0] = columns(vn); Z = columns(zs); S = columns(sn)
    Q = np.zeros((N, 8, W, 16), np.int32); Q[:, :, :T0] = columns(nq)
    child = np.tile(np.arange(W), (N, 8, 1)); child[:, :, :T0] = kid
    best = bst.astype(np.int64); lane = np.arange(L)
    for t in range(RO):
        v = M * lane + TILE[t]; z = Z[:, :, v]; z1 = z[:, :, :, None, :]; s = S[:, :, v].astype(np.int64)
        e = child[R4, G4, s]
        ds = dist(V[R4, G4, s], z1); de = dist(V[R4, G4, e], z1)
        s = np.where(de < ds, e, s); d = np.minimum(ds, de)
        if t > 0:
            m = GB + L * (t - 1) + lane; dm = dist(V[:, :, m], z)
            put = (np.arange(16) == np.argmax(d, axis=3)[..., None]) & (dm < np.max(d, axis=3))[..., None]
            s = np.where(put, m[:, None], s); d = np.where(put, dm[..., None], d)
        S[:, :, v] = s
        b = np.argmin(d, axis=3); a = np.take_along_axis(s, b[..., None], 3)[..., 0]
        live = np.max(d, axis=3) >= KILL
        best[:, :, v] = np.where(live, a, -1)
        va = V[R3, G3, a]; va1 = va[:, :, :, None, :]; qa = Q[R3, G3, a]
        bq = best[R4, G4, qa]; zq = Z[R4, G4, qa]
        att = (bq >= 0) & ((bq == a[..., None]) | (dist(V[R4, G4, np.maximum(bq, 0)], va1) >= dist(zq, va1)))
        pull = np.add.reduce(np.where(att[..., None], np.clip(zq - va1, -1, 1), 0), axis=3)
        new = np.clip(va + np.clip(pull, -2, 2), 0, 63); n = T0 + L * t + lane
        V[:, :, n] = new
        low = np.full((N, 8, W), L); np.minimum.at(low, (R3, G3, a), np.where(live, lane, L))
        child = np.where(low < L, T0 + L * t + low, child)
        if t < RO - 1:
            Q[:, :, n] = qa; m = GB + L * t + lane
            V[:, :, m] = np.roll(new, HOPS[t], axis=0); Q[:, :, m] = np.roll(qa, HOPS[t], axis=0)
    h = NS // 2
    return {"yv": rows(V[:, :, T0:GB]).astype(np.float32).astype(BF), "ys": rows(S[:, :, :h] + 4096 * S[:, :, h:]).astype(np.float32), "yk": child.astype(np.float32), "yb": best.astype(np.float32)}

@@ -1,0 +1,806 @@
+import numpy as np
+from concourse.mybir import AluOpType, ActivationFunctionType
+
+A = AluOpType
+AF = ActivationFunctionType
+TILE = [0, 1, 2, 1, 2]
+HOP = [1, 4, 1, 4]
+T0, L, GB, W = 1024, 256, 2304, 3328
+PAD = 256
+WT = PAD + W
+MAGIC = 1.5 * 2.0 ** 36
+BIG = 2.0 ** 26
+KOFF = -2040.0 * 8192.0
+CEN = 3700.0
+NSMALL = 2
+VSIGN = ()
+CYC, CPE, WAKE, LREM, GAT, SCA = 0.00104, 0.00052, 0.06, 4.0, 1.56, 3.8
+PASSES, ROUNDS, BLEND, SEED, JIT = 1, 12, 0.3, 0, 0.3
+STEP4 = [(1, "D1", 0), (1, "D1", 1), (1, "D2", 0), (1, "D2", 1), (0, "D1", 0), (1,), (0, "D1", 1), (0, "D2", 0), (0, "D2", 1)]
+SDUP = ()
+SQUAD = (0, 0, 2, 2, 2)
+PG, PA = 256, 512
+ORDER = {}
+
+f32, b16, i32, u16 = "float32", "bfloat16", "int32", "uint16"
+SCRATCH = {}
+for _n, _w, _d in [
+    ("VN", 1024, b16), ("ZS", 768, b16), ("ZT", 768, b16), ("ZB", 768, b16), ("SN", 768, i32), ("NQ", 1024, i32),
+    ("KC", 64, i32), ("KF", 96, f32), ("KLO", 64, b16), ("KHI", 64, b16), ("KI", 64, i32), ("BC", 48, i32), ("BCF", 48, f32),
+    ("BR", 768, f32), ("KO", 64, u16), ("BO", 48, u16), ("VCB", 1024, b16),
+    ("QT", W, f32), ("VP", WT, f32), ("VC", WT, f32), ("AUX", WT, f32), ("IO", WT, f32), ("VB", 768, f32),
+    ("IDB", 2304, b16), ("IC", 144, i32), ("IC2", 144, i32), ("ILO", 144, b16), ("IHI", 144, b16), ("GA", 1024, b16), ("GC", 1024, b16),
+    ("D1", 4096, b16), ("D2", 4096, b16), ("A1", 4096, b16), ("A2", 4096, b16), ("ZX0", 4096, b16), ("ZX1", 4096, b16), ("FW", 2048, b16),
+    ("B0", 144, b16), ("WM", 144, b16), ("WN", 144, b16), ("WP", 144, b16), ("WA", 144, b16), ("WA0", 144, b16), ("WA2", 144, b16), ("BF", 144, f32),
+    ("ID", 128, b16), ("NI", 128, b16), ("CI", 128, b16), ("M1", 128, b16), ("M2", 128, b16), ("P2", 128, b16), ("IDF", 128, f32), ("NIF", 128, f32), ("RB", 512, b16), ("GZ", 1024, b16), ("ONE", 144, b16),
+    ("PI", 8, i32), ("CL", 24, f32), ("TI", 16, i32), ("TF", 16, f32), ("TG", 16, f32), ("TH", 16, f32),
+    ("LMK", 16, u16), ("LKM", 16, u16), ("LK", 4, u16), ("LB", 16, u16), ("LB2", 32, u16), ("LX", 2, u16), ("LI", 16, f32),
+    ("TRI", 512, f32), ("RMAX", 256, b16), ("RMIN", 256, b16), ("RZ", 256, b16), ("RZ2", 512, b16), ("KA", 256, f32), ("KB", 256, f32),
+    ("THR", 48, f32), ("NF", 288, f32), ("QN", 288, f32), ("Y", 544, f32), ("KS", 768, f32), ("SO", 768, u16), ("QO", 256, u16),
+    ("DP", 256, f32), ("SM", 256, f32), ("E", 256, f32), ("E2", 256, f32),
+    ("S1", 16, i32), ("S2", 16, i32), ("AI", 16, i32), ("A16", 16, u16), ("KM", 16, f32), ("LV", 16, f32), ("U", 16, f32), ("U2", 16, f32),
+    ("AD", 16, f32), ("AD16", 16, u16), ("OX", 32, u16), ("O1", 16, u16), ("X1", 512, f32), ("X2", 512, f32), ("SI", 256, i32), ("SI2", 256, i32),
+    ("XG", 256, b16), ("LAND", 1024, b16), ("VAB", 1024, b16), ("VAF", 1024, f32),
+    ("D1M", 256, f32), ("N1", 256, b16), ("N3", 256, b16), ("NA", 256, b16), ("CN", 16, b16), ("H1", 256, b16), ("YV", 1280, b16),
+    ("AXN", 512, f32), ("YS", 384, f32), ("YB", 768, f32),
+]:
+    SCRATCH[_n] = ("sbuf", [128, _w], _d)
+ALIAS = {"XM": "A1", "XA": "A2", "XS": "D2", "ZX2": "ZX0", "N2": "E2", "KD": "GC"}
+PART = {}
+for _grp in (("KLO", "KHI", "ILO", "IHI"), ("IC", "IC2"), ("U", "U2", "LV"), ("N1", "N3")):
+    _o = 0
+    for _n in _grp:
+        _where, _s, _d = SCRATCH.pop(_n)
+        PART[_n] = ("X" + _grp[0], _o, _s[1])
+        _o += _s[1]
+    SCRATCH["X" + _grp[0]] = ("sbuf", [128, _o], _d)
+SCRATCH["ZG"] = ("sbuf", [128, 16, 256], b16)
+SCRATCH["ZG2"] = ("sbuf", [128, 16, 256], b16)
+SCRATCH["SG"] = ("sbuf", [128, 256, 16], b16)
+SCRATCH["VAU"] = ("sbuf", [128, 16, 16], b16)
+for _j in range(8):
+    SCRATCH["PS%d" % _j] = ("psum", [128, 32, 16] if _j == 3 else [128, 128, 4] if _j in (4, 5, 6) else [128, 512], f32)
+NDMA = 120
+SEMAPHORES = ["cV", "cS", "cT", "cG"] + ["d%d" % _j for _j in range(NDMA)] + ["aq%d" % _j for _j in range(4)] + ["an%d" % _j for _j in range(4)] + ["fwd"]
+MASKS = {}
+
+
+def bits(shape, idx):
+    key = (tuple(shape), repr(idx))
+    if key not in MASKS:
+        n = int(np.prod(shape))
+        m = np.zeros(n, bool)
+        m[np.arange(n).reshape(shape)[idx].reshape(-1)] = True
+        MASKS[key] = int.from_bytes(np.packbits(m).tobytes(), "big")
+    return MASKS[key]
+
+
+def relay_of(T, topo, src, dst):
+    c = [x for x in topo.cores_of(src) if T.rank_of(x) is None and topo.may_write(x, dst)]
+    c.sort(key=lambda x: topo.die(x) != topo.die(src))
+    return c[0]
+
+
+def routes(T, topo):
+    n = len(T.cores)
+    out = []
+    for t in range(4):
+        for r in range(n):
+            s, d = T.cores[r], T.cores[(r + HOP[t]) % n]
+            out.append((t, s, None if topo.may_write(s, d) else relay_of(T, topo, s, d), d))
+    return out
+
+
+def qslot(T, t):
+    return T["QT"][:, GB + L * t:GB + L * t + L]
+
+
+def nslot(T, t):
+    return T["LAND"][:, L * t:L * t + L]
+
+
+def relay_program(g, core, T, topo):
+    sent = 0
+    for t, s, via, d in routes(T, topo):
+        if via != core:
+            continue
+        n_in = len(topo.engines(s, core))
+        rid, pid = topo.addr(d, core)
+        for sem, ap in (("aq%d" % t, qslot(T, t)), ("an%d" % t, nslot(T, t))):
+            g.wait_ge(T.sem[sem], n_in)
+            g.remote_dma(ap, ap, T.sem[sem], T.sem["fwd"], pid, rid, topo.mask(core, d))
+            sent += len(topo.engines(core, d))
+    if sent:
+        g.wait_ge(T.sem["fwd"], sent)
+
+
+def place(ops, order, edges, first):
+    line = {}
+    start = [0.0] * len(ops)
+    for i in order:
+        o = ops[i]
+        t = max([start[j] + ops[j]["cost"] + d for j, d in edges[i]] + [first[i]])
+        if o["q"]:
+            ln = line.setdefault(o["q"], [])
+            k = len(ln)
+            while k > 0 and ln[k - 1][0] >= t:
+                k -= 1
+            if k > 0:
+                t = max(t, ln[k - 1][1])
+            while k < len(ln) and t + o["cost"] > ln[k][0] + 1e-9:
+                t = max(t, ln[k][1])
+                k += 1
+            ln.insert(k, (t, t + o["cost"], i))
+        start[i] = t
+    return start, {q: [e[2] for e in ln] for q, ln in line.items()}
+
+
+def plan_calls(ops):
+    n = len(ops)
+    acc = {}
+    pred = []
+    for i, o in enumerate(ops):
+        q = o["q"]
+        need = {}
+        if o["ext"]:
+            need[i - 1] = False
+        if o["after"] is not None:
+            need[o["after"]] = False
+        for regs, w in ((o["rd"], False), (o["wr"], True)):
+            for name, cm, pm in regs:
+                ps = name.startswith("PS")
+                for j, cm2, pm2, w2 in acc.get(name, []):
+                    if j == i or not (cm & cm2 and pm & pm2):
+                        continue
+                    same = ops[j]["q"] == q and not ops[j]["dma"] and not o["dma"]
+                    if not (w or w2 or (ps and not same)):
+                        continue
+                    need[j] = not (same and q == "T")
+        for regs, w in ((o["rd"], False), (o["wr"], True)):
+            for name, cm, pm in regs:
+                lst = acc.setdefault(name, [])
+                if w:
+                    lst[:] = [e for e in lst if (e[1] & ~cm) or (e[2] & ~pm) or e[0] == i]
+                lst.append((i, cm, pm, w))
+        pred.append(need)
+    fwd = [[(j, ops[j]["lat"] + (WAKE if s else 0.0)) for j, s in pred[i].items()] for i in range(n)]
+    bwd = [[] for _ in range(n)]
+    for i in range(n):
+        for j, d in fwd[i]:
+            bwd[j].append((i, d))
+    level = [0.0] * n
+    for i in range(n - 1, -1, -1):
+        level[i] = ops[i]["cost"] + max([level[j] + d for j, d in bwd[i]] + [ops[i]["lat"]])
+    zero = [0.0] * n
+    lats = [o["lat"] for o in ops]
+    best_end, seq = None, None
+    for _ in range(ROUNDS):
+        start, sq = place(ops, sorted(range(n), key=lambda i: (-level[i], i)), fwd, zero)
+        first = (start, sq)
+        for p in range(PASSES + 1):
+            end = max(start[i] + ops[i]["cost"] + lats[i] for i in range(n))
+            if best_end is None or end < best_end:
+                best_end, seq, first = end, sq, (start, sq)
+            if p < PASSES:
+                back, _s = place(ops, sorted(range(n), key=lambda i: (-(start[i] + ops[i]["cost"]), -i)), bwd, lats)
+                start, sq = place(ops, sorted(range(n), key=lambda i: (-(back[i] + ops[i]["cost"]), i)), fwd, zero)
+        nxt = {a: b for ln in first[1].values() for a, b in zip(ln, ln[1:])}
+        true = [0.0] * n
+        for i in sorted(range(n), key=lambda i: (-first[0][i], -i)):
+            true[i] = ops[i]["cost"] + max([true[j] + d for j, d in bwd[i]] + [lats[i], true[nxt[i]] if i in nxt else 0.0])
+        level = [(1 - BLEND) * a + BLEND * b for a, b in zip(level, true)]
+        if _ % 3 == 2:
+            jit = np.random.default_rng(SEED + _).uniform(1 - JIT, 1 + JIT, n).tolist()
+            for i in range(n - 1, -1, -1):
+                level[i] = ops[i]["cost"] * jit[i] + max([level[j] + d for j, d in bwd[i]] + [lats[i], 0.98 * true[i]])
+    ORDER["end"] = best_end
+    pos = {}
+    for q in seq:
+        for k, i in enumerate(seq[q]):
+            pos[i] = k
+    wait = [[] for _ in range(n)]
+    for q in seq:
+        seen = {}
+        for i in seq[q]:
+            best = {}
+            for j, s in pred[i].items():
+                if s:
+                    key = ("x", j) if (ops[j]["dma"] or ops[j]["ext"]) else ops[j]["q"]
+                    if key not in best or pos.get(j, 0) > pos.get(best[key], 0):
+                        best[key] = j
+            for key, j in best.items():
+                if seen.get(key, -1) < pos.get(j, 0):
+                    seen[key] = pos.get(j, 0)
+                    wait[i].append(j)
+    return seq, wait
+
+
+def rank_program(g, core, T, topo):
+    if T.rank_of(core) is None:
+        relay_program(g, core, T, topo)
+        return
+    ops = []
+    chain = [False, None]
+    Q = {"V": g.vector, "S": g.scalar, "T": g.tensor, "G": g, "Y": g.sync}
+    ALL = slice(None)
+
+    def R(name, *idx, p=ALL):
+        name = ALIAS.get(name, name)
+        if name in PART:
+            name, o, w = PART[name]
+            s = idx[0] if idx else slice(0, w)
+            idx = (slice(o + s.start, o + s.stop, s.step),)
+        if name not in SCRATCH:
+            return {"ap": T[name][(p,) + idx] if idx else T[name][p], "reg": [], "n": 0, "w": 0, "ps": False}
+        where, shape, d = SCRATCH[name]
+        if not idx:
+            idx = tuple(slice(0, n) for n in shape[1:])
+        ap = T[name][(p,) + idx]
+        cm = bits(shape[1:], idx)
+        reg = (name, 1, 1) if where == "psum" else (name, cm, bits([128], p))
+        return {"ap": ap, "reg": [reg], "n": cm.bit_count(), "w": 2 if d in (b16, u16) else 4, "ps": where == "psum"}
+
+    def C(name, a, b, s=None, p=ALL):
+        return R(name, slice(a, b, s), p=p)
+
+    def IND(win, off):
+        return {"ap": win["ap"].indirect(off["ap"]), "reg": win["reg"], "off": off["reg"], "n": 16 * off["n"], "w": 4, "ps": False}
+
+    def op(q, fn, outs, ins, dma=0, ext=None, two=False, key=None):
+        rd, wr = [], []
+        ins = [x for x in ins if isinstance(x, dict)]
+        for x in ins:
+            rd += x["reg"] + x.get("off", [])
+        for x in outs:
+            wr += x["reg"]
+            rd += x.get("off", [])
+        n = outs[0]["n"] if outs else 0
+        lat = 0.0
+        if ext:
+            cost, lat = 0.001, LREM
+        elif dma:
+            by = 128 * max([x["n"] * x["w"] for x in outs + ins])
+            cost, lat = (1.0 if q == "G" else 0.1), 2.0 + by / (2e5 if dma > 0 else 4e4)
+        elif q == "T":
+            cost = max(64, ins[1]["n"]) * CPE * (1 if ins[1]["w"] == 2 else 4)
+        elif q == "G":
+            cost = 0.15 + 2 * n * CYC
+        elif "off" in outs[0]:
+            cost = 0.05 + n * SCA * CYC
+        elif any("off" in x for x in ins):
+            cost = 0.06 + n * GAT * CYC
+        elif q == "S":
+            cost = 0.08 + n * CYC
+        else:
+            f = 0.5 if all(x["w"] == 2 for x in outs + ins if x["n"] > 1) else 1.0
+            if two and not any(x["ps"] for x in ins):
+                f *= 2
+            cost = max(0.066, n * f * CYC)
+        ops.append({"q": q, "fn": fn, "rd": rd, "wr": wr, "dma": dma, "ext": ext, "inc": False, "cost": cost, "lat": lat, "key": key,
+                    "after": chain[1] if chain[0] and q == "V" else None})
+        if chain[0] and q == "V":
+            chain[1] = len(ops) - 1
+
+    def a_(x):
+        return x["ap"] if isinstance(x, dict) else x
+
+    def tt(o, a, b, f):
+        op("V", lambda e: e.tensor_tensor(o["ap"], a["ap"], b["ap"], f), [o], [a, b], two=True)
+
+    def ts(o, a, s1, f1, s2=None, f2=None):
+        if s2 is None:
+            op("V", lambda e: e.tensor_scalar(o["ap"], a["ap"], a_(s1), None, f1), [o], [a, s1])
+        else:
+            op("V", lambda e: e.tensor_scalar(o["ap"], a["ap"], a_(s1), a_(s2), f1, f2), [o], [a, s1, s2])
+
+    def cp(o, a):
+        op("V", lambda e: e.tensor_copy(o["ap"], a["ap"]), [o], [a])
+
+    def ms(o, c):
+        op("V", lambda e: e.memset(o["ap"], c), [o], [])
+
+    def scan(o, a, b, f1, f2):
+        op("V", lambda e: e.tensor_tensor_scan(o["ap"], a["ap"], b["ap"], 0.0, f1, f2), [o], [a, b])
+
+    def tr(o, a):
+        op("V", lambda e: e.transpose(o["ap"], a["ap"]), [o], [a])
+
+    def act(o, a, f, bias=None, scale=None):
+        kw = {}
+        if bias is not None:
+            kw["bias"] = a_(bias)
+        if scale is not None:
+            kw["scale"] = a_(scale)
+        op("S", lambda e: e.activation(o["ap"], a["ap"], f, **kw), [o], [a, bias, scale])
+
+    def mm(o, l, r, st, sp):
+        op("T", lambda e: e.matmul(o["ap"], l["ap"], r["ap"], st, sp), [o], [l, r])
+
+    def iota(o, pat, base, cm, isint=False):
+        if isint:
+            op("G", lambda e: e.iota(o["ap"], pat, base, cm), [o], [])
+        else:
+            op("G", lambda e: e.iota(o["ap"], pat, base, cm, allow_small_or_imprecise_dtypes=True), [o], [])
+
+    def gfill(o, c):
+        iota(o, [[0, o["n"]]], c, 0)
+
+    def asel(o, pat, f, base, cm, a=None):
+        a = a or o
+        op("G", lambda e: e.affine_select(o["ap"], a["ap"], pat, f, 0.0, base, cm), [o], [a])
+
+    def dma(q, o, a, add=False, key=None):
+        if add:
+            op(q, lambda e: e.dma_start(o["ap"], a["ap"], accum_op=A.add), [o], [a, o], dma=16)
+        else:
+            op(q, lambda e: e.dma_start(o["ap"], a["ap"]), [o], [a], dma=16, key=key)
+
+    def hand_on(t, src, dst_ap, landed, sem):
+        for t2, s, via, d in routes(T, topo):
+            if t2 == t and s == core:
+                to = d if via is None else via
+                rid, pid = topo.addr(to, core)
+                mask = topo.mask(core, to)
+                op("G", lambda e, ls: e.remote_dma(dst_ap, src["ap"], T.sem[sem], ls, pid, rid, mask), [], [src],
+                   dma=-len(topo.engines(core, to)))
+        for t2, s, via, d in routes(T, topo):
+            if t2 == t and d == core:
+                op(None, None, [landed], [], ext=(sem, len(topo.engines(s if via is None else via, core))))
+
+    def Wr(name, r):
+        return C(name, 15 - r, 143 - r)
+
+    def PS(b, a=0, e=512):
+        return R("PS%d" % b, slice(a // 4, e // 4), ALL) if b in (4, 5, 6) else C("PS%d" % b, a, e)
+
+    rows = lambda x: slice(x, 128, 16)
+    CLc = lambda j: C("CL", j, j + 1)
+    PIc = lambda j: C("PI", j, j + 1)
+    CH = lambda nm, c, r=0, s=None: C(nm, 1024 * c + r, 1024 * c + 1024, s)
+
+    dma("Y", R("ZS"), R("zs"))
+    dma("S", R("SN"), R("sn"))
+    dma("Y", R("KC"), R("kid"))
+    dma("Y", R("VN"), R("vn"))
+    dma("Y", R("BC"), R("bst"))
+    dma("Y", R("NQ"), R("nq"))
+
+    iota(PIc(0), [[1, 1]], 0, 1, True)
+    iota(R("TF"), [[0, 8], [1, 2]], 0, 0)
+    iota(R("TG"), [[16, 16]], 0, 0)
+    iota(R("TH"), [[128, 2], [2, 8]], 0, 0)
+    iota(R("TI"), [[1, 16]], 0, 0, True)
+    ms(R("B0"), 0.0)
+    ms(R("ID"), 1.0)
+    ms(R("M1"), 0.0)
+    ms(R("M2"), 0.0)
+    ms(C("B0", 15, 144, 16), 1.0)
+    for j in range(4):
+        ms(C("M1", j, 128, 16), 1.0)
+        ms(C("M2", 4 + j, 128, 16), 1.0)
+    ts(PIc(1), PIc(0), 15, A.bitwise_and)
+    ts(PIc(2), PIc(0), 4, A.arith_shift_right, 1, A.bitwise_and)
+    ts(PIc(3), PIc(0), 1, A.bitwise_and)
+    ts(PIc(4), PIc(0), 2, A.arith_shift_right, 3, A.bitwise_and)
+    ts(PIc(5), PIc(0), 3, A.bitwise_and)
+    ts(PIc(6), PIc(0), 7, A.bitwise_and)
+    ts(PIc(7), PIc(0), 3, A.arith_shift_right, 1, A.bitwise_and)
+    for nm in ("NF", "QN"):
+        ms(C(nm, 0, 16), 0.0)
+        ms(C(nm, 272, 288), 0.0)
+    ms(R("KF"), 0.0)
+    ms(R("KD"), 0.0)
+    cp(C("CL", 0, 7), C("PI", 1, 8))
+    asel(R("B0"), [[-1, 144]], A.is_ge, 15, 1)
+    asel(R("B0"), [[1, 144]], A.is_ge, 0, -1)
+    for nm, j0 in (("M1", 0), ("M2", 4)):
+        asel(R(nm), [[-16, 8], [-4, 16]], A.is_ge, 4 * j0, 1)
+        asel(R(nm), [[16, 8], [4, 16]], A.is_ge, 3 - 4 * j0, -1)
+    asel(R("ID"), [[-1, 128]], A.is_equal, 0, 1)
+    ms(R("ONE"), 1.0)
+    ts(R("TF"), R("TF"), CLc(1), A.not_equal, 272.0, A.mult)
+    ts(R("LI"), R("TG"), CLc(0), A.add)
+    ts(CLc(7), CLc(2), CLc(1), A.not_equal, 272.0, A.mult)
+    ts(CLc(8), CLc(4), 16.0, A.mult, CLc(3), A.add)
+    tt(R("TF"), R("TF"), R("LI"), A.add)
+    ts(CLc(8), CLc(8), CLc(7), A.add)
+    ts(CLc(9), CLc(5), 16.0, A.mult, CLc(6), A.add)
+    cp(R("LMK"), R("TF"))
+    ts(R("LK"), C("TG", 0, 4), 0.25, A.mult, CLc(8), A.add)
+    ts(R("LKM"), R("TH"), CLc(9), A.add, CLc(7), A.add)
+    ts(CLc(20), CLc(3), 2.0, A.mult, CLc(2), A.add)
+    cp(R("LB"), R("TI"))
+    ts(R("LX"), C("TG", 0, 2), 0.5, A.mult, CLc(20), A.add)
+    gfill(R("FW"), -128)
+    ts(CLc(10), CLc(0), 8.0, A.is_equal)
+    ts(CLc(11), CLc(0), 9.0, A.is_equal)
+    ts(CLc(12), CLc(0), 11.0, A.is_equal)
+    ts(CLc(13), CLc(0), 4.0, A.is_lt, -8192.0, A.mult)
+    ts(CLc(14), CLc(0), 8.0, A.is_lt, -8192.0, A.mult)
+    ts(CLc(15), CLc(0), 0.0, A.is_equal, 2.0 ** -17, A.mult)
+    ts(CLc(16), CLc(11), 64.0, A.mult, CLc(10), A.add)
+    ts(CLc(17), CLc(10), CLc(11), A.add, CLc(12), A.add)
+    ts(CLc(18), CLc(12), 4096.0 - CEN, A.mult, CLc(16), A.add)
+    ts(CLc(21), CLc(14), CLc(13), A.subtract)
+    ts(CLc(19), CLc(18), CLc(13), A.add)
+    for nm, src, f in (("WM", "B0", 16384.0), ("WN", "B0", -8192.0), ("WP", "B0", 8192.0), ("CI", "ID", KOFF), ("NI", "ID", -1.0),
+                       ("WA", "B0", CLc(19)), ("WA0", "B0", CLc(21)), ("WA2", "B0", CLc(18)), ("P2", "ID", CLc(17))):
+        ts(R(nm), R(src), f, A.mult)
+    ts(C("P2", 12, 128, 16), C("B0", 15, 128, 16), CLc(16), A.mult)
+    cp(R("BF"), R("B0"))
+
+    def stile(tau):
+        cp(C("NF", 16, 272), C("SN", tau, 768, 3))
+        tr(C("Y", 0, 256), C("NF", 16, 272))
+        tr(C("Y", 256, 544), R("NF"))
+        ts(C("KS", L * tau, L * tau + L), IND(R("Y"), R("LMK")), -CEN, A.add)
+        ts(C("SO", L * tau, L * tau + L), C("KS", L * tau, L * tau + L), CEN, A.add)
+
+    def zexp(tau, m0=0, m1=16):
+        zg = "ZG2" if tau else "ZG"
+
+        def f(o, a, n):
+            if tau:
+                asel(o, [[0, n]], A.is_ge, 0, 0, a)
+            else:
+                act(o, a, AF.Copy)
+        ms_ = slice(m0, m1)
+        f(R(zg, ms_, slice(0, 16)), C("ZS", tau + 48 * m0, 48 * m1, 3), 16 * (m1 - m0))
+        for w in (16, 32, 64, 128):
+            f(R(zg, ms_, slice(w, 2 * w)), R(zg, ms_, slice(0, w)), w * (m1 - m0))
+        dma("Y", C("ZX%d" % tau, L * m0, L * m1), R(zg, ms_, ALL))
+
+    for tau in range(3):
+        act(C("ZT", L * tau, L * tau + L), C("ZS", tau, 768, 3), AF.Copy)
+    for m0, m1 in ((0, 4), (4, 10), (10, 16)):
+        zexp(0, m0, m1)
+    zexp(1)
+    cp(C("KF", 16, 80), R("KC"))
+    tr(C("Y", 0, 64), C("KF", 16, 80))
+    tr(C("Y", 256, 352), R("KF"))
+    ms(C("Y", 64, 256), 0.0)
+    cp(R("KO"), IND(C("Y", 0, 352), R("LK")))
+    ts(R("KI"), R("KC"), 63, A.bitwise_and)
+    cp(R("KLO"), R("KI"))
+    ts(R("KI"), R("KC"), 6, A.arith_shift_right)
+    cp(R("KHI"), R("KI"))
+    dma("Y", R("KD", p=rows(8)), R("KLO"))
+    dma("Y", R("KD", p=rows(9)), R("KHI"))
+    dma("Y", R("KD", p=rows(11)), C("ONE", 0, 64))
+    stile(0)
+    act(R("VCB"), IND(R("VN"), R("KO")), AF.Copy)
+    for hf in range(2):
+        cols = lambda nm, o=0: C(nm, o + 512 * hf, o + 512 * hf + 512)
+        mm(PS(4 + hf), R("M2"), cols("VN"), True, False)
+        mm(PS(4 + hf), R("P2"), cols("KD"), False, False)
+        mm(PS(4 + hf), R("M1"), cols("VCB"), False, True)
+        act(cols("AUX", PAD), PS(4 + hf), AF.Copy)
+    act(R("ZB"), R("ZS"), AF.Identity, bias=64.0)
+    iota(R("KB"), [[0, 16], [1, 16]], 1, 0)
+    iota(R("KA"), [[0, 16], [-1, 16]], 15, 0)
+    for a, b in ((PAD, PAD + T0), (PAD + T0, PAD + GB), (PAD + GB, WT)):
+        iota(C("IO", a, b), [[1, b - a]], a, 0)
+    act(C("VP", PAD, PAD + T0), C("IO", PAD, PAD + T0), AF.Identity, bias=64.0, scale=CLc(15))
+    dma("G", C("VP", PAD, PAD + T0), R("vn"), add=True)
+    dma("G", C("VC", PAD, PAD + T0), R("VCB"))
+    for m in range(16):
+        tt(C("XS", L * m, L * m + L), IND(R("VN"), C("SO", 16 * m, 16 * m + 16)), R("ZG", m, ALL), A.max)
+    ts(R("BCF"), R("BC"), float(PAD), A.add)
+    gfill(R("BR"), 0)
+    dma("Y", R("BR", p=rows(12)), R("BCF"))
+    for nm, v0, v in (("RMAX", -BIG, 1.0), ("RMIN", BIG, -1.0), ("RZ", 0.0, 1.0)):
+        gfill(R(nm), int(v))
+        ms(C(nm, 0, 256, 16), v0)
+    gfill(C("VP", 0, PAD), 1024)
+    ms(C("KB", 15, 256, 16), 0.0)
+    for hf in range(2):
+        cp(C("QT", 512 * hf, 512 * hf + 512), C("NQ", 512 * hf, 512 * hf + 512))
+    stile(1)
+    early = len(ops) - 1
+    iota(R("TRI"), [[0, 8], [-16, 2], [1, 32]], 0, 0)
+    iota(C("X1", 0, 32), [[1, 16], [0, 2]], 0, 0)
+    asel(R("FW"), [[-1, 16], [-16, 8], [0, 16]], A.is_equal, 0, 1)
+    iota(R("IC"), [[1, 144]], T0, 0, True)
+    ts(CLc(22), CLc(0), 144.0, A.mult)
+    ts(R("IC"), R("IC"), CLc(22), A.add)
+    ts(R("IC2"), R("IC"), 63, A.bitwise_and)
+    cp(R("ILO"), R("IC2"))
+    ts(R("IC2"), R("IC"), 6, A.arith_shift_right)
+    cp(R("IHI"), R("IC2"))
+    dma("Y", R("IDB"), C("ZX0", 0, 2304))
+    dma("Y", R("IDB", p=rows(8)), R("ILO"))
+    dma("Y", C("QT", T0, GB), C("IO", T0, GB))
+    dma("Y", C("VC", PAD + T0, WT), C("IO", PAD + T0, WT))
+    for r in range(16):
+        mm(PS(6, 0, 48), Wr("BF", r), C("BR", r, 768, 16), r == 0, r == 15)
+    for r in range(16):
+        mm(PS(7, 0, 48), Wr("B0", r), C("ZT", r, 768, 16), r == 0, r == 15)
+    act(R("THR"), PS(7, 0, 48), AF.Identity, bias=200.0 * 8192.0 + KOFF, scale=8192.0)
+    cp(R("BO"), PS(6, 0, 48))
+    act(R("VB"), IND(C("VP", 0, PAD + T0), R("BO")), AF.Copy)
+    dma("Y", R("IDB", p=rows(9)), R("IHI"))
+    dma("Y", R("IDB", p=rows(11)), R("ONE"))
+    dma("G", C("AUX", PAD + T0, WT), R("IDB"))
+    dma("Y", C("AUX", PAD + T0, WT, p=rows(12)), C("IO", T0, W, p=rows(12)))
+    cp(R("LB2"), C("X1", 0, 32))
+    ts(CLc(23), CLc(0), -8192.0, A.mult, 4096.0, A.add)
+    act(R("TRI"), R("TRI"), AF.Relu, bias=CLc(23), scale=8192.0)
+    gfill(R("RZ2"), 1)
+    gfill(C("IO", 0, PAD), PAD - 1)
+    ms(C("RZ2", 0, 512, 32), 0.0)
+    if SDUP:
+        ts(R("RB"), R("RZ2"), -BIG, A.mult, BIG, A.add)
+        act(R("IDF"), R("ID"), AF.Copy)
+        act(R("NIF"), R("NI"), AF.Copy)
+    for a in range(PAD + T0, WT, L):
+        act(C("VP", a, a + L), C("IO", a, a + L), AF.Identity, bias=64.0, scale=CLc(15))
+
+    def own_dist(tau):
+        zx = "ZX%d" % tau
+        for c in range(4):
+            src = "GA" if c % 2 == 0 else "VCB"
+            for a in range(0, 1024, PG):
+                so = L * tau + 64 * c + a // 16
+                act(C(src, a, a + PG), IND(R("VN"), C("SO", so, so + PG // 16)), AF.Copy)
+            for a in range(0, 1024, PA):
+                mm(PS(7, 0, PA), R("ID"), C(src, a, a + PA), True, False)
+                mm(PS(7, 0, PA), R("NI"), C(zx, 1024 * c + a, 1024 * c + a + PA), False, True)
+                act(C("GC", a, a + PA), PS(7, 0, PA), AF.Abs)
+            o = PS(0, 64 * c, 64 * c + 64)
+            for r in range(16):
+                mm(o, Wr("WP", r), CH(zx, c, r, 16), r == 0, False)
+            mm(o, R("CI"), C("ONE", 0, 64), False, False)
+            for r in range(16):
+                mm(o, Wr("WP", r), C("GC", r, 1024, 16), False, r == 15)
+        kn = C("KS", L * tau, L * tau + L)
+        tt(kn, PS(0, 0, L), kn, A.add)
+
+    for t in range(5):
+        tau = TILE[t]
+        zx = "ZX%d" % tau
+        wend = PAD + (T0 if t < 3 else GB + L * (t - 2))
+        aend = PAD + (T0 if t == 0 else GB + L * t)
+        own = PAD + T0 + L * t
+        ks = C("KS", L * tau, L * tau + L)
+        for c in range(4):
+            so = C("SO", L * tau + 64 * c, L * tau + 64 * c + 64)
+            act(CH("XA", c), IND(C("AUX", PAD, wend), so), AF.Copy)
+            tt(CH("XM", c), IND(R("VCB") if t == 0 else C("VC", PAD, wend), so), CH(zx, c), A.max)
+            for b, x, wa in ([(1, "XS", "WA0")] if t == 0 else []) + [(0, "XM", "WA")]:
+                o = PS(b, 64 * c, 64 * c + 64)
+                for r in range(16):
+                    mm(o, Wr(wa, r), CH("XA", c, r, 16), r == 0, False)
+                for r in range(16):
+                    mm(o, Wr("WM", r), CH(x, c, r, 16), False, False)
+                mm(o, R("CI"), C("ONE", 0, 64), False, True)
+        if t == 0:
+            tt(ks, PS(1, 0, L), ks, A.add)
+            ops[-1]["after"] = early
+        else:
+            gs = GB - T0 + L * (t - 1)
+            ld = L * (t - 1)
+            gcol = PAD + GB + ld
+            land = C("LAND", ld, ld + L)
+            dma("G", C("VP", gcol, gcol + L), land, add=True)
+            tt(R("XG"), land, C("ZT", L * tau, L * tau + L), A.max)
+            o = PS(2, 0, 16)
+            for r in range(16):
+                mm(o, Wr("WA2", r), C("IDB", gs + r, gs + L, 16), r == 0, False)
+            for r in range(16):
+                mm(o, Wr("WN", r), C("LAND", ld + r, ld + L, 16), False, False)
+            for r in range(16):
+                mm(o, Wr("WM", r), C("XG", r, L, 16), False, False)
+            mm(o, R("CI"), C("ONE", 0, 16), False, True)
+            act(R("KM"), o, AF.Copy)
+        if t in (1, 2):
+            po = own - L
+            dma("G", C("VC", po, po + L), C("YV", L * (t - 1), L * t))
+            dma("Y", C("AUX", po, po + L), C("AXN", 0, L))
+            dma("G", C("VC", gcol, gcol + L), land)
+            mm(PS(1, 0, L), R("M1"), land, True, False)
+            mm(PS(1, 0, L), R("P2"), C("IDB", gs, gs + L), False, True)
+            act(C("AUX", gcol, gcol + L), PS(1, 0, L), AF.Copy)
+        k2 = PS(4, 0, L)
+        tt(k2, PS(0, 0, L), ks, A.min)
+        ts(R("DP"), k2, MAGIC, A.add, MAGIC, A.subtract)
+        if t >= 1:
+            scan(R("SM"), R("RMAX"), R("DP"), A.add, A.max)
+            cp(R("S1"), C("SM", 15, 256, 16))
+            ts(R("S2"), R("S1"), 15, A.bitwise_and)
+            tt(R("E"), IND(R("S2"), R("LB")), R("KA"), A.is_equal)
+            tt(R("E2"), IND(R("KM"), R("LB")), R("E"), A.mult)
+            tt(PS(5, 0, L), k2, R("E2"), A.min)
+            k2 = PS(5, 0, L)
+            ts(R("DP"), k2, MAGIC, A.add, MAGIC, A.subtract)
+        scan(R("SM"), R("RMIN"), R("DP"), A.add, A.min)
+        cp(R("S1"), C("SM", 15, 256, 16))
+        ts(R("S2"), R("S1"), 15, A.bitwise_and)
+        tt(R("E"), IND(R("S2"), R("LB")), R("KB"), A.is_equal)
+        tt(R("E2"), k2, R("E"), A.mult)
+        scan(R("SM"), R("RZ"), R("E2"), A.mult, A.min)
+        ts(R("S1"), C("SM", 15, 256, 16), CEN, A.add)
+        ts(R("AI"), R("S1"), 4095, A.bitwise_and)
+        cp(R("A16"), R("AI"))
+        act(C("QN", 16, 272), IND(C("QT", 0, aend - PAD), R("A16")), AF.Copy)
+        for h in (1, 0):
+            for va in ("VAB", "VAF"):
+                act(C(va, 512 * h, 512 * h + 128), IND(C("VP", PAD, aend), C("A16", 8 * h, 8 * h + 8)), AF.Copy)
+                for j in range(1, 4):
+                    dma("Y", C(va, 512 * h + 128 * j, 512 * h + 128 * j + 128), C(va, 512 * h, 512 * h + 128), key=(va, h, j))
+        scan(R("E"), R("RMAX"), R("DP"), A.add, A.max)
+        ts(R("U"), R("AI"), float(PAD), A.add)
+        ts(R("SI"), k2, CEN, A.add)
+        tt(R("LV"), C("E", 15, 256, 16), C("THR", 16 * tau, 16 * tau + 16), A.is_ge)
+        tt(R("U"), R("U"), R("LI"), A.subtract)
+        tt(R("U"), R("U"), R("LV"), A.mult)
+        tt(R("AD"), R("U"), R("LI"), A.add)
+        cp(R("AD16"), R("AD"))
+        tr(C("Y", 0, 256), C("QN", 16, 272))
+        tr(C("Y", 256, 544), R("QN"))
+        cp(R("QO"), IND(R("Y"), R("LKM")))
+        if t < 4:
+            hand_on(t, C("QN", 16, 272), qslot(T, t), C("QT", GB + L * t, GB + L * t + L), "aq%d" % t)
+            dma("Y", C("QT", own - PAD, own - PAD + L), C("QN", 16, 272))
+        act(C("VB", tau, 768, 3), IND(C("VP", 0, aend), R("AD16")), AF.Copy)
+        if t == 0:
+            zexp(2)
+            stile(2)
+        if t < 2:
+            own_dist(t + 1)
+        ts(R("SI2"), R("SI"), 4095, A.bitwise_and)
+        if t in (1, 2):
+            cp(C("SO", L * tau, L * tau + L), R("SI2"))
+            tt(R("SM"), R("DP"), R("SI2"), A.add)
+            act(ks, R("SM"), AF.Identity, bias=-CEN)
+        else:
+            ts(C("NF", 16, 144), C("SI2", 128, 256), 4096.0, A.mult)
+            tt(C("NF", 16, 144), C("NF", 16, 144), C("SI2", 0, 128), A.add)
+            tr(C("Y", 0, 128), C("NF", 16, 144))
+            tr(C("Y", 256, 416), C("NF", 0, 160))
+            act(C("YS", tau, 384, 3), IND(R("Y"), C("LMK", 0, 8)), AF.Copy)
+            act(C("YB", tau, 768, 3), IND(C("IO", 0, aend), R("AD16")), AF.Identity, bias=-float(PAD))
+        cp(R("OX"), IND(R("AD"), R("LX")))
+        tt(R("U2"), R("LI"), R("AD"), A.subtract)
+        if t in SDUP:
+            act(R("X1"), IND(C("IO", 0, aend), R("OX")), AF.Copy)
+            act(R("X2"), IND(R("AD"), R("LB2")), AF.Copy)
+            mm(PS(7), R("IDF"), R("TRI"), True, False)
+            mm(PS(7), R("IDF"), R("X1"), False, False)
+            mm(PS(7), R("NIF"), R("X2"), False, True)
+            act(R("X2"), PS(7), AF.Abs)
+            scan(R("X1"), R("RB"), R("X2"), A.add, A.min)
+            ts(R("LV"), C("X1", 31, 512, 32), 0.0, A.is_equal)
+            tt(R("U2"), R("U2"), R("LV"), A.mult)
+        else:
+            tt(R("X1"), IND(C("IO", 0, aend), R("OX")), R("TRI"), A.add)
+            tt(R("X2"), IND(R("AD"), R("LB2")), R("X1"), A.is_equal)
+            scan(R("X1"), R("RZ2"), R("X2"), A.mult, A.max)
+            tt(R("U2"), R("U2"), C("X1", 31, 512, 32), A.mult)
+        tt(R("U2"), R("U2"), R("AD"), A.add)
+        cp(R("O1"), R("U2"))
+        if t == 4:
+            dma("Y", R("ys"), R("YS"))
+            dma("Y", R("yb"), R("YB", p=rows(0)))
+            mm(PS(0, 0, L), R("P2"), C("IDB", L * t, L * t + L), True, True)
+            act(C("AXN", L, 2 * L), PS(0, 0, L), AF.Copy)
+            for b in range(7, -1, -1):
+                cp(IND(R("AUX"), C("O1", 2 * b, 2 * b + 2)), C("AXN", L + 32 * b, L + 32 * b + 32))
+            dma("Y", R("yk"), C("AUX", PAD, WT, p=rows(12)))
+        def diffs(h, x, c):
+            b = 2 - h
+            win, va, ab, pc = ("ZB", "VAB", "A1", 0) if x == "D1" else ("VB", "VAF", "A2", 128)
+            for u in range(2 * c, 2 * c + 2):
+                o, q0 = 2048 * h + 512 * u, 128 * h + 32 * u
+                if x == "D1" and h == 0 and u < SQUAD[t]:
+                    gz = C("GZ", 512 * (u % 2), 512 * (u % 2) + 512)
+                    act(gz, IND(R(win), C("QO", q0, q0 + 32)), AF.Copy)
+                    mm(PS(0), R("ID"), gz, True, False)
+                    mm(PS(0), R("NI"), C(va, 0, 512), False, True)
+                    act(C(x, o, o + 512), PS(0), AF.Copy)
+                elif x == "D1" and h == 1 and u < NSMALL:
+                    for k in range(4):
+                        tt(C(x, o + 128 * k, o + 128 * k + 128), IND(R(win), C("QO", q0 + 8 * k, q0 + 8 * k + 8)),
+                           C(va, 512 * h, 512 * h + 128), A.subtract)
+                else:
+                    tt(C(x, o, o + 512), IND(R(win), C("QO", q0, q0 + 32)), C(va, 512 * h, 512 * h + 512), A.subtract)
+            act(CH(ab, 2 * h + c), CH(x, 2 * h + c), AF.Abs)
+            for r in range(16):
+                mm(PS(b, pc + 64 * c, pc + 64 * c + 64), Wr("B0", r), CH(ab, 2 * h + c, r, 16), r == 0, r == 15)
+            if x == "D1" and c == 1:
+                act(C("D1M", 128 * h, 128 * h + 128), PS(b, 0, 128), AF.Identity, bias=-0.5)
+
+        def attract(h):
+            hs = lambda nm, o=0: C(nm, o + 128 * h, o + 128 * h + 128)
+            d2 = PS(2 - h, 128, 256)
+            tt(hs("N2"), hs("D1M"), d2, A.subtract)
+            ts(hs("N1"), d2, 1100.0, A.is_gt)
+            tt(hs("N2"), hs("N2"), d2, A.min)
+            ts(hs("N3"), hs("N2"), 0.0, A.is_gt)
+            tt(hs("NA"), hs("N3"), hs("N1"), A.add)
+
+        chain[:] = [True, None]
+        for step in STEP4:
+            if len(step) == 1:
+                attract(step[0])
+            else:
+                diffs(*step)
+        chain[0] = False
+        for h in (1, 0):
+            b = 2 - h
+            hs = lambda nm, o=0: C(nm, o + 128 * h, o + 128 * h + 128)
+            vab = C("VAB", 512 * h, 512 * h + 128)
+            act(R("VAU", slice(8 * h, 8 * h + 8), ALL), vab, AF.Identity, bias=-64.0)
+            if h == 0:
+                attract(0)
+            for k in range(16):
+                mm(PS(b, 0, 8), R("ID"), C("NA", 128 * h + 8 * k, 128 * h + 8 * k + 8), k == 0, k == 15)
+            act(C("CN", 8 * h, 8 * h + 8), PS(b, 0, 8), AF.Identity, scale=-1.0 / 128.0)
+            for rc in range(4):
+                ub = 4 + (rc + 4 * (1 - h) + 2) % 3
+                for r in range(4 * rc, 4 * rc + 4):
+                    o = R("PS%d" % ub, ALL, r % 4)
+                    mm(o, R("ID"), C("D1", 2048 * h + r, 2048 * h + 2048, 16), True, False)
+                    mm(o, C("FW", 128 * r, 128 * r + 128), hs("NA"), False, True)
+                sg = R("SG", slice(128 * h, 128 * h + 128), slice(4 * rc, 4 * rc + 4))
+                if (h, rc) in VSIGN:
+                    ts(sg, PS(ub), -1.0, A.max, 1.0, A.min)
+                else:
+                    act(sg, PS(ub), AF.Sign)
+            for c in range(2):
+                rc, mh = slice(8 * c, 8 * c + 8), slice(8 * h, 8 * h + 8)
+                o = R("PS3", mh, rc)
+                for k in range(16):
+                    mm(o, R("ID"), R("SG", slice(128 * h + 8 * k, 128 * h + 8 * k + 8), rc), k == 0, False)
+                for r in range(8 * c, 8 * c + 8):
+                    mm(R("PS3", mh, r), C("FW", 128 * r, 128 * r + 128), C("CN", 8 * h, 8 * h + 8), False, r == 8 * c + 7)
+            ts(hs("H1"), R("PS3", slice(8 * h, 8 * h + 8), ALL), -2.0, A.max, 2.0, A.min)
+            tt(hs("H1"), hs("H1"), R("VAU", slice(8 * h, 8 * h + 8), ALL), A.add)
+            ts(hs("YV", L * t), hs("H1"), 0.0, A.max, 63.0, A.min)
+            if t < 4:
+                mm(PS(b, 0, 128), R("P2"), hs("IDB", L * t), True, False)
+                mm(PS(b, 0, 128), R("M1"), hs("YV", L * t), False, True)
+                act(hs("AXN"), PS(b, 0, 128), AF.Copy)
+                for bl in range(4 * h + 3, 4 * h - 1, -1):
+                    cp(IND(R("VC"), C("O1", 2 * bl, 2 * bl + 2)), C("YV", L * t + 32 * bl, L * t + 32 * bl + 32))
+                for bl in range(4 * h + 3, 4 * h - 1, -1):
+                    cp(IND(R("AUX"), C("O1", 2 * bl, 2 * bl + 2)), C("AXN", 32 * bl, 32 * bl + 32))
+        new = C("YV", L * t, L * t + L)
+        if t < 4:
+            hand_on(t, new, nslot(T, t), C("LAND", L * t, L * t + L), "an%d" % t)
+            dma("G", C("VP", own, own + L), new, add=True)
+        dma("Y", C("yv", L * t, L * t + L), new)
+
+    if "seq" not in ORDER:
+        ORDER["seq"], ORDER["wait"] = plan_calls(ops)
+    sems = {}
+    for i, o in enumerate(ops):
+        for j in ORDER["wait"][i]:
+            ops[j]["inc"] = True
+        if o["dma"]:
+            s = sems.setdefault(o["key"] or i, ["d%d" % len(sems), 0])
+            s[1] += abs(o["dma"])
+            o["sem"] = (s[0], s[1])
+        elif o["ext"]:
+            o["sem"] = o["ext"]
+    for q in Q:
+        cnt = 0
+        for i in ORDER["seq"][q]:
+            if ops[i]["inc"] and not ops[i]["dma"]:
+                cnt += 1
+                ops[i]["sem"] = ("c" + q, cnt)
+    for q in Q:
+        for i in ORDER["seq"][q]:
+            o = ops[i]
+            for j in ORDER["wait"][i]:
+                Q[q].wait_ge(T.sem[ops[j]["sem"][0]], ops[j]["sem"][1])
+            if o["dma"] < 0:
+                o["fn"](Q[q], T.sem[o["sem"][0]])
+            elif o["dma"]:
+                o["fn"](Q[q]).then_inc(T.sem[o["sem"][0]], 16)
+            else:
+                ins = o["fn"](Q[q])
+                if o["inc"]:
+                    ins.then_inc(T.sem["c" + q], 1)
+    for o in ops:
+        if (o["dma"] or o["ext"]) and not o["inc"]:
+            g.sync.wait_ge(T.sem[o["sem"][0]], o["sem"][1])

@@ -14,7 +14,7 @@ KOFF = -2040.0 * 8192.0
 CEN = 3700.0
 NSMALL = 2
 VSIGN = ()
-CYC, CPE, WAKE, LREM, GAT, SCA = 0.00104, 0.00052, 0.06, 4.0, 1.56, 3.8
+CYC, CPE, WAKE, LREM, GAT, SCA = 0.00092, 0.00050, 0.2, 5.0, 1.56, 3.8
 PASSES, ROUNDS, BLEND, SEED, JIT = 1, 12, 0.3, 0, 0.3
 STEP4 = [(1, "D1", 0), (1, "D1", 1), (1, "D2", 0), (1, "D2", 1), (0, "D1", 0), (1,), (0, "D1", 1), (0, "D2", 0), (0, "D2", 1)]
 SDUP = ()
@@ -61,7 +61,7 @@ SCRATCH["VAU"] = ("sbuf", [128, 16, 16], b16)
 for _j in range(8):
     SCRATCH["PS%d" % _j] = ("psum", [128, 32, 16] if _j == 3 else [128, 128, 4] if _j in (4, 5, 6) else [128, 512], f32)
 NDMA = 120
-SEMAPHORES = ["cV", "cS", "cT", "cG"] + ["d%d" % _j for _j in range(NDMA)] + ["aq%d" % _j for _j in range(4)] + ["an%d" % _j for _j in range(4)] + ["fwd"]
+SEMAPHORES = ["cV", "cS", "cT", "cG"] + ["d%d" % _j for _j in range(NDMA)] + ["aq%d" % _j for _j in range(4)] + ["an%d" % _j for _j in range(8)] + ["fwd"]
 MASKS = {}
 
 
@@ -95,8 +95,8 @@ def qslot(T, t):
     return T["QT"][:, GB + L * t:GB + L * t + L]
 
 
-def nslot(T, t):
-    return T["LAND"][:, L * t:L * t + L]
+def nslot(T, t, h):
+    return T["LAND"][:, L * t + 128 * h:L * t + 128 * h + 128]
 
 
 def relay_program(g, core, T, topo):
@@ -106,7 +106,7 @@ def relay_program(g, core, T, topo):
             continue
         n_in = len(topo.engines(s, core))
         rid, pid = topo.addr(d, core)
-        for sem, ap in (("aq%d" % t, qslot(T, t)), ("an%d" % t, nslot(T, t))):
+        for sem, ap in (("aq%d" % t, qslot(T, t)), ("an%d" % (2 * t + 1), nslot(T, t, 1)), ("an%d" % (2 * t), nslot(T, t, 0))):
             g.wait_ge(T.sem[sem], n_in)
             g.remote_dma(ap, ap, T.sem[sem], T.sem["fwd"], pid, rid, topo.mask(core, d))
             sent += len(topo.engines(core, d))
@@ -260,7 +260,7 @@ def rank_program(g, core, T, topo):
             cost, lat = 0.001, LREM
         elif dma:
             by = 128 * max([x["n"] * x["w"] for x in outs + ins])
-            cost, lat = (1.0 if q == "G" else 0.1), 2.0 + by / (2e5 if dma > 0 else 4e4)
+            cost, lat = (1.0 if q == "G" else 0.2), 2.5 + by / (2e5 if dma > 0 else 4e4)
         elif q == "T":
             cost = max(64, ins[1]["n"]) * CPE * (1 if ins[1]["w"] == 2 else 4)
         elif q == "G":
@@ -757,6 +757,8 @@ def rank_program(g, core, T, topo):
             tt(hs("H1"), hs("H1"), R("VAU", slice(8 * h, 8 * h + 8), ALL), A.add)
             ts(hs("YV", L * t), hs("H1"), 0.0, A.max, 63.0, A.min)
             if t < 4:
+                hand_on(t, hs("YV", L * t), nslot(T, t, h), hs("LAND", L * t), "an%d" % (2 * t + h))
+            if t < 4:
                 mm(PS(b, 0, 128), R("P2"), hs("IDB", L * t), True, False)
                 mm(PS(b, 0, 128), R("M1"), hs("YV", L * t), False, True)
                 act(hs("AXN"), PS(b, 0, 128), AF.Copy)
@@ -766,7 +768,6 @@ def rank_program(g, core, T, topo):
                     cp(IND(R("AUX"), C("O1", 2 * bl, 2 * bl + 2)), C("AXN", 32 * bl, 32 * bl + 32))
         new = C("YV", L * t, L * t + L)
         if t < 4:
-            hand_on(t, new, nslot(T, t), C("LAND", L * t, L * t + L), "an%d" % t)
             dma("G", C("VP", own, own + L), new, add=True)
         dma("Y", C("yv", L * t, L * t + L), new)
 

@@ -10,16 +10,26 @@ PAD = 256
 WT = PAD + W
 MAGIC = 1.5 * 2.0 ** 36
 BIG = 2.0 ** 26
+TOP = 2.0 ** 24
 KOFF = -2040.0 * 8192.0
 CEN = 3700.0
-NSMALL = 2
-VSIGN = ()
-CYC, CPE, WAKE, LREM, GAT, SCA = 0.00092, 0.00050, 0.2, 5.0, 1.56, 3.8
+CYC, CPE, WAKE, LREM, GAT, SCA = 0.00087, 0.00045, 0.2, (3.5, 0.5, 3.5, 0.5), 1.56, 3.8
 PASSES, ROUNDS, BLEND, SEED, JIT = 1, 12, 0.3, 0, 0.3
-STEP4 = [(1, "D1", 0), (1, "D1", 1), (1, "D2", 0), (1, "D2", 1), (0, "D1", 0), (1,), (0, "D1", 1), (0, "D2", 0), (0, "D2", 1)]
-SDUP = ()
-SQUAD = (0, 0, 2, 2, 2)
-PG, PA = 256, 512
+MOVES, SPREAD, LATE, HEAT, SWEEPS = 3000, 0.1, 0.3, 0.1, 1
+NOWAIT = False
+OPT = {
+    "SQ": [()] * 5,
+    "SD": [((0, 0), (0, 1), (0, 2), (0, 3))] * 5,
+    "RELU": [((0, "D2", 0), (0, "D2", 1))] * 5,
+    "SMALL": ((1, "D1", 0), (1, "D1", 1)),
+    "VSIGN": ((0, 1), (0, 3)),
+    "OWNS": {1: (0, 1), 2: (0, 1)},
+    "GV": (0,),
+    "CHAIN": (),
+    "STEP4": ["o3 o2 o1 o0 d l g110v g010D g111v g011D g112V g012D g113V g013D z110S z111S i10 i11 i12 i13 g120V g121V z120S g122V g123V z121S g020V g021V "
+              "a1 z010S z011S g022V s10S s11S c1 z020S g023V s12S s13S z021V i00 i01 p10 a0 i02 p11 f1 s00S s01V s02S s03V c0 p00 p01 f0"] * 5,
+}
+PG, PA = 512, 512
 ORDER = {}
 
 f32, b16, i32, u16 = "float32", "bfloat16", "int32", "uint16"
@@ -31,23 +41,26 @@ for _n, _w, _d in [
     ("QT", W, f32), ("VP", WT, f32), ("VC", WT, f32), ("AUX", WT, f32), ("IO", WT, f32), ("VB", 768, f32),
     ("IDB", 2304, b16), ("IC", 144, i32), ("IC2", 144, i32), ("ILO", 144, b16), ("IHI", 144, b16), ("GA", 1024, b16), ("GC", 1024, b16),
     ("D1", 4096, b16), ("D2", 4096, b16), ("A1", 4096, b16), ("A2", 4096, b16), ("ZX0", 4096, b16), ("ZX1", 4096, b16), ("FW", 2048, b16),
-    ("B0", 144, b16), ("WM", 144, b16), ("WN", 144, b16), ("WP", 144, b16), ("WA", 144, b16), ("WA0", 144, b16), ("WA2", 144, b16), ("BF", 144, f32),
-    ("ID", 128, b16), ("NI", 128, b16), ("CI", 128, b16), ("M1", 128, b16), ("M2", 128, b16), ("P2", 128, b16), ("IDF", 128, f32), ("NIF", 128, f32), ("RB", 512, b16), ("GZ", 1024, b16), ("ONE", 144, b16),
+    ("B0", 144, b16), ("WM", 144, b16), ("WN", 144, b16), ("WP", 144, b16), ("WA", 144, b16), ("WA0", 144, b16), ("W2", 144, b16), ("WB", 144, b16), ("BF", 144, f32),
+    ("ID", 128, b16), ("NI", 128, b16), ("CI", 128, b16), ("M1", 128, b16), ("M2", 128, b16), ("P2", 128, b16), ("ONE", 144, b16),
     ("PI", 8, i32), ("CL", 24, f32), ("TI", 16, i32), ("TF", 16, f32), ("TG", 16, f32), ("TH", 16, f32),
-    ("LMK", 16, u16), ("LKM", 16, u16), ("LK", 4, u16), ("LB", 16, u16), ("LB2", 32, u16), ("LX", 2, u16), ("LI", 16, f32),
-    ("TRI", 512, f32), ("RMAX", 256, b16), ("RMIN", 256, b16), ("RZ", 256, b16), ("RZ2", 512, b16), ("KA", 256, f32), ("KB", 256, f32),
+    ("LMK", 16, u16), ("LM0", 8, u16), ("LKM", 16, u16), ("LK", 4, u16), ("LB", 16, u16), ("LB2", 32, u16), ("LX", 2, u16), ("REV", 8, u16), ("LI", 16, f32),
+    ("TRI", 512, f32), ("RMAX", 256, b16), ("RMIN", 256, b16), ("RL", 256, b16), ("RZ2", 512, b16), ("KA", 256, f32),
     ("THR", 48, f32), ("NF", 288, f32), ("QN", 288, f32), ("Y", 544, f32), ("KS", 768, f32), ("SO", 768, u16), ("QO", 256, u16),
-    ("DP", 256, f32), ("SM", 256, f32), ("E", 256, f32), ("E2", 256, f32),
-    ("S1", 16, i32), ("S2", 16, i32), ("AI", 16, i32), ("A16", 16, u16), ("KM", 16, f32), ("LV", 16, f32), ("U", 16, f32), ("U2", 16, f32),
+    ("SMN", 256, f32), ("SMX", 256, f32), ("SM2", 256, f32), ("NM", 256, b16), ("E", 256, f32), ("E2", 256, f32), ("K3", 256, f32),
+    ("S1", 16, i32), ("S2", 16, i32), ("S3", 16, i32), ("AI", 16, i32), ("A16", 16, u16), ("KM", 16, f32), ("LV", 16, f32), ("U", 16, f32), ("U2", 16, f32),
+    ("GD", 16, f32), ("YG", 16, f32), ("GW", 16, f32), ("AF", 16, f32), ("GID", 64, f32), ("GK", 64, f32),
     ("AD", 16, f32), ("AD16", 16, u16), ("OX", 32, u16), ("O1", 16, u16), ("X1", 512, f32), ("X2", 512, f32), ("SI", 256, i32), ("SI2", 256, i32),
-    ("XG", 256, b16), ("LAND", 1024, b16), ("VAB", 1024, b16), ("VAF", 1024, f32),
-    ("D1M", 256, f32), ("N1", 256, b16), ("N3", 256, b16), ("NA", 256, b16), ("CN", 16, b16), ("H1", 256, b16), ("YV", 1280, b16),
-    ("AXN", 512, f32), ("YS", 384, f32), ("YB", 768, f32),
+    ("XG", 256, b16), ("LAND", 1024, b16), ("NVA", 1024, b16), ("VAF", 1024, f32), ("VA", 256, b16),
+    ("D1M", 256, f32), ("N1", 256, b16), ("N2", 256, b16), ("N3", 256, b16), ("NA", 256, b16), ("CN", 16, b16), ("H1", 256, b16), ("LO", 256, b16), ("HI", 256, b16),
+    ("YV", 1280, b16), ("AXN", 512, f32), ("YS", 384, f32), ("YB", 768, f32),
 ]:
     SCRATCH[_n] = ("sbuf", [128, _w], _d)
-ALIAS = {"XM": "A1", "XA": "A2", "XS": "D2", "ZX2": "ZX0", "N2": "E2", "KD": "GC"}
+ALIAS = {"XM": "A1", "XA": "A2", "XS": "D2", "ZX2": "ZX0", "KD": "GC"}
 PART = {}
-for _grp in (("KLO", "KHI", "ILO", "IHI"), ("IC", "IC2"), ("U", "U2", "LV"), ("N1", "N3")):
+for _grp in (("KLO", "KHI", "ILO", "IHI"), ("IC", "IC2"), ("U", "U2", "LV", "GD", "YG", "GW", "AF", "GID", "GK"), ("N1", "N2", "N3", "H1", "LO", "HI", "NM"),
+             ("S1", "S3", "AI"), ("WM", "WN", "WP", "WA", "WA0", "W2", "WB"), ("TF", "TG", "TH", "LI"), ("LMK", "LM0", "LKM", "LK", "LB", "LB2", "LX", "REV"),
+             ("NI", "CI"), ("RMAX", "RMIN", "RL")):
     _o = 0
     for _n in _grp:
         _where, _s, _d = SCRATCH.pop(_n)
@@ -57,10 +70,10 @@ for _grp in (("KLO", "KHI", "ILO", "IHI"), ("IC", "IC2"), ("U", "U2", "LV"), ("N
 SCRATCH["ZG"] = ("sbuf", [128, 16, 256], b16)
 SCRATCH["ZG2"] = ("sbuf", [128, 16, 256], b16)
 SCRATCH["SG"] = ("sbuf", [128, 256, 16], b16)
-SCRATCH["VAU"] = ("sbuf", [128, 16, 16], b16)
 for _j in range(8):
     SCRATCH["PS%d" % _j] = ("psum", [128, 32, 16] if _j == 3 else [128, 128, 4] if _j in (4, 5, 6) else [128, 512], f32)
-NDMA = 120
+DBANK = (7, 2)
+NDMA = 128
 SEMAPHORES = ["cV", "cS", "cT", "cG"] + ["d%d" % _j for _j in range(NDMA)] + ["aq%d" % _j for _j in range(4)] + ["an%d" % _j for _j in range(8)] + ["fwd"]
 MASKS = {}
 
@@ -71,7 +84,7 @@ def bits(shape, idx):
         n = int(np.prod(shape))
         m = np.zeros(n, bool)
         m[np.arange(n).reshape(shape)[idx].reshape(-1)] = True
-        MASKS[key] = int.from_bytes(np.packbits(m).tobytes(), "big")
+        MASKS[key] = int.from_bytes(np.packbits(m, bitorder="little").tobytes(), "little")
     return MASKS[key]
 
 
@@ -114,12 +127,16 @@ def relay_program(g, core, T, topo):
         g.wait_ge(T.sem["fwd"], sent)
 
 
-def place(ops, order, edges, first):
+def place(ops, order, edges, first, fixed=None, near=()):
     line = {}
-    start = [0.0] * len(ops)
+    start = list(fixed) if fixed else [0.0] * len(ops)
+    floor = min([fixed[i] for i in near], default=0.0)
+    for i in sorted(near, key=lambda i: fixed[i]):
+        if ops[i]["q"]:
+            line.setdefault(ops[i]["q"], []).append((fixed[i], fixed[i] + ops[i]["cost"], i))
     for i in order:
         o = ops[i]
-        t = max([start[j] + ops[j]["cost"] + d for j, d in edges[i]] + [first[i]])
+        t = max([start[j] + ops[j]["cost"] + d for j, d in edges[i]] + [first[i], floor])
         if o["q"]:
             ln = line.setdefault(o["q"], [])
             k = len(ln)
@@ -138,29 +155,38 @@ def place(ops, order, edges, first):
 def plan_calls(ops):
     n = len(ops)
     acc = {}
+    bank = {}
     pred = []
     for i, o in enumerate(ops):
         q = o["q"]
         need = {}
         if o["ext"]:
-            need[i - 1] = False
+            need[o["sent"]] = False
         if o["after"] is not None:
             need[o["after"]] = False
         for regs, w in ((o["rd"], False), (o["wr"], True)):
             for name, cm, pm in regs:
-                ps = name.startswith("PS")
                 for j, cm2, pm2, w2 in acc.get(name, []):
-                    if j == i or not (cm & cm2 and pm & pm2):
+                    if j == i or not (cm & cm2 and pm & pm2) or not (w or w2):
                         continue
                     same = ops[j]["q"] == q and not ops[j]["dma"] and not o["dma"]
-                    if not (w or w2 or (ps and not same)):
-                        continue
-                    need[j] = not (same and q == "T")
+                    free = same and (q == "T" or (NOWAIT and o["sct"] == name and ops[j]["sct"] == name))
+                    need[j] = need.get(j, False) or not free
+        for name in {r[0] for r in o["rd"] + o["wr"] if r[0].startswith("PS")}:
+            user, run, before = bank.setdefault(name, [q, [], []])
+            if user != q:
+                bank[name] = [q, [], run]
+                before, run = run, bank[name][1]
+            for j in before:
+                need[j] = True
+            if q == "T" and run:
+                need.setdefault(run[-1], False)
+            run.append(i)
         for regs, w in ((o["rd"], False), (o["wr"], True)):
             for name, cm, pm in regs:
                 lst = acc.setdefault(name, [])
                 if w:
-                    lst[:] = [e for e in lst if (e[1] & ~cm) or (e[2] & ~pm) or e[0] == i]
+                    lst[:] = [e for e in lst if (e[1] & ~cm) or (e[2] & ~pm) or e[0] == i or (NOWAIT and ops[e[0]]["sct"] == name and o["sct"] == name)]
                 lst.append((i, cm, pm, w))
         pred.append(need)
     fwd = [[(j, ops[j]["lat"] + (WAKE if s else 0.0)) for j, s in pred[i].items()] for i in range(n)]
@@ -180,7 +206,7 @@ def plan_calls(ops):
         for p in range(PASSES + 1):
             end = max(start[i] + ops[i]["cost"] + lats[i] for i in range(n))
             if best_end is None or end < best_end:
-                best_end, seq, first = end, sq, (start, sq)
+                best_end, seq, first, best_start = end, sq, (start, sq), start
             if p < PASSES:
                 back, _s = place(ops, sorted(range(n), key=lambda i: (-(start[i] + ops[i]["cost"]), -i)), bwd, lats)
                 start, sq = place(ops, sorted(range(n), key=lambda i: (-(back[i] + ops[i]["cost"]), i)), fwd, zero)
@@ -193,6 +219,79 @@ def plan_calls(ops):
             jit = np.random.default_rng(SEED + _).uniform(1 - JIT, 1 + JIT, n).tolist()
             for i in range(n - 1, -1, -1):
                 level[i] = ops[i]["cost"] * jit[i] + max([level[j] + d for j, d in bwd[i]] + [lats[i], 0.98 * true[i]])
+    rng = np.random.default_rng(SEED)
+    start = best_start
+    done = lambda st, i: st[i] + ops[i]["cost"] + lats[i]
+    marks = [i for i in range(n) if ops[i]["key"] == "mark"] + [None]
+    for w in list(range(len(marks))) * SWEEPS:
+        lo = start[marks[w - 1]] if w else -1.0
+        hi = start[marks[w]] + 3.0 if marks[w] is not None else 1e9
+        free = [i for i in range(n) if lo < start[i] <= hi]
+        near = [i for i in range(n) if lo - 8.0 < start[i] <= lo]
+        some = [i for i in free if ops[i]["q"] in ("V", "S", "T", "G")]
+        inside = set(free)
+
+        def score(st):
+            if marks[w] is None:
+                return max(done(st, i) for i in free) + SPREAD * sum(st[i] for i in free) / len(free)
+            m = st[marks[w]]
+            return m + SPREAD * sum(st[i] for i in free) / len(free) + LATE * sum(ops[i]["cost"] for i in some if st[i] > m)
+
+        def held_up(st, sq):
+            before = {b: a for ln in sq.values() for a, b in zip(ln, ln[1:])}
+            i = marks[w] if marks[w] is not None else max(free, key=lambda i: done(st, i))
+            out = []
+            while i in inside:
+                j = max(fwd[i], key=lambda e: st[e[0]] + ops[e[0]]["cost"] + e[1], default=None)
+                if j is not None and st[j[0]] + ops[j[0]]["cost"] + j[1] >= st[i] - 1e-9:
+                    i = j[0]
+                elif i in before:
+                    if before[i] in inside:
+                        out.append((before[i], i))
+                    i = before[i]
+                else:
+                    break
+            return out, before
+
+        cur, cur_seq = place(ops, sorted(free, key=lambda i: (start[i], i)), fwd, zero, start, near)
+        best = now = score(cur)
+        keep = cur
+        pairs, before = held_up(cur, cur_seq)
+        for _ in range(MOVES):
+            key = {i: cur[i] + 1e-7 * i for i in free}
+            u = rng.random()
+            if u < 0.3 or not pairs:
+                i = some[int(rng.integers(0, len(some)))]
+                sign = -1 if rng.random() < 0.5 else 1
+                key[i] += sign * float(rng.uniform(0.2, 5.0))
+            else:
+                j, i = pairs[int(rng.integers(0, len(pairs)))]
+                if u < 0.65:
+                    for _s in range(int(rng.integers(0, 4))):
+                        if before.get(j) in inside:
+                            j = before[j]
+                    sign, key[i] = -1, key[j] - 1e-3
+                else:
+                    sign, key[j], i = 1, key[i] + float(rng.uniform(1e-3, 3.0)), j
+            edges = fwd if sign < 0 else bwd
+            todo = [i]
+            while todo:
+                a = todo.pop()
+                for b, d in edges[a]:
+                    if b in inside and sign * (key[a] - key[b]) >= 0:
+                        key[b] = key[a] + sign * 1e-5
+                        todo.append(b)
+            st, sq = place(ops, sorted(free, key=key.get), fwd, zero, start, near)
+            s = score(st)
+            if s <= now + HEAT * (1 - _ / MOVES) * rng.random():
+                now, cur = s, st
+                pairs, before = held_up(st, sq)
+                if s < best:
+                    best, keep = s, st
+        shift = keep[marks[w]] - start[marks[w]] if marks[w] is not None else 0.0
+        order = sorted(range(n), key=lambda i: (0, keep[i], i) if start[i] <= hi else (1, start[i], i))
+        start, seq = place(ops, order, fwd, zero)
+    best_end = max(start[i] + ops[i]["cost"] + lats[i] for i in range(n))
     ORDER["end"] = best_end
     pos = {}
     for q in seq:
@@ -220,7 +319,7 @@ def rank_program(g, core, T, topo):
         relay_program(g, core, T, topo)
         return
     ops = []
-    chain = [False, None]
+    chain = {"on": ()}
     Q = {"V": g.vector, "S": g.scalar, "T": g.tensor, "G": g, "Y": g.sync}
     ALL = slice(None)
 
@@ -237,8 +336,7 @@ def rank_program(g, core, T, topo):
             idx = tuple(slice(0, n) for n in shape[1:])
         ap = T[name][(p,) + idx]
         cm = bits(shape[1:], idx)
-        reg = (name, 1, 1) if where == "psum" else (name, cm, bits([128], p))
-        return {"ap": ap, "reg": [reg], "n": cm.bit_count(), "w": 2 if d in (b16, u16) else 4, "ps": where == "psum"}
+        return {"ap": ap, "reg": [(name, cm, bits([128], p))], "n": cm.bit_count(), "w": 2 if d in (b16, u16) else 4, "ps": where == "psum"}
 
     def C(name, a, b, s=None, p=ALL):
         return R(name, slice(a, b, s), p=p)
@@ -246,7 +344,7 @@ def rank_program(g, core, T, topo):
     def IND(win, off):
         return {"ap": win["ap"].indirect(off["ap"]), "reg": win["reg"], "off": off["reg"], "n": 16 * off["n"], "w": 4, "ps": False}
 
-    def op(q, fn, outs, ins, dma=0, ext=None, two=False, key=None):
+    def op(q, fn, outs, ins, dma=0, ext=None, two=False, key=None, sent=None):
         rd, wr = [], []
         ins = [x for x in ins if isinstance(x, dict)]
         for x in ins:
@@ -256,8 +354,9 @@ def rank_program(g, core, T, topo):
             rd += x.get("off", [])
         n = outs[0]["n"] if outs else 0
         lat = 0.0
+        sct = None
         if ext:
-            cost, lat = 0.001, LREM
+            cost, lat = 0.001, LREM[key]
         elif dma:
             by = 128 * max([x["n"] * x["w"] for x in outs + ins])
             cost, lat = (1.0 if q == "G" else 0.2), 2.5 + by / (2e5 if dma > 0 else 4e4)
@@ -267,6 +366,7 @@ def rank_program(g, core, T, topo):
             cost = 0.15 + 2 * n * CYC
         elif "off" in outs[0]:
             cost = 0.05 + n * SCA * CYC
+            sct = outs[0]["reg"][0][0]
         elif any("off" in x for x in ins):
             cost = 0.06 + n * GAT * CYC
         elif q == "S":
@@ -276,10 +376,10 @@ def rank_program(g, core, T, topo):
             if two and not any(x["ps"] for x in ins):
                 f *= 2
             cost = max(0.066, n * f * CYC)
-        ops.append({"q": q, "fn": fn, "rd": rd, "wr": wr, "dma": dma, "ext": ext, "inc": False, "cost": cost, "lat": lat, "key": key,
-                    "after": chain[1] if chain[0] and q == "V" else None})
-        if chain[0] and q == "V":
-            chain[1] = len(ops) - 1
+        ops.append({"q": q, "fn": fn, "rd": rd, "wr": wr, "dma": dma, "ext": ext, "inc": False, "cost": cost, "lat": lat, "key": key, "sct": sct,
+                    "sent": sent, "after": chain.get(q) if q in chain["on"] and not (dma or sct) else None})
+        if q in chain["on"] and not (dma or sct):
+            chain[q] = len(ops) - 1
 
     def a_(x):
         return x["ap"] if isinstance(x, dict) else x
@@ -313,8 +413,24 @@ def rank_program(g, core, T, topo):
             kw["scale"] = a_(scale)
         op("S", lambda e: e.activation(o["ap"], a["ap"], f, **kw), [o], [a, bias, scale])
 
+    run = [None]
+
     def mm(o, l, r, st, sp):
         op("T", lambda e: e.matmul(o["ap"], l["ap"], r["ap"], st, sp), [o], [l, r])
+        bank = o["reg"][0][0]
+        if run[0] == (len(ops) - 2, bank):
+            new, old = ops.pop(), ops[-1]
+            if "T" in chain["on"]:
+                chain["T"] = len(ops) - 1
+            f0, f1 = old["fn"], new["fn"]
+            old["fn"] = lambda e: (f0(e), f1(e))[1]
+            old["rd"] += new["rd"]
+            old["wr"] += new["wr"]
+            old["cost"] += new["cost"]
+        run[0] = (len(ops) - 1, bank)
+
+    def cut():
+        run[0] = None
 
     def iota(o, pat, base, cm, isint=False):
         if isint:
@@ -331,7 +447,7 @@ def rank_program(g, core, T, topo):
 
     def dma(q, o, a, add=False, key=None):
         if add:
-            op(q, lambda e: e.dma_start(o["ap"], a["ap"], accum_op=A.add), [o], [a, o], dma=16)
+            op(q, lambda e: e.dma_start(o["ap"], a["ap"], accum_op=A.add), [o], [a, o], dma=16, key=key)
         else:
             op(q, lambda e: e.dma_start(o["ap"], a["ap"]), [o], [a], dma=16, key=key)
 
@@ -343,9 +459,10 @@ def rank_program(g, core, T, topo):
                 mask = topo.mask(core, to)
                 op("G", lambda e, ls: e.remote_dma(dst_ap, src["ap"], T.sem[sem], ls, pid, rid, mask), [], [src],
                    dma=-len(topo.engines(core, to)))
+        sent = len(ops) - 1
         for t2, s, via, d in routes(T, topo):
             if t2 == t and d == core:
-                op(None, None, [landed], [], ext=(sem, len(topo.engines(s if via is None else via, core))))
+                op(None, None, [landed], [], ext=(sem, len(topo.engines(s if via is None else via, core))), sent=sent, key=t)
 
     def Wr(name, r):
         return C(name, 15 - r, 143 - r)
@@ -385,9 +502,8 @@ def rank_program(g, core, T, topo):
     ts(PIc(5), PIc(0), 3, A.bitwise_and)
     ts(PIc(6), PIc(0), 7, A.bitwise_and)
     ts(PIc(7), PIc(0), 3, A.arith_shift_right, 1, A.bitwise_and)
-    for nm in ("NF", "QN"):
-        ms(C(nm, 0, 16), 0.0)
-        ms(C(nm, 272, 288), 0.0)
+    ms(C("NF", 0, 16), 0.0)
+    ms(C("NF", 272, 288), 0.0)
     ms(R("KF"), 0.0)
     ms(R("KD"), 0.0)
     cp(C("CL", 0, 7), C("PI", 1, 8))
@@ -402,10 +518,10 @@ def rank_program(g, core, T, topo):
     ts(R("LI"), R("TG"), CLc(0), A.add)
     ts(CLc(7), CLc(2), CLc(1), A.not_equal, 272.0, A.mult)
     ts(CLc(8), CLc(4), 16.0, A.mult, CLc(3), A.add)
-    tt(R("TF"), R("TF"), R("LI"), A.add)
+    tt(R("TF"), R("TF"), R("TG"), A.add)
     ts(CLc(8), CLc(8), CLc(7), A.add)
     ts(CLc(9), CLc(5), 16.0, A.mult, CLc(6), A.add)
-    cp(R("LMK"), R("TF"))
+    ts(R("LMK"), R("TF"), CLc(0), A.subtract, 15.0, A.add)
     ts(R("LK"), C("TG", 0, 4), 0.25, A.mult, CLc(8), A.add)
     ts(R("LKM"), R("TH"), CLc(9), A.add, CLc(7), A.add)
     ts(CLc(20), CLc(3), 2.0, A.mult, CLc(2), A.add)
@@ -424,7 +540,7 @@ def rank_program(g, core, T, topo):
     ts(CLc(21), CLc(14), CLc(13), A.subtract)
     ts(CLc(19), CLc(18), CLc(13), A.add)
     for nm, src, f in (("WM", "B0", 16384.0), ("WN", "B0", -8192.0), ("WP", "B0", 8192.0), ("CI", "ID", KOFF), ("NI", "ID", -1.0),
-                       ("WA", "B0", CLc(19)), ("WA0", "B0", CLc(21)), ("WA2", "B0", CLc(18)), ("P2", "ID", CLc(17))):
+                       ("WA", "B0", CLc(19)), ("WA0", "B0", CLc(21)), ("W2", "B0", 2.0), ("WB", "B0", -1.0), ("P2", "ID", CLc(17))):
         ts(R(nm), R(src), f, A.mult)
     ts(C("P2", 12, 128, 16), C("B0", 15, 128, 16), CLc(16), A.mult)
     cp(R("BF"), R("B0"))
@@ -452,7 +568,7 @@ def rank_program(g, core, T, topo):
 
     for tau in range(3):
         act(C("ZT", L * tau, L * tau + L), C("ZS", tau, 768, 3), AF.Copy)
-    for m0, m1 in ((0, 4), (4, 10), (10, 16)):
+    for m0, m1 in ((12, 16), (6, 12), (0, 6)):
         zexp(0, m0, m1)
     zexp(1)
     cp(C("KF", 16, 80), R("KC"))
@@ -476,27 +592,42 @@ def rank_program(g, core, T, topo):
         mm(PS(4 + hf), R("M1"), cols("VCB"), False, True)
         act(cols("AUX", PAD), PS(4 + hf), AF.Copy)
     act(R("ZB"), R("ZS"), AF.Identity, bias=64.0)
-    iota(R("KB"), [[0, 16], [1, 16]], 1, 0)
     iota(R("KA"), [[0, 16], [-1, 16]], 15, 0)
     for a, b in ((PAD, PAD + T0), (PAD + T0, PAD + GB), (PAD + GB, WT)):
         iota(C("IO", a, b), [[1, b - a]], a, 0)
     act(C("VP", PAD, PAD + T0), C("IO", PAD, PAD + T0), AF.Identity, bias=64.0, scale=CLc(15))
     dma("G", C("VP", PAD, PAD + T0), R("vn"), add=True)
     dma("G", C("VC", PAD, PAD + T0), R("VCB"))
-    for m in range(16):
-        tt(C("XS", L * m, L * m + L), IND(R("VN"), C("SO", 16 * m, 16 * m + 16)), R("ZG", m, ALL), A.max)
+
+    def own_sum(tau, c, src):
+        o = PS(DBANK[c % 2], 384, 448)
+        for r in range(16):
+            mm(o, Wr("WM", r), src(r), r == 0, False)
+        mm(o, R("CI"), C("ONE", 0, 64), False, True)
+        kn = C("KS", L * tau + 64 * c, L * tau + 64 * c + 64)
+        tt(kn, o, kn, A.add)
+
+    for c in range(3, -1, -1):
+        for m in range(4 * c + 3, 4 * c - 1, -1):
+            tt(C("XS", L * m, L * m + L), IND(R("VN"), C("SO", 16 * m, 16 * m + 16)), R("ZG", m, ALL), A.max)
+        own_sum(0, c, lambda r: CH("XS", c, r, 16))
     ts(R("BCF"), R("BC"), float(PAD), A.add)
     gfill(R("BR"), 0)
     dma("Y", R("BR", p=rows(12)), R("BCF"))
-    for nm, v0, v in (("RMAX", -BIG, 1.0), ("RMIN", BIG, -1.0), ("RZ", 0.0, 1.0)):
-        gfill(R(nm), int(v))
+    for nm, v0, v in (("RMAX", -BIG, -1.0), ("RMIN", BIG, 1.0), ("RL", -BIG, 0.0)):
+        ms(R(nm), v)
         ms(C(nm, 0, 256, 16), v0)
     gfill(C("VP", 0, PAD), 1024)
-    ms(C("KB", 15, 256, 16), 0.0)
+    ms(C("QN", 0, 16), 0.0)
+    ms(C("QN", 272, 288), 0.0)
     for hf in range(2):
         cp(C("QT", 512 * hf, 512 * hf + 512), C("NQ", 512 * hf, 512 * hf + 512))
     stile(1)
-    early = len(ops) - 1
+    ts(R("LM0"), C("TF", 0, 8), CLc(0), A.add)
+    ts(R("REV"), C("TG", 0, 8), CLc(0), A.subtract, 15.0, A.add)
+    for t in range(4):
+        ts(C("GID", 16 * t, 16 * t + 16), R("LI"), float(GB + L * t), A.add)
+    ts(R("GK"), R("GID"), KOFF + 4096.0 - CEN, A.add)
     iota(R("TRI"), [[0, 8], [-16, 2], [1, 32]], 0, 0)
     iota(C("X1", 0, 32), [[1, 16], [0, 2]], 0, 0)
     asel(R("FW"), [[-1, 16], [-16, 8], [0, 16]], A.is_equal, 0, 1)
@@ -515,7 +646,7 @@ def rank_program(g, core, T, topo):
         mm(PS(6, 0, 48), Wr("BF", r), C("BR", r, 768, 16), r == 0, r == 15)
     for r in range(16):
         mm(PS(7, 0, 48), Wr("B0", r), C("ZT", r, 768, 16), r == 0, r == 15)
-    act(R("THR"), PS(7, 0, 48), AF.Identity, bias=200.0 * 8192.0 + KOFF, scale=8192.0)
+    act(R("THR"), PS(7, 0, 48), AF.Identity, bias=200.0 * 8192.0 + KOFF - 4096.0, scale=8192.0)
     cp(R("BO"), PS(6, 0, 48))
     act(R("VB"), IND(C("VP", 0, PAD + T0), R("BO")), AF.Copy)
     dma("Y", R("IDB", p=rows(9)), R("IHI"))
@@ -528,32 +659,44 @@ def rank_program(g, core, T, topo):
     gfill(R("RZ2"), 1)
     gfill(C("IO", 0, PAD), PAD - 1)
     ms(C("RZ2", 0, 512, 32), 0.0)
-    if SDUP:
-        ts(R("RB"), R("RZ2"), -BIG, A.mult, BIG, A.add)
-        act(R("IDF"), R("ID"), AF.Copy)
-        act(R("NIF"), R("NI"), AF.Copy)
     for a in range(PAD + T0, WT, L):
         act(C("VP", a, a + L), C("IO", a, a + L), AF.Identity, bias=64.0, scale=CLc(15))
 
-    def own_dist(tau):
+    turn = [4, 5, 6, 0, 1]
+    held = set()
+
+    def next_bank(banks=(4, 5, 6)):
+        b = [x for x in turn if x in banks and x not in held][0]
+        turn.remove(b)
+        turn.append(b)
+        return b
+
+    def own_dist(tau, c0):
         zx = "ZX%d" % tau
-        for c in range(4):
+        for c in (c0,):
             src = "GA" if c % 2 == 0 else "VCB"
+            so = L * tau + 64 * c
+            if c not in OPT["OWNS"][tau]:
+                for a in range(0, 1024, 512):
+                    tt(C(src, a, a + 512), IND(R("VN"), C("SO", so + a // 16, so + a // 16 + 32)), C(zx, 1024 * c + a, 1024 * c + a + 512), A.max)
+                own_sum(tau, c, lambda r: C(src, r, 1024, 16))
+                continue
             for a in range(0, 1024, PG):
-                so = L * tau + 64 * c + a // 16
-                act(C(src, a, a + PG), IND(R("VN"), C("SO", so, so + PG // 16)), AF.Copy)
+                act(C(src, a, a + PG), IND(R("VN"), C("SO", so + a // 16, so + (a + PG) // 16)), AF.Copy)
             for a in range(0, 1024, PA):
-                mm(PS(7, 0, PA), R("ID"), C(src, a, a + PA), True, False)
-                mm(PS(7, 0, PA), R("NI"), C(zx, 1024 * c + a, 1024 * c + a + PA), False, True)
-                act(C("GC", a, a + PA), PS(7, 0, PA), AF.Abs)
-            o = PS(0, 64 * c, 64 * c + 64)
+                b = next_bank()
+                mm(PS(b, 0, PA), R("ID"), C(src, a, a + PA), True, False)
+                mm(PS(b, 0, PA), R("NI"), C(zx, 1024 * c + a, 1024 * c + a + PA), False, True)
+                act(C("GC", a, a + PA), PS(b, 0, PA), AF.Abs)
+            o = PS(DBANK[c % 2], 384, 448)
             for r in range(16):
                 mm(o, Wr("WP", r), CH(zx, c, r, 16), r == 0, False)
             mm(o, R("CI"), C("ONE", 0, 64), False, False)
+            cut()
             for r in range(16):
                 mm(o, Wr("WP", r), C("GC", r, 1024, 16), False, r == 15)
-        kn = C("KS", L * tau, L * tau + L)
-        tt(kn, PS(0, 0, L), kn, A.add)
+            kn = C("KS", so, so + 64)
+            tt(kn, o, kn, A.add)
 
     for t in range(5):
         tau = TILE[t]
@@ -561,215 +704,270 @@ def rank_program(g, core, T, topo):
         wend = PAD + (T0 if t < 3 else GB + L * (t - 2))
         aend = PAD + (T0 if t == 0 else GB + L * t)
         own = PAD + T0 + L * t
-        ks = C("KS", L * tau, L * tau + L)
-        for c in range(4):
+        ld = L * (t - 1)
+        gcol = PAD + GB + ld
+        H = lambda nm, h, o=0: C(nm, o + 128 * h, o + 128 * h + 128)
+        M = lambda nm, h, o=0: C(nm, o + 8 * h, o + 8 * h + 8)
+        last = lambda nm: C(nm, 15, 256, 16)
+        for c in range(3, -1, -1):
             so = C("SO", L * tau + 64 * c, L * tau + 64 * c + 64)
             act(CH("XA", c), IND(C("AUX", PAD, wend), so), AF.Copy)
             tt(CH("XM", c), IND(R("VCB") if t == 0 else C("VC", PAD, wend), so), CH(zx, c), A.max)
-            for b, x, wa in ([(1, "XS", "WA0")] if t == 0 else []) + [(0, "XM", "WA")]:
-                o = PS(b, 64 * c, 64 * c + 64)
+            if t < 3 and c not in OPT["OWNS"].get(t, ()):
+                o = PS(DBANK[c % 2], 0, 64)
                 for r in range(16):
-                    mm(o, Wr(wa, r), CH("XA", c, r, 16), r == 0, False)
-                for r in range(16):
-                    mm(o, Wr("WM", r), CH(x, c, r, 16), False, False)
-                mm(o, R("CI"), C("ONE", 0, 64), False, True)
-        if t == 0:
-            tt(ks, PS(1, 0, L), ks, A.add)
-            ops[-1]["after"] = early
+                    mm(o, Wr("WA0", r), CH("XA", c, r, 16), r == 0, r == 15)
+                kn = C("KS", L * tau + 64 * c, L * tau + 64 * c + 64)
+                tt(kn, o, kn, A.add)
+            o = PS(0, 64 * c, 64 * c + 64)
+            for r in range(16):
+                mm(o, Wr("WA", r), CH("XA", c, r, 16), r == 0, False)
+            cut()
+            for r in range(16):
+                mm(o, Wr("WM", r), CH("XM", c, r, 16), False, False)
+            mm(o, R("CI"), C("ONE", 0, 64), False, True)
+        if t >= 1:
+            for h in (1, 0):
+                if h in OPT["GV"]:
+                    tt(H("VP", h, gcol), H("LAND", h, ld), H("VP", h, gcol), A.add)
+                else:
+                    dma("G", H("VP", h, gcol), H("LAND", h, ld), add=True)
+            tt(R("XG"), C("LAND", ld, ld + L), C("ZT", L * tau, L * tau + L), A.max)
+            o = R("PS3", 16, ALL)
+            for r in range(16):
+                mm(o, Wr("WN", r), C("LAND", ld + r, ld + L, 16), r == 0, False)
+            cut()
+            for r in range(16):
+                mm(o, Wr("WM", r), C("XG", r, L, 16), False, r == 15)
+            tt(R("KM"), o, C("GK", 16 * t - 16, 16 * t), A.add)
+            ts(R("GD"), R("KM"), MAGIC, A.add, MAGIC, A.subtract)
+        k2, dp = PS(0, L, 2 * L), PS(1, 0, L)
+        tt(k2, PS(0, 0, L), C("KS", L * tau, L * tau + L), A.min)
+        ts(dp, k2, MAGIC, A.add, MAGIC, A.subtract)
+        scan(R("SMN"), R("RMIN"), dp, A.add, A.min)
+        tt(R("NM"), R("SMN"), dp, A.not_equal)
+        scan(R("SM2"), R("NM"), k2, A.mult, A.min)
+        ts(R("S1"), last("SM2"), CEN, A.add)
+        ts(R("AI"), R("S1"), 4095, A.bitwise_and)
+        if t >= 1:
+            scan(R("SMX"), R("RMAX"), dp, A.add, A.max)
+            ts(R("S3"), last("SMX"), -1.0, A.mult)
+            ts(R("S2"), R("S3"), 15, A.bitwise_and)
+            tt(R("YG"), last("SMN"), R("GD"), A.subtract)
+            tt(R("GW"), R("S2"), R("YG"), A.is_lt)
+            tt(R("GW"), R("GW"), C("GID", 16 * t - 16, 16 * t), A.mult)
+            tt(R("AF"), R("AI"), R("GW"), A.max)
+            par = R("AF")
         else:
-            gs = GB - T0 + L * (t - 1)
-            ld = L * (t - 1)
-            gcol = PAD + GB + ld
-            land = C("LAND", ld, ld + L)
-            dma("G", C("VP", gcol, gcol + L), land, add=True)
-            tt(R("XG"), land, C("ZT", L * tau, L * tau + L), A.max)
-            o = PS(2, 0, 16)
-            for r in range(16):
-                mm(o, Wr("WA2", r), C("IDB", gs + r, gs + L, 16), r == 0, False)
-            for r in range(16):
-                mm(o, Wr("WN", r), C("LAND", ld + r, ld + L, 16), False, False)
-            for r in range(16):
-                mm(o, Wr("WM", r), C("XG", r, L, 16), False, False)
-            mm(o, R("CI"), C("ONE", 0, 16), False, True)
-            act(R("KM"), o, AF.Copy)
+            par = R("AI")
+        cp(R("A16"), par)
+        ops[-1]["key"] = "mark"
+        act(C("QN", 16, 272), IND(C("QT", 0, aend - PAD), R("A16")), AF.Copy)
+        for va, sc in (("NVA", -1.0), ("VAF", 1.0)):
+            for h in (1, 0):
+                act(C(va, 512 * h, 512 * h + 128), IND(C("VP", PAD, aend), M("A16", h)), AF.Copy, scale=sc)
+                for j in range(1, 4):
+                    dma("Y", C(va, 512 * h + 128 * j, 512 * h + 128 * j + 128), C(va, 512 * h, 512 * h + 128), key=(va, h, j))
+        tr(C("Y", 0, 256), C("QN", 16, 272))
+        tr(C("Y", 256, 544), R("QN"))
+        for h in (1, 0):
+            cp(H("QO", h), IND(R("Y"), M("LKM", h)))
+        if t >= 1:
+            tt(R("E"), IND(R("S2"), R("LB")), R("KA"), A.is_equal)
+            tt(R("E2"), IND(R("KM"), R("LB")), R("E"), A.mult)
+            tt(R("K3"), k2, R("E2"), A.min)
+            k3 = R("K3")
+        else:
+            k3 = k2
+        scan(R("SMX"), R("RL"), k3, A.add, A.max)
+        ts(R("U"), par, float(PAD), A.add)
+        tt(R("LV"), last("SMX"), C("THR", 16 * tau, 16 * tau + 16), A.is_ge)
+        tt(R("U"), R("U"), R("LV"), A.mult)
+        tt(R("AD"), R("U"), R("LI"), A.max)
+        cp(R("AD16"), R("AD"))
+        act(C("VB", tau, 768, 3), IND(C("VP", 0, aend), R("AD16")), AF.Copy)
+        ts(R("SI"), k3, CEN, A.add, TOP, A.add)
         if t in (1, 2):
             po = own - L
+            gs = GB - T0 + ld
+            land = C("LAND", ld, ld + L)
             dma("G", C("VC", po, po + L), C("YV", L * (t - 1), L * t))
             dma("Y", C("AUX", po, po + L), C("AXN", 0, L))
             dma("G", C("VC", gcol, gcol + L), land)
-            mm(PS(1, 0, L), R("M1"), land, True, False)
-            mm(PS(1, 0, L), R("P2"), C("IDB", gs, gs + L), False, True)
-            act(C("AUX", gcol, gcol + L), PS(1, 0, L), AF.Copy)
-        k2 = PS(4, 0, L)
-        tt(k2, PS(0, 0, L), ks, A.min)
-        ts(R("DP"), k2, MAGIC, A.add, MAGIC, A.subtract)
-        if t >= 1:
-            scan(R("SM"), R("RMAX"), R("DP"), A.add, A.max)
-            cp(R("S1"), C("SM", 15, 256, 16))
-            ts(R("S2"), R("S1"), 15, A.bitwise_and)
-            tt(R("E"), IND(R("S2"), R("LB")), R("KA"), A.is_equal)
-            tt(R("E2"), IND(R("KM"), R("LB")), R("E"), A.mult)
-            tt(PS(5, 0, L), k2, R("E2"), A.min)
-            k2 = PS(5, 0, L)
-            ts(R("DP"), k2, MAGIC, A.add, MAGIC, A.subtract)
-        scan(R("SM"), R("RMIN"), R("DP"), A.add, A.min)
-        cp(R("S1"), C("SM", 15, 256, 16))
-        ts(R("S2"), R("S1"), 15, A.bitwise_and)
-        tt(R("E"), IND(R("S2"), R("LB")), R("KB"), A.is_equal)
-        tt(R("E2"), k2, R("E"), A.mult)
-        scan(R("SM"), R("RZ"), R("E2"), A.mult, A.min)
-        ts(R("S1"), C("SM", 15, 256, 16), CEN, A.add)
-        ts(R("AI"), R("S1"), 4095, A.bitwise_and)
-        cp(R("A16"), R("AI"))
-        act(C("QN", 16, 272), IND(C("QT", 0, aend - PAD), R("A16")), AF.Copy)
-        for h in (1, 0):
-            for va in ("VAB", "VAF"):
-                act(C(va, 512 * h, 512 * h + 128), IND(C("VP", PAD, aend), C("A16", 8 * h, 8 * h + 8)), AF.Copy)
-                for j in range(1, 4):
-                    dma("Y", C(va, 512 * h + 128 * j, 512 * h + 128 * j + 128), C(va, 512 * h, 512 * h + 128), key=(va, h, j))
-        scan(R("E"), R("RMAX"), R("DP"), A.add, A.max)
-        ts(R("U"), R("AI"), float(PAD), A.add)
-        ts(R("SI"), k2, CEN, A.add)
-        tt(R("LV"), C("E", 15, 256, 16), C("THR", 16 * tau, 16 * tau + 16), A.is_ge)
-        tt(R("U"), R("U"), R("LI"), A.subtract)
-        tt(R("U"), R("U"), R("LV"), A.mult)
-        tt(R("AD"), R("U"), R("LI"), A.add)
-        cp(R("AD16"), R("AD"))
-        tr(C("Y", 0, 256), C("QN", 16, 272))
-        tr(C("Y", 256, 544), R("QN"))
-        cp(R("QO"), IND(R("Y"), R("LKM")))
+            b = next_bank()
+            mm(PS(b, 0, L), R("M1"), land, True, False)
+            mm(PS(b, 0, L), R("P2"), C("IDB", gs, gs + L), False, True)
+            act(C("AUX", gcol, gcol + L), PS(b, 0, L), AF.Copy)
         if t < 4:
             hand_on(t, C("QN", 16, 272), qslot(T, t), C("QT", GB + L * t, GB + L * t + L), "aq%d" % t)
             dma("Y", C("QT", own - PAD, own - PAD + L), C("QN", 16, 272))
-        act(C("VB", tau, 768, 3), IND(C("VP", 0, aend), R("AD16")), AF.Copy)
         if t == 0:
             zexp(2)
             stile(2)
-        if t < 2:
-            own_dist(t + 1)
-        ts(R("SI2"), R("SI"), 4095, A.bitwise_and)
-        if t in (1, 2):
-            cp(C("SO", L * tau, L * tau + L), R("SI2"))
-            tt(R("SM"), R("DP"), R("SI2"), A.add)
-            act(ks, R("SM"), AF.Identity, bias=-CEN)
-        else:
-            ts(C("NF", 16, 144), C("SI2", 128, 256), 4096.0, A.mult)
-            tt(C("NF", 16, 144), C("NF", 16, 144), C("SI2", 0, 128), A.add)
-            tr(C("Y", 0, 128), C("NF", 16, 144))
-            tr(C("Y", 256, 416), C("NF", 0, 160))
-            act(C("YS", tau, 384, 3), IND(R("Y"), C("LMK", 0, 8)), AF.Copy)
-            act(C("YB", tau, 768, 3), IND(C("IO", 0, aend), R("AD16")), AF.Identity, bias=-float(PAD))
-        cp(R("OX"), IND(R("AD"), R("LX")))
-        tt(R("U2"), R("LI"), R("AD"), A.subtract)
-        if t in SDUP:
-            act(R("X1"), IND(C("IO", 0, aend), R("OX")), AF.Copy)
-            act(R("X2"), IND(R("AD"), R("LB2")), AF.Copy)
-            mm(PS(7), R("IDF"), R("TRI"), True, False)
-            mm(PS(7), R("IDF"), R("X1"), False, False)
-            mm(PS(7), R("NIF"), R("X2"), False, True)
-            act(R("X2"), PS(7), AF.Abs)
-            scan(R("X1"), R("RB"), R("X2"), A.add, A.min)
-            ts(R("LV"), C("X1", 31, 512, 32), 0.0, A.is_equal)
-            tt(R("U2"), R("U2"), R("LV"), A.mult)
-        else:
+        for h in (1, 0):
+            ts(H("VA", h), C("NVA", 512 * h, 512 * h + 128), -1.0, A.mult, -64.0, A.add)
+        ts(R("LO"), R("VA"), -2.0, A.add, 0.0, A.max)
+        ts(R("HI"), R("VA"), 2.0, A.add, 63.0, A.min)
+
+        def lists():
+            ts(R("SI2"), R("SI"), 4095, A.bitwise_and)
+            if t in (1, 2):
+                cp(C("SO", L * tau, L * tau + L), R("SI2"))
+                ts(R("SI"), R("SI"), 2 ** 24 - 1 - 4096, A.bitwise_and)
+                ts(C("KS", L * tau, L * tau + L), R("SI"), -TOP, A.add, -CEN, A.add)
+            else:
+                ts(C("E", 0, 128), IND(C("SI2", 128, 256), R("REV")), 4096.0, A.mult)
+                tt(C("NF", 16, 144), IND(C("SI2", 0, 128), R("REV")), C("E", 0, 128), A.add)
+                tr(C("Y", 0, 128), C("NF", 16, 144))
+                tr(C("Y", 256, 416), C("NF", 0, 160))
+                act(C("YS", tau, 384, 3), IND(R("Y"), R("LM0")), AF.Copy)
+                act(C("YB", tau, 768, 3), IND(C("IO", 0, aend), R("AD16")), AF.Identity, bias=-float(PAD))
+            if t == 4:
+                dma("Y", R("ys"), R("YS"))
+                dma("Y", R("yb"), R("YB", p=rows(0)))
+
+        def lowest():
+            cp(R("OX"), IND(R("AD"), R("LX")))
+            tt(R("U2"), R("LI"), R("AD"), A.subtract)
             tt(R("X1"), IND(C("IO", 0, aend), R("OX")), R("TRI"), A.add)
             tt(R("X2"), IND(R("AD"), R("LB2")), R("X1"), A.is_equal)
             scan(R("X1"), R("RZ2"), R("X2"), A.mult, A.max)
             tt(R("U2"), R("U2"), C("X1", 31, 512, 32), A.mult)
-        tt(R("U2"), R("U2"), R("AD"), A.add)
-        cp(R("O1"), R("U2"))
-        if t == 4:
-            dma("Y", R("ys"), R("YS"))
-            dma("Y", R("yb"), R("YB", p=rows(0)))
-            mm(PS(0, 0, L), R("P2"), C("IDB", L * t, L * t + L), True, True)
-            act(C("AXN", L, 2 * L), PS(0, 0, L), AF.Copy)
-            for b in range(7, -1, -1):
-                cp(IND(R("AUX"), C("O1", 2 * b, 2 * b + 2)), C("AXN", L + 32 * b, L + 32 * b + 32))
-            dma("Y", R("yk"), C("AUX", PAD, WT, p=rows(12)))
-        def diffs(h, x, c):
-            b = 2 - h
-            win, va, ab, pc = ("ZB", "VAB", "A1", 0) if x == "D1" else ("VB", "VAF", "A2", 128)
-            for u in range(2 * c, 2 * c + 2):
-                o, q0 = 2048 * h + 512 * u, 128 * h + 32 * u
-                if x == "D1" and h == 0 and u < SQUAD[t]:
-                    gz = C("GZ", 512 * (u % 2), 512 * (u % 2) + 512)
-                    act(gz, IND(R(win), C("QO", q0, q0 + 32)), AF.Copy)
-                    mm(PS(0), R("ID"), gz, True, False)
-                    mm(PS(0), R("NI"), C(va, 0, 512), False, True)
-                    act(C(x, o, o + 512), PS(0), AF.Copy)
-                elif x == "D1" and h == 1 and u < NSMALL:
-                    for k in range(4):
-                        tt(C(x, o + 128 * k, o + 128 * k + 128), IND(R(win), C("QO", q0 + 8 * k, q0 + 8 * k + 8)),
-                           C(va, 512 * h, 512 * h + 128), A.subtract)
+            tt(R("U2"), R("U2"), R("AD"), A.add)
+            cp(R("O1"), R("U2"))
+            if t == 4:
+                ub = next_bank()
+                mm(PS(ub, 0, L), R("P2"), C("IDB", L * t, L * t + L), True, True)
+                act(C("AXN", L, 2 * L), PS(ub, 0, L), AF.Copy)
+                for b in range(7, -1, -1):
+                    cp(IND(R("AUX"), C("O1", 2 * b, 2 * b + 2)), C("AXN", L + 32 * b, L + 32 * b + 32))
+                dma("Y", R("yk"), C("AUX", PAD, WT, p=rows(12)))
+
+        raw, sized, sbank = set(), set(), {}
+
+        def gather(h, x, u, how):
+            win, va, f = ("ZB", "NVA", A.add) if x == 1 else ("VB", "VAF", A.subtract)
+            o, q0 = 2048 * h + 512 * u, 128 * h + 32 * u
+            d = lambda a, e: C("D%d" % x, o + a, o + e)
+            if how == "T":
+                act(d(0, 512), IND(R(win), C("QO", q0, q0 + 32)), AF.Copy)
+                ub = next_bank()
+                mm(PS(ub), R("ID"), d(0, 512), True, False)
+                for k in range(4):
+                    mm(PS(ub, 128 * k, 128 * k + 128), R("ID"), C(va, 512 * h, 512 * h + 128), False, k == 3)
+                act(C("A1", o, o + 512), PS(ub), AF.Abs)
+                raw.add((h, u))
+            elif how == "D":
+                act(d(0, 512), IND(R(win), C("QO", q0, q0 + 32)), AF.Copy)
+                dma("G", d(0, 512), C(va, 512 * h, 512 * h + 512), add=True, key=("sd", h, u))
+            elif how == "v":
+                for k in range(4):
+                    tt(d(128 * k, 128 * k + 128), IND(R(win), C("QO", q0 + 8 * k, q0 + 8 * k + 8)), C(va, 512 * h, 512 * h + 128), f)
+            else:
+                tt(d(0, 512), IND(R(win), C("QO", q0, q0 + 32)), C(va, 512 * h, 512 * h + 512), f)
+
+        def size(h, x, c, how):
+            d, ab, b = "D%d" % x, "A%d" % x, DBANK[h]
+            o = PS(b, 128 * x - 128 + 64 * c, 128 * x - 64 + 64 * c)
+            parts = [(a, a + 512) for a in (2048 * h + 1024 * c, 2048 * h + 1024 * c + 512) if x == 2 or (h, a % 2048 // 512) not in raw]
+            if how == "S" and len(parts) == 2:
+                parts = [(parts[0][0], parts[1][1])]
+            for a, e in parts:
+                if how == "V":
+                    ts(C(ab, a, e), C(d, a, e), 0.0, A.max, 64.0, A.min)
                 else:
-                    tt(C(x, o, o + 512), IND(R(win), C("QO", q0, q0 + 32)), C(va, 512 * h, 512 * h + 512), A.subtract)
-            act(CH(ab, 2 * h + c), CH(x, 2 * h + c), AF.Abs)
+                    act(C(ab, a, e), C(d, a, e), AF.Abs)
+            if how == "V":
+                for r in range(16):
+                    mm(o, Wr("WB", r), CH(d, 2 * h + c, r, 16), r == 0, False)
+                cut()
+            else:
+                sized.add((h, x))
             for r in range(16):
-                mm(PS(b, pc + 64 * c, pc + 64 * c + 64), Wr("B0", r), CH(ab, 2 * h + c, r, 16), r == 0, r == 15)
-            if x == "D1" and c == 1:
-                act(C("D1M", 128 * h, 128 * h + 128), PS(b, 0, 128), AF.Identity, bias=-0.5)
+                mm(o, Wr("W2" if how == "V" else "B0", r), CH(ab, 2 * h + c, r, 16), r == 0 and how != "V", r == 15)
+            if x == 1 and c == 1:
+                act(H("D1M", h), PS(b, 0, 128), AF.Identity, bias=-0.5)
 
         def attract(h):
-            hs = lambda nm, o=0: C(nm, o + 128 * h, o + 128 * h + 128)
-            d2 = PS(2 - h, 128, 256)
-            tt(hs("N2"), hs("D1M"), d2, A.subtract)
-            ts(hs("N1"), d2, 1100.0, A.is_gt)
-            tt(hs("N2"), hs("N2"), d2, A.min)
-            ts(hs("N3"), hs("N2"), 0.0, A.is_gt)
-            tt(hs("NA"), hs("N3"), hs("N1"), A.add)
+            d2 = PS(DBANK[h], 128, 256)
+            tt(H("N1", h), H("D1M", h), d2, A.is_gt)
+            ts(H("N2", h), d2, 0.0, A.not_equal)
+            if (h, 2) in sized:
+                ts(H("N3", h), d2, 1100.0, A.is_gt)
+                tt(H("N1", h), H("N1", h), H("N3", h), A.add)
+            tt(H("NA", h), H("N1", h), H("N2", h), A.mult)
 
-        chain[:] = [True, None]
-        for step in STEP4:
-            if len(step) == 1:
-                attract(step[0])
+        def col(ub, r, a=0, e=128):
+            return R("PS%d" % ub, slice(a, e), r % 4) if ub in (4, 5, 6) else C("PS%d" % ub, 4 * a + r % 4, 4 * e, 4)
+
+        def ahead(h, rc):
+            ub = sbank[h, rc] = next_bank((4, 5, 6, 0, 1))
+            held.add(ub)
+            for r in range(4 * rc, 4 * rc + 4):
+                mm(col(ub, r), R("ID"), C("D1", 2048 * h + r, 2048 * h + 2048, 16), r % 4 == 0, False)
+                for u in range(4):
+                    if (h, u) in raw:
+                        mm(col(ub, r, 32 * u, 32 * u + 32), R("ID"), C("NVA", 512 * h + r, 512 * h + 512, 16), False, False)
+            cut()
+
+        def sign(h, rc, how):
+            if (h, rc) not in sbank:
+                ahead(h, rc)
+            ub = sbank[h, rc]
+            held.discard(ub)
+            for r in range(4 * rc, 4 * rc + 4):
+                mm(col(ub, r), C("FW", 128 * r, 128 * r + 128), H("NA", h), False, r % 4 == 3)
+            sg = R("SG", slice(128 * h, 128 * h + 128), slice(4 * rc, 4 * rc + 4))
+            if how == "V":
+                ts(sg, PS(ub), -1.0, A.max, 1.0, A.min)
             else:
-                diffs(*step)
-        chain[0] = False
-        for h in (1, 0):
-            b = 2 - h
-            hs = lambda nm, o=0: C(nm, o + 128 * h, o + 128 * h + 128)
-            vab = C("VAB", 512 * h, 512 * h + 128)
-            act(R("VAU", slice(8 * h, 8 * h + 8), ALL), vab, AF.Identity, bias=-64.0)
-            if h == 0:
-                attract(0)
+                act(sg, PS(ub), AF.Sign)
+
+        def count(h):
+            b, mh = DBANK[h], slice(8 * h, 8 * h + 8)
             for k in range(16):
                 mm(PS(b, 0, 8), R("ID"), C("NA", 128 * h + 8 * k, 128 * h + 8 * k + 8), k == 0, k == 15)
-            act(C("CN", 8 * h, 8 * h + 8), PS(b, 0, 8), AF.Identity, scale=-1.0 / 128.0)
-            for rc in range(4):
-                ub = 4 + (rc + 4 * (1 - h) + 2) % 3
-                for r in range(4 * rc, 4 * rc + 4):
-                    o = R("PS%d" % ub, ALL, r % 4)
-                    mm(o, R("ID"), C("D1", 2048 * h + r, 2048 * h + 2048, 16), True, False)
-                    mm(o, C("FW", 128 * r, 128 * r + 128), hs("NA"), False, True)
-                sg = R("SG", slice(128 * h, 128 * h + 128), slice(4 * rc, 4 * rc + 4))
-                if (h, rc) in VSIGN:
-                    ts(sg, PS(ub), -1.0, A.max, 1.0, A.min)
-                else:
-                    act(sg, PS(ub), AF.Sign)
-            for c in range(2):
-                rc, mh = slice(8 * c, 8 * c + 8), slice(8 * h, 8 * h + 8)
-                o = R("PS3", mh, rc)
-                for k in range(16):
-                    mm(o, R("ID"), R("SG", slice(128 * h + 8 * k, 128 * h + 8 * k + 8), rc), k == 0, False)
-                for r in range(8 * c, 8 * c + 8):
-                    mm(R("PS3", mh, r), C("FW", 128 * r, 128 * r + 128), C("CN", 8 * h, 8 * h + 8), False, r == 8 * c + 7)
-            ts(hs("H1"), R("PS3", slice(8 * h, 8 * h + 8), ALL), -2.0, A.max, 2.0, A.min)
-            tt(hs("H1"), hs("H1"), R("VAU", slice(8 * h, 8 * h + 8), ALL), A.add)
-            ts(hs("YV", L * t), hs("H1"), 0.0, A.max, 63.0, A.min)
-            if t < 4:
-                hand_on(t, hs("YV", L * t), nslot(T, t, h), hs("LAND", L * t), "an%d" % (2 * t + h))
-            if t < 4:
-                mm(PS(b, 0, 128), R("P2"), hs("IDB", L * t), True, False)
-                mm(PS(b, 0, 128), R("M1"), hs("YV", L * t), False, True)
-                act(hs("AXN"), PS(b, 0, 128), AF.Copy)
-                for bl in range(4 * h + 3, 4 * h - 1, -1):
-                    cp(IND(R("VC"), C("O1", 2 * bl, 2 * bl + 2)), C("YV", L * t + 32 * bl, L * t + 32 * bl + 32))
-                for bl in range(4 * h + 3, 4 * h - 1, -1):
-                    cp(IND(R("AUX"), C("O1", 2 * bl, 2 * bl + 2)), C("AXN", 32 * bl, 32 * bl + 32))
+            act(M("CN", h), PS(b, 0, 8), AF.Identity, scale=-1.0 / 128.0)
+            mm(R("PS3", mh, ALL), R("ID"), H("VA", h), True, False)
+            cut()
+            for r in range(16):
+                mm(R("PS3", mh, r), C("FW", 128 * r, 128 * r + 128), M("CN", h), False, False)
+            cut()
+
+        def pull(h, c):
+            mh, rc = slice(8 * h, 8 * h + 8), slice(8 * c, 8 * c + 8)
+            for k in range(16):
+                mm(R("PS3", mh, rc), R("ID"), R("SG", slice(128 * h + 8 * k, 128 * h + 8 * k + 8), rc), False, c == 1 and k == 15)
+            cut()
+
+        def finish(h):
+            tt(H("H1", h), R("PS3", slice(8 * h, 8 * h + 8), ALL), H("HI", h), A.min)
+            tt(H("YV", h, L * t), H("H1", h), H("LO", h), A.max)
+            if t == 4:
+                dma("Y", H("yv", h, L * t), H("YV", h, L * t))
+                return
+            hand_on(t, H("YV", h, L * t), nslot(T, t, h), H("LAND", h, L * t), "an%d" % (2 * t + h))
+            o = PS(DBANK[h], 256, 384)
+            mm(o, R("P2"), H("IDB", h, L * t), True, False)
+            if t < 2:
+                mm(o, R("M2"), H("VA", h), False, False)
+            cut()
+            mm(o, R("M1"), H("YV", h, L * t), False, True)
+            act(H("AXN", h), o, AF.Copy)
+            for bl in range(4 * h + 3, 4 * h - 1, -1):
+                cp(IND(R("VC"), C("O1", 2 * bl, 2 * bl + 2)), C("YV", L * t + 32 * bl, L * t + 32 * bl + 32))
+                cp(IND(R("AUX"), C("O1", 2 * bl, 2 * bl + 2)), C("AXN", 32 * bl, 32 * bl + 32))
+
+        steps = {"g": gather, "z": size, "a": attract, "i": ahead, "s": sign, "c": count, "p": pull, "f": finish, "l": lists, "d": lowest,
+                 "o": lambda c: own_dist(t + 1, c) if t < 2 else None}
+        for w in OPT["STEP4"][t].split():
+            chain["on"] = () if w[0] in "ldo" else OPT["CHAIN"]
+            steps[w[0]](*[int(x) if x.isdigit() else x for x in w[1:]])
+        chain["on"] = ()
         new = C("YV", L * t, L * t + L)
         if t < 4:
             dma("G", C("VP", own, own + L), new, add=True)
-        dma("Y", C("yv", L * t, L * t + L), new)
+            dma("Y", C("yv", L * t, L * t + L), new)
 
     if "seq" not in ORDER:
         ORDER["seq"], ORDER["wait"] = plan_calls(ops)

@@ -13,53 +13,61 @@ BIG = 2.0 ** 26
 TOP = 2.0 ** 24
 KOFF = -2040.0 * 8192.0
 CEN = 3700.0
-CYC, CPE, WAKE, LREM, GAT, SCA = 0.00087, 0.00045, 0.2, (3.5, 0.5, 3.5, 0.5), 1.56, 3.8
+CYC, CPE, WAKE, LREM, GAT, SCA = 0.00087, 0.00045, 0.3, (5.0, 1.5, 5.0, 1.5), 1.56, 3.8
 PASSES, ROUNDS, BLEND, SEED, JIT = 1, 12, 0.3, 0, 0.3
-MOVES, SPREAD, LATE, HEAT, SWEEPS = 3000, 0.1, 0.3, 0.1, 1
+MOVES, SPREAD, LATE, HEAT, SWEEPS = 2000, 0.03, 0.3, 0.1, 4
+ONLY = None
+LQ = 14.0
+UNITS = [(8, 8), (0, 8)]
+UBANK, SBANK = [2, 7], (4, 5, 6, 0, 1)
+SENDS = [(128, 256), (0, 128)]
 NOWAIT = False
 OPT = {
-    "SQ": [()] * 5,
-    "SD": [((0, 0), (0, 1), (0, 2), (0, 3))] * 5,
-    "RELU": [((0, "D2", 0), (0, "D2", 1))] * 5,
-    "SMALL": ((1, "D1", 0), (1, "D1", 1)),
-    "VSIGN": ((0, 1), (0, 3)),
-    "OWNS": {1: (0, 1), 2: (0, 1)},
-    "GV": (0,),
+    "OWNS": {0: (0,), 1: (3, 1, 0), 2: (3, 2, 1, 0)},
+    "ZG": ((8, 16, "V"), (0, 8, "G")),
+    "GV": [(), (1,), (), (1,), ()],
+    "FIRST": ((3,), (3,)),
+    "EQ": "VVVVV",
+    "LATER": True,
+    "COPY": {"NVA": "VVVV", "VAF": "YYYY"},
+    "QO": ((8, 16), (0, 8)),
     "CHAIN": (),
-    "STEP4": ["o3 o2 o1 o0 d l g110v g010D g111v g011D g112V g012D g113V g013D z110S z111S i10 i11 i12 i13 g120V g121V z120S g122V g123V z121S g020V g021V "
-              "a1 z010S z011S g022V s10S s11S c1 z020S g023V s12S s13S z021V i00 i01 p10 a0 i02 p11 f1 s00S s01V s02S s03V c0 p00 p01 f0"] * 5,
+    "STEP4": ["o3 o2 g110D g111D g112D g113D g010V g011V z010S g012V g013V z011S g020V g021V z020S g022V g023V z021V d i00 i01 i02 i03 "
+              "z110S e10 z111S e11 g120V g121V z120S g122V g123V z121V a0 s00S c0V s01S s02S s03S p00 p01 f0 a1 c1M s10M s11M s12M s13M "
+              "p10 p11 f1 l o1 o0"] * 5,
 }
 PG, PA = 512, 512
 ORDER = {}
 
-f32, b16, i32, u16 = "float32", "bfloat16", "int32", "uint16"
+f32, b16, f16, i32, u16 = "float32", "bfloat16", "float16", "int32", "uint16"
 SCRATCH = {}
 for _n, _w, _d in [
     ("VN", 1024, b16), ("ZS", 768, b16), ("ZT", 768, b16), ("ZB", 768, b16), ("SN", 768, i32), ("NQ", 1024, i32),
-    ("KC", 64, i32), ("KF", 96, f32), ("KLO", 64, b16), ("KHI", 64, b16), ("KI", 64, i32), ("BC", 48, i32), ("BCF", 48, f32),
-    ("BR", 768, f32), ("KO", 64, u16), ("BO", 48, u16), ("VCB", 1024, b16),
+    ("KC", 64, i32), ("KF", 96, f32), ("KLO", 64, b16), ("KHI", 64, b16), ("KI", 128, i32), ("BC", 48, i32), ("BCF", 96, b16), ("BCI", 96, i32),
+    ("BR", 768, b16), ("KO", 64, u16), ("BO", 48, u16), ("VCB", 1024, b16),
     ("QT", W, f32), ("VP", WT, f32), ("VC", WT, f32), ("AUX", WT, f32), ("IO", WT, f32), ("VB", 768, f32),
-    ("IDB", 2304, b16), ("IC", 144, i32), ("IC2", 144, i32), ("ILO", 144, b16), ("IHI", 144, b16), ("GA", 1024, b16), ("GC", 1024, b16),
-    ("D1", 4096, b16), ("D2", 4096, b16), ("A1", 4096, b16), ("A2", 4096, b16), ("ZX0", 4096, b16), ("ZX1", 4096, b16), ("FW", 2048, b16),
-    ("B0", 144, b16), ("WM", 144, b16), ("WN", 144, b16), ("WP", 144, b16), ("WA", 144, b16), ("WA0", 144, b16), ("W2", 144, b16), ("WB", 144, b16), ("BF", 144, f32),
-    ("ID", 128, b16), ("NI", 128, b16), ("CI", 128, b16), ("M1", 128, b16), ("M2", 128, b16), ("P2", 128, b16), ("ONE", 144, b16),
-    ("PI", 8, i32), ("CL", 24, f32), ("TI", 16, i32), ("TF", 16, f32), ("TG", 16, f32), ("TH", 16, f32),
-    ("LMK", 16, u16), ("LM0", 8, u16), ("LKM", 16, u16), ("LK", 4, u16), ("LB", 16, u16), ("LB2", 32, u16), ("LX", 2, u16), ("REV", 8, u16), ("LI", 16, f32),
-    ("TRI", 512, f32), ("RMAX", 256, b16), ("RMIN", 256, b16), ("RL", 256, b16), ("RZ2", 512, b16), ("KA", 256, f32),
+    ("IDB", 2304, b16), ("ILO", 144, b16), ("IHI", 144, b16), ("GA", 1024, b16), ("GC", 1024, b16),
+    ("D1", 4096, b16), ("D2", 4096, b16), ("A1", 4096, b16), ("A2", 4096, b16), ("FW", 2048, b16), ("ZX0", 4096, b16), ("ZX1", 4096, b16),
+    ("B0", 144, b16), ("WM", 144, b16), ("WN", 144, b16), ("WP", 144, b16), ("WA", 144, b16), ("WA0", 144, b16), ("W2", 144, b16), ("WB", 144, b16), ("BF", 144, b16),
+    ("ID", 128, b16), ("NI", 128, b16), ("CI", 128, b16), ("MX", 132, b16), ("NJ", 128, b16), ("P2", 128, b16), ("ONE", 144, b16),
+    ("PI", 8, i32), ("CL", 26, f32), ("PF", 128, b16), ("TI", 16, i32), ("TF", 16, f32), ("TG", 16, f32), ("TH", 16, f32),
+    ("LMK", 16, u16), ("LM0", 8, u16), ("LKM", 16, u16), ("LK", 4, u16), ("LB", 16, u16), ("LD", 4, u16), ("REV", 8, u16), ("LI", 16, f32),
+    ("TRI", 512, b16), ("RMAX", 256, b16), ("RMIN", 256, b16), ("RL", 256, b16), ("EQ", 512, b16), ("KA", 256, f32),
+    ("ADH", 64, f16), ("EQS", 512, b16), ("RZ2", 512, b16), ("I128", 128, b16), ("NT", 128, b16),
     ("THR", 48, f32), ("NF", 288, f32), ("QN", 288, f32), ("Y", 544, f32), ("KS", 768, f32), ("SO", 768, u16), ("QO", 256, u16),
     ("SMN", 256, f32), ("SMX", 256, f32), ("SM2", 256, f32), ("NM", 256, b16), ("E", 256, f32), ("E2", 256, f32), ("K3", 256, f32),
     ("S1", 16, i32), ("S2", 16, i32), ("S3", 16, i32), ("AI", 16, i32), ("A16", 16, u16), ("KM", 16, f32), ("LV", 16, f32), ("U", 16, f32), ("U2", 16, f32),
     ("GD", 16, f32), ("YG", 16, f32), ("GW", 16, f32), ("AF", 16, f32), ("GID", 64, f32), ("GK", 64, f32),
-    ("AD", 16, f32), ("AD16", 16, u16), ("OX", 32, u16), ("O1", 16, u16), ("X1", 512, f32), ("X2", 512, f32), ("SI", 256, i32), ("SI2", 256, i32),
-    ("XG", 256, b16), ("LAND", 1024, b16), ("NVA", 1024, b16), ("VAF", 1024, f32), ("VA", 256, b16),
+    ("AD", 16, f32), ("AD16", 16, u16), ("O1", 16, u16), ("SI", 256, i32), ("SI2", 256, i32),
+    ("XG", 256, b16), ("LAND", 1024, b16), ("NVA", 2048, b16), ("VAF", 2048, f32), ("VA", 256, b16),
     ("D1M", 256, f32), ("N1", 256, b16), ("N2", 256, b16), ("N3", 256, b16), ("NA", 256, b16), ("CN", 16, b16), ("H1", 256, b16), ("LO", 256, b16), ("HI", 256, b16),
     ("YV", 1280, b16), ("AXN", 512, f32), ("YS", 384, f32), ("YB", 768, f32),
 ]:
     SCRATCH[_n] = ("sbuf", [128, _w], _d)
-ALIAS = {"XM": "A1", "XA": "A2", "XS": "D2", "ZX2": "ZX0", "KD": "GC"}
+ALIAS = {"XM": "A1", "XA": "A2", "XS": "D2", "KD": "GC"}
 PART = {}
-for _grp in (("KLO", "KHI", "ILO", "IHI"), ("IC", "IC2"), ("U", "U2", "LV", "GD", "YG", "GW", "AF", "GID", "GK"), ("N1", "N2", "N3", "H1", "LO", "HI", "NM"),
-             ("S1", "S3", "AI"), ("WM", "WN", "WP", "WA", "WA0", "W2", "WB"), ("TF", "TG", "TH", "LI"), ("LMK", "LM0", "LKM", "LK", "LB", "LB2", "LX", "REV"),
+for _grp in (("KLO", "KHI", "ILO", "IHI"), ("U", "U2", "LV", "GD", "YG", "GW", "AF", "GID", "GK"), ("N1", "N2", "N3", "H1", "LO", "HI", "NM"),
+             ("S1", "S3", "AI"), ("WM", "WN", "WP", "WA", "WA0", "W2", "WB"), ("TF", "TG", "TH", "LI"), ("LMK", "LM0", "LKM", "LK", "LB", "LD", "REV"),
              ("NI", "CI"), ("RMAX", "RMIN", "RL")):
     _o = 0
     for _n in _grp:
@@ -108,8 +116,8 @@ def qslot(T, t):
     return T["QT"][:, GB + L * t:GB + L * t + L]
 
 
-def nslot(T, t, h):
-    return T["LAND"][:, L * t + 128 * h:L * t + 128 * h + 128]
+def nslot(T, t, j):
+    return T["LAND"][:, L * t + SENDS[j][0]:L * t + SENDS[j][1]]
 
 
 def relay_program(g, core, T, topo):
@@ -119,7 +127,7 @@ def relay_program(g, core, T, topo):
             continue
         n_in = len(topo.engines(s, core))
         rid, pid = topo.addr(d, core)
-        for sem, ap in (("aq%d" % t, qslot(T, t)), ("an%d" % (2 * t + 1), nslot(T, t, 1)), ("an%d" % (2 * t), nslot(T, t, 0))):
+        for sem, ap in (("aq%d" % t, qslot(T, t)), ("an%d" % (2 * t), nslot(T, t, 0)), ("an%d" % (2 * t + 1), nslot(T, t, 1))):
             g.wait_ge(T.sem[sem], n_in)
             g.remote_dma(ap, ap, T.sem[sem], T.sem["fwd"], pid, rid, topo.mask(core, d))
             sent += len(topo.engines(core, d))
@@ -134,21 +142,27 @@ def place(ops, order, edges, first, fixed=None, near=()):
     for i in sorted(near, key=lambda i: fixed[i]):
         if ops[i]["q"]:
             line.setdefault(ops[i]["q"], []).append((fixed[i], fixed[i] + ops[i]["cost"], i))
+    end = [s + o["cost"] for s, o in zip(start, ops)]
     for i in order:
         o = ops[i]
-        t = max([start[j] + ops[j]["cost"] + d for j, d in edges[i]] + [first[i], floor])
+        t = first[i] if first[i] > floor else floor
+        for j, d in edges[i]:
+            if end[j] + d > t:
+                t = end[j] + d
+        c = o["cost"]
         if o["q"]:
             ln = line.setdefault(o["q"], [])
-            k = len(ln)
+            k = m = len(ln)
             while k > 0 and ln[k - 1][0] >= t:
                 k -= 1
-            if k > 0:
-                t = max(t, ln[k - 1][1])
-            while k < len(ln) and t + o["cost"] > ln[k][0] + 1e-9:
+            if k > 0 and ln[k - 1][1] > t:
+                t = ln[k - 1][1]
+            while k < m and t + c > ln[k][0] + 1e-9:
                 t = max(t, ln[k][1])
                 k += 1
-            ln.insert(k, (t, t + o["cost"], i))
+            ln.insert(k, (t, t + c, i))
         start[i] = t
+        end[i] = t + c
     return start, {q: [e[2] for e in ln] for q, ln in line.items()}
 
 
@@ -222,8 +236,9 @@ def plan_calls(ops):
     rng = np.random.default_rng(SEED)
     start = best_start
     done = lambda st, i: st[i] + ops[i]["cost"] + lats[i]
-    marks = [i for i in range(n) if ops[i]["key"] == "mark"] + [None]
-    for w in list(range(len(marks))) * SWEEPS:
+    tags = {ops[i]["tag"]: i for i in range(n)}
+    for sweep, w in [(s, w) for s in range(SWEEPS) for w in ONLY or range(6)]:
+        marks = [i for i in range(n) if ops[i]["key"] == "mark%d" % (sweep % 2)] + [None]
         lo = start[marks[w - 1]] if w else -1.0
         hi = start[marks[w]] + 3.0 if marks[w] is not None else 1e9
         free = [i for i in range(n) if lo < start[i] <= hi]
@@ -254,7 +269,18 @@ def plan_calls(ops):
             return out, before
 
         cur, cur_seq = place(ops, sorted(free, key=lambda i: (start[i], i)), fwd, zero, start, near)
-        best = now = score(cur)
+        now = score(cur)
+        for w2 in range(1, 5) if w else ():
+            key = {}
+            for i in free:
+                rd, tag = ops[i]["tag"]
+                j = tags.get((rd - w + w2, tag))
+                key[i] = start[i] - lo if j is None else start[j] - start[marks[w2 - 1]]
+                key[i] = max([key[i]] + [key[a] + 1e-5 for a, d in fwd[i] if a in inside])
+            st, sq = place(ops, sorted(free, key=key.get), fwd, zero, start, near)
+            if score(st) < now:
+                cur, cur_seq, now = st, sq, score(st)
+        best = now
         keep = cur
         pairs, before = held_up(cur, cur_seq)
         for _ in range(MOVES):
@@ -283,16 +309,18 @@ def plan_calls(ops):
                         todo.append(b)
             st, sq = place(ops, sorted(free, key=key.get), fwd, zero, start, near)
             s = score(st)
-            if s <= now + HEAT * (1 - _ / MOVES) * rng.random():
+            if s <= now - HEAT * 0.03 ** (_ / MOVES) * np.log(1.0 - rng.random()):
                 now, cur = s, st
                 pairs, before = held_up(st, sq)
                 if s < best:
                     best, keep = s, st
-        shift = keep[marks[w]] - start[marks[w]] if marks[w] is not None else 0.0
         order = sorted(range(n), key=lambda i: (0, keep[i], i) if start[i] <= hi else (1, start[i], i))
-        start, seq = place(ops, order, fwd, zero)
+        st, sq = place(ops, order, fwd, zero)
+        if sweep == 0 or max(done(st, i) for i in range(n)) <= max(done(start, i) for i in range(n)):
+            start, seq = st, sq
     best_end = max(start[i] + ops[i]["cost"] + lats[i] for i in range(n))
     ORDER["end"] = best_end
+    ORDER["dbg"] = (ops, start, fwd, seq, marks)
     pos = {}
     for q in seq:
         for k, i in enumerate(seq[q]):
@@ -319,6 +347,7 @@ def rank_program(g, core, T, topo):
         relay_program(g, core, T, topo)
         return
     ops = []
+    part = [-9, "", 0]
     chain = {"on": ()}
     Q = {"V": g.vector, "S": g.scalar, "T": g.tensor, "G": g, "Y": g.sync}
     ALL = slice(None)
@@ -336,7 +365,7 @@ def rank_program(g, core, T, topo):
             idx = tuple(slice(0, n) for n in shape[1:])
         ap = T[name][(p,) + idx]
         cm = bits(shape[1:], idx)
-        return {"ap": ap, "reg": [(name, cm, bits([128], p))], "n": cm.bit_count(), "w": 2 if d in (b16, u16) else 4, "ps": where == "psum"}
+        return {"ap": ap, "reg": [(name, cm, bits([128], p))], "n": cm.bit_count(), "w": 2 if d in (b16, f16, u16) else 4, "ps": where == "psum"}
 
     def C(name, a, b, s=None, p=ALL):
         return R(name, slice(a, b, s), p=p)
@@ -356,10 +385,10 @@ def rank_program(g, core, T, topo):
         lat = 0.0
         sct = None
         if ext:
-            cost, lat = 0.001, LREM[key]
+            cost, lat = 0.001, LREM[key] + (LQ if ext[0].startswith("aq") else 0.0)
         elif dma:
-            by = 128 * max([x["n"] * x["w"] for x in outs + ins])
-            cost, lat = (1.0 if q == "G" else 0.2), 2.5 + by / (2e5 if dma > 0 else 4e4)
+            by = 128 * max([x["n"] * x["w"] for x in outs + ins]) * (2 if two else 1)
+            cost, lat = (1.0 if q == "G" else 0.15), 2.2 + by / (2e5 if dma > 0 else 4e4)
         elif q == "T":
             cost = max(64, ins[1]["n"]) * CPE * (1 if ins[1]["w"] == 2 else 4)
         elif q == "G":
@@ -377,9 +406,13 @@ def rank_program(g, core, T, topo):
                 f *= 2
             cost = max(0.066, n * f * CYC)
         ops.append({"q": q, "fn": fn, "rd": rd, "wr": wr, "dma": dma, "ext": ext, "inc": False, "cost": cost, "lat": lat, "key": key, "sct": sct,
-                    "sent": sent, "after": chain.get(q) if q in chain["on"] and not (dma or sct) else None})
+                    "tag": (part[0], (part[1], len(ops) - part[2])), "sent": sent, "after": chain.get(q) if q in chain["on"] and not (dma or sct) else None})
         if q in chain["on"] and not (dma or sct):
             chain[q] = len(ops) - 1
+
+    def begin(t, name):
+        part[:] = [t, name, len(ops)]
+        cut()
 
     def a_(x):
         return x["ap"] if isinstance(x, dict) else x
@@ -447,7 +480,7 @@ def rank_program(g, core, T, topo):
 
     def dma(q, o, a, add=False, key=None):
         if add:
-            op(q, lambda e: e.dma_start(o["ap"], a["ap"], accum_op=A.add), [o], [a, o], dma=16, key=key)
+            op(q, lambda e: e.dma_start(o["ap"], a["ap"], accum_op=A.add), [o], [a, o], dma=16, key=key, two=True)
         else:
             op(q, lambda e: e.dma_start(o["ap"], a["ap"]), [o], [a], dma=16, key=key)
 
@@ -479,22 +512,18 @@ def rank_program(g, core, T, topo):
     dma("S", R("SN"), R("sn"))
     dma("Y", R("KC"), R("kid"))
     dma("Y", R("VN"), R("vn"))
+    dma("Y", R("KD"), R("vn"))
     dma("Y", R("BC"), R("bst"))
+    dma("Y", R("BR"), R("zs"))
     dma("Y", R("NQ"), R("nq"))
 
     iota(PIc(0), [[1, 1]], 0, 1, True)
     iota(R("TF"), [[0, 8], [1, 2]], 0, 0)
     iota(R("TG"), [[16, 16]], 0, 0)
-    iota(R("TH"), [[128, 2], [2, 8]], 0, 0)
     iota(R("TI"), [[1, 16]], 0, 0, True)
     ms(R("B0"), 0.0)
     ms(R("ID"), 1.0)
-    ms(R("M1"), 0.0)
-    ms(R("M2"), 0.0)
     ms(C("B0", 15, 144, 16), 1.0)
-    for j in range(4):
-        ms(C("M1", j, 128, 16), 1.0)
-        ms(C("M2", 4 + j, 128, 16), 1.0)
     ts(PIc(1), PIc(0), 15, A.bitwise_and)
     ts(PIc(2), PIc(0), 4, A.arith_shift_right, 1, A.bitwise_and)
     ts(PIc(3), PIc(0), 1, A.bitwise_and)
@@ -505,13 +534,14 @@ def rank_program(g, core, T, topo):
     ms(C("NF", 0, 16), 0.0)
     ms(C("NF", 272, 288), 0.0)
     ms(R("KF"), 0.0)
-    ms(R("KD"), 0.0)
     cp(C("CL", 0, 7), C("PI", 1, 8))
     asel(R("B0"), [[-1, 144]], A.is_ge, 15, 1)
     asel(R("B0"), [[1, 144]], A.is_ge, 0, -1)
-    for nm, j0 in (("M1", 0), ("M2", 4)):
-        asel(R(nm), [[-16, 8], [-4, 16]], A.is_ge, 4 * j0, 1)
-        asel(R(nm), [[16, 8], [4, 16]], A.is_ge, 3 - 4 * j0, -1)
+    ts(C("TH", 8, 12), C("TG", 0, 4), 1.0 / 16.0, A.mult, CLc(3), A.is_equal)
+    act(R("MX"), C("B0", 0, 132), AF.Copy, scale=0.0)
+    for j in range(4):
+        act(C("MX", 4 + j, 132, 16), C("B0", 15, 128, 16), AF.Copy, scale=C("TH", 8 + j, 9 + j))
+    M1, M2 = C("MX", 4, 132), C("MX", 0, 128)
     asel(R("ID"), [[-1, 128]], A.is_equal, 0, 1)
     ms(R("ONE"), 1.0)
     ts(R("TF"), R("TF"), CLc(1), A.not_equal, 272.0, A.mult)
@@ -523,63 +553,79 @@ def rank_program(g, core, T, topo):
     ts(CLc(9), CLc(5), 16.0, A.mult, CLc(6), A.add)
     ts(R("LMK"), R("TF"), CLc(0), A.subtract, 15.0, A.add)
     ts(R("LK"), C("TG", 0, 4), 0.25, A.mult, CLc(8), A.add)
-    ts(R("LKM"), R("TH"), CLc(9), A.add, CLc(7), A.add)
-    ts(CLc(20), CLc(3), 2.0, A.mult, CLc(2), A.add)
+    ts(CLc(9), CLc(9), CLc(7), A.add)
+    for u, (m0, nm) in enumerate(UNITS):
+        ts(C("TH", u, u + 1), CLc(9 if nm == 8 else 8), 16.0 * m0, A.add)
+        ts(C("LKM", m0, m0 + nm), C("TG", 0, nm), 1.0 / nm, A.mult, C("TH", u, u + 1), A.add)
     cp(R("LB"), R("TI"))
-    ts(R("LX"), C("TG", 0, 2), 0.5, A.mult, CLc(20), A.add)
-    gfill(R("FW"), -128)
     ts(CLc(10), CLc(0), 8.0, A.is_equal)
     ts(CLc(11), CLc(0), 9.0, A.is_equal)
     ts(CLc(12), CLc(0), 11.0, A.is_equal)
     ts(CLc(13), CLc(0), 4.0, A.is_lt, -8192.0, A.mult)
     ts(CLc(14), CLc(0), 8.0, A.is_lt, -8192.0, A.mult)
     ts(CLc(15), CLc(0), 0.0, A.is_equal, 2.0 ** -17, A.mult)
-    ts(CLc(16), CLc(11), 64.0, A.mult, CLc(10), A.add)
+    ts(CLc(16), CLc(11), 16.0, A.mult, CLc(10), A.add)
     ts(CLc(17), CLc(10), CLc(11), A.add, CLc(12), A.add)
     ts(CLc(18), CLc(12), 4096.0 - CEN, A.mult, CLc(16), A.add)
     ts(CLc(21), CLc(14), CLc(13), A.subtract)
     ts(CLc(19), CLc(18), CLc(13), A.add)
-    for nm, src, f in (("WM", "B0", 16384.0), ("WN", "B0", -8192.0), ("WP", "B0", 8192.0), ("CI", "ID", KOFF), ("NI", "ID", -1.0),
+    for nm, src, f in (("WM", "B0", 16384.0), ("WN", "B0", -8192.0), ("WP", "B0", 8192.0), ("CI", "ID", KOFF), ("NI", "ID", -1.0), ("NJ", "ID", -1.0 / 128.0),
                        ("WA", "B0", CLc(19)), ("WA0", "B0", CLc(21)), ("W2", "B0", 2.0), ("WB", "B0", -1.0), ("P2", "ID", CLc(17))):
-        ts(R(nm), R(src), f, A.mult)
-    ts(C("P2", 12, 128, 16), C("B0", 15, 128, 16), CLc(16), A.mult)
-    cp(R("BF"), R("B0"))
+        act(R(nm), R(src), AF.Copy, scale=f)
+    act(C("P2", 12, 128, 16), C("B0", 15, 128, 16), AF.Copy, scale=CLc(16))
+    act(R("BF"), R("B0"), AF.Copy, scale=CLc(16))
 
     def stile(tau):
         cp(C("NF", 16, 272), C("SN", tau, 768, 3))
         tr(C("Y", 0, 256), C("NF", 16, 272))
         tr(C("Y", 256, 544), R("NF"))
-        ts(C("KS", L * tau, L * tau + L), IND(R("Y"), R("LMK")), -CEN, A.add)
-        ts(C("SO", L * tau, L * tau + L), C("KS", L * tau, L * tau + L), CEN, A.add)
+        if tau:
+            act(C("KS", L * tau, L * tau + L), IND(R("Y"), R("LMK")), AF.Identity, bias=-CEN)
+            ts(C("SO", L * tau, L * tau + L), C("KS", L * tau, L * tau + L), CEN, A.add)
+        else:
+            cp(C("SO", 0, L), IND(R("Y"), R("LMK")))
+            act(C("KS", 0, L), IND(R("Y"), R("LMK")), AF.Identity, bias=-CEN)
 
-    def zexp(tau, m0=0, m1=16):
-        zg = "ZG2" if tau else "ZG"
+    def zexp(tau, m0=0, m1=16, q="G"):
+        zg = "ZG2" if tau == 1 else "ZG"
 
         def f(o, a, n):
-            if tau:
+            if q == "G":
                 asel(o, [[0, n]], A.is_ge, 0, 0, a)
+            elif q == "V":
+                cp(o, a)
             else:
                 act(o, a, AF.Copy)
         ms_ = slice(m0, m1)
         f(R(zg, ms_, slice(0, 16)), C("ZS", tau + 48 * m0, 48 * m1, 3), 16 * (m1 - m0))
         for w in (16, 32, 64, 128):
             f(R(zg, ms_, slice(w, 2 * w)), R(zg, ms_, slice(0, w)), w * (m1 - m0))
-        dma("Y", C("ZX%d" % tau, L * m0, L * m1), R(zg, ms_, ALL))
+        for a in range(m0, m1, 4):
+            dma("Y", C("ZX1" if tau == 1 else "ZX0", L * a, L * a + 4 * L), R(zg, slice(a, a + 4), ALL), key=("zx", tau % 2, a))
+
+    def maxz(out, o, win, so, tau, c, first=False):
+        if first:
+            for m in range(3, -1, -1):
+                tt(C(out, o + L * m, o + L * m + L), IND(win, C("SO", so + 16 * m, so + 16 * m + 16)), R("ZG", 4 * c + m, ALL), A.max)
+        else:
+            tt(C(out, o, o + 1024), IND(win, C("SO", so, so + 64)), CH("ZX1" if tau == 1 else "ZX0", c), A.max)
+
+    def ZX(tau, c, a=0, e=1024, r=None):
+        return R("ZG2" if tau == 1 else "ZG", slice(4 * c + a // L, 4 * c + e // L), ALL if r is None else slice(r, L, 16))
 
     for tau in range(3):
         act(C("ZT", L * tau, L * tau + L), C("ZS", tau, 768, 3), AF.Copy)
-    for m0, m1 in ((12, 16), (6, 12), (0, 6)):
-        zexp(0, m0, m1)
+    for m0, m1, q in OPT["ZG"]:
+        zexp(0, m0, m1, q)
     zexp(1)
     cp(C("KF", 16, 80), R("KC"))
     tr(C("Y", 0, 64), C("KF", 16, 80))
     tr(C("Y", 256, 352), R("KF"))
     ms(C("Y", 64, 256), 0.0)
     cp(R("KO"), IND(C("Y", 0, 352), R("LK")))
-    ts(R("KI"), R("KC"), 63, A.bitwise_and)
-    cp(R("KLO"), R("KI"))
-    ts(R("KI"), R("KC"), 6, A.arith_shift_right)
-    cp(R("KHI"), R("KI"))
+    ts(C("KI", 0, 64), R("KC"), 15, A.bitwise_and)
+    ts(C("KI", 64, 128), R("KC"), 4, A.arith_shift_right)
+    cp(C("XKLO", 0, 128), R("KI"))
     dma("Y", R("KD", p=rows(8)), R("KLO"))
     dma("Y", R("KD", p=rows(9)), R("KHI"))
     dma("Y", R("KD", p=rows(11)), C("ONE", 0, 64))
@@ -587,15 +633,16 @@ def rank_program(g, core, T, topo):
     act(R("VCB"), IND(R("VN"), R("KO")), AF.Copy)
     for hf in range(2):
         cols = lambda nm, o=0: C(nm, o + 512 * hf, o + 512 * hf + 512)
-        mm(PS(4 + hf), R("M2"), cols("VN"), True, False)
+        mm(PS(4 + hf), M2, cols("VN"), True, False)
         mm(PS(4 + hf), R("P2"), cols("KD"), False, False)
-        mm(PS(4 + hf), R("M1"), cols("VCB"), False, True)
+        mm(PS(4 + hf), M1, cols("VCB"), False, True)
         act(cols("AUX", PAD), PS(4 + hf), AF.Copy)
     act(R("ZB"), R("ZS"), AF.Identity, bias=64.0)
     iota(R("KA"), [[0, 16], [-1, 16]], 15, 0)
     for a, b in ((PAD, PAD + T0), (PAD + T0, PAD + GB), (PAD + GB, WT)):
         iota(C("IO", a, b), [[1, b - a]], a, 0)
-    act(C("VP", PAD, PAD + T0), C("IO", PAD, PAD + T0), AF.Identity, bias=64.0, scale=CLc(15))
+    ts(CLc(25), CLc(15), -float(PAD), A.mult, 64.0, A.add)
+    act(C("VP", PAD, PAD + T0), C("IO", PAD, PAD + T0), AF.Identity, bias=CLc(25), scale=CLc(15))
     dma("G", C("VP", PAD, PAD + T0), R("vn"), add=True)
     dma("G", C("VC", PAD, PAD + T0), R("VCB"))
 
@@ -607,16 +654,51 @@ def rank_program(g, core, T, topo):
         kn = C("KS", L * tau + 64 * c, L * tau + 64 * c + 64)
         tt(kn, o, kn, A.add)
 
+    turn = [4, 5, 6, 0, 1]
+    held = set()
+
+    def next_bank(banks=(4, 5, 6)):
+        b = [x for x in turn if x in banks and x not in held][0]
+        turn.remove(b)
+        turn.append(b)
+        return b
+
+    def own_dist(tau, c):
+        src, s0, ab, a0 = ("XS", 1024 * c, "D1", 1024 * c) if tau == 0 else ("GA" if c % 2 == 0 else "VCB", 0, "GC", 0)
+        so = L * tau + 64 * c
+        if c not in OPT["OWNS"][tau]:
+            maxz(src, s0, R("VN"), so, tau, c, tau == 0 and c in OPT["FIRST"][0])
+            own_sum(tau, c, lambda r: C(src, s0 + r, s0 + 1024, 16))
+            return
+        for a in range(0, 1024, PG):
+            act(C(src, s0 + a, s0 + a + PG), IND(R("VN"), C("SO", so + a // 16, so + (a + PG) // 16)), AF.Copy)
+        for a in range(0, 1024, PA):
+            b = next_bank()
+            mm(PS(b, 0, PA), R("ID"), C(src, s0 + a, s0 + a + PA), True, False)
+            mm(PS(b, 0, PA), R("NI"), ZX(tau, c, a, a + PA), False, True)
+            act(C(ab, a0 + a, a0 + a + PA), PS(b, 0, PA), AF.Abs)
+        o = PS(DBANK[c % 2], 384, 448)
+        for r in range(16):
+            mm(o, Wr("WP", r), ZX(tau, c, r=r), r == 0, False)
+        mm(o, R("CI"), C("ONE", 0, 64), False, False)
+        cut()
+        for r in range(16):
+            mm(o, Wr("WP", r), C(ab, a0 + r, a0 + 1024, 16), False, r == 15)
+        kn = C("KS", so, so + 64)
+        tt(kn, o, kn, A.add)
+
     for c in range(3, -1, -1):
-        for m in range(4 * c + 3, 4 * c - 1, -1):
-            tt(C("XS", L * m, L * m + L), IND(R("VN"), C("SO", 16 * m, 16 * m + 16)), R("ZG", m, ALL), A.max)
-        own_sum(0, c, lambda r: CH("XS", c, r, 16))
-    ts(R("BCF"), R("BC"), float(PAD), A.add)
-    gfill(R("BR"), 0)
-    dma("Y", R("BR", p=rows(12)), R("BCF"))
-    for nm, v0, v in (("RMAX", -BIG, -1.0), ("RMIN", BIG, 1.0), ("RL", -BIG, 0.0)):
-        ms(R(nm), v)
-        ms(C(nm, 0, 256, 16), v0)
+        own_dist(0, c)
+    ts(R("BC"), R("BC"), float(PAD), A.add)
+    ts(C("BCI", 0, 48), R("BC"), 15, A.bitwise_and)
+    ts(C("BCI", 48, 96), R("BC"), 4, A.arith_shift_right)
+    cp(R("BCF"), R("BCI"))
+    dma("Y", R("BR", p=rows(8)), C("BCF", 0, 48))
+    dma("Y", R("BR", p=rows(9)), C("BCF", 48, 96))
+    ms(R("RMIN"), 1.0)
+    ms(C("RMIN", 0, 256, 16), BIG)
+    act(R("RMAX"), R("RMIN"), AF.Copy, scale=-1.0)
+    act(R("RL"), R("RMIN"), AF.Identity, bias=1.0, scale=-1.0)
     gfill(C("VP", 0, PAD), 1024)
     ms(C("QN", 0, 16), 0.0)
     ms(C("QN", 272, 288), 0.0)
@@ -625,20 +707,21 @@ def rank_program(g, core, T, topo):
     stile(1)
     ts(R("LM0"), C("TF", 0, 8), CLc(0), A.add)
     ts(R("REV"), C("TG", 0, 8), CLc(0), A.subtract, 15.0, A.add)
-    for t in range(4):
-        ts(C("GID", 16 * t, 16 * t + 16), R("LI"), float(GB + L * t), A.add)
-    ts(R("GK"), R("GID"), KOFF + 4096.0 - CEN, A.add)
+    iota(R("GID"), [[L, 4], [16, 16]], GB, 0)
+    act(R("GID"), R("GID"), AF.Identity, bias=CLc(0))
+    act(R("GK"), R("GID"), AF.Identity, bias=4096.0 - CEN)
+    act(R("GID"), R("GID"), AF.Identity, bias=4096.0 - CEN - TOP)
     iota(R("TRI"), [[0, 8], [-16, 2], [1, 32]], 0, 0)
-    iota(C("X1", 0, 32), [[1, 16], [0, 2]], 0, 0)
-    asel(R("FW"), [[-1, 16], [-16, 8], [0, 16]], A.is_equal, 0, 1)
-    iota(R("IC"), [[1, 144]], T0, 0, True)
-    ts(CLc(22), CLc(0), 144.0, A.mult)
-    ts(R("IC"), R("IC"), CLc(22), A.add)
-    ts(R("IC2"), R("IC"), 63, A.bitwise_and)
-    cp(R("ILO"), R("IC2"))
-    ts(R("IC2"), R("IC"), 6, A.arith_shift_right)
-    cp(R("IHI"), R("IC2"))
-    dma("Y", R("IDB"), C("ZX0", 0, 2304))
+    act(R("I128"), R("ID"), AF.Copy, scale=128.0)
+    for a in range(0, 16, 4):
+        b = next_bank()
+        for r in range(a, a + 4):
+            mm(PS(b, 128 * (r - a), 128 * (r - a) + 128), Wr("WB", r), R("I128"), r == a, r == a + 3)
+        act(C("FW", 128 * a, 128 * a + 512), PS(b), AF.Copy)
+    iota(R("ILO"), [[1, 144]], 0, 0)
+    ts(CLc(22), CLc(0), 9.0, A.mult, T0 / 16.0, A.add)
+    act(R("IHI"), R("ONE"), AF.Copy, scale=CLc(22))
+    dma("Y", R("IDB"), R("ZG", slice(7, 16), ALL))
     dma("Y", R("IDB", p=rows(8)), R("ILO"))
     dma("Y", C("QT", T0, GB), C("IO", T0, GB))
     dma("Y", C("VC", PAD + T0, WT), C("IO", PAD + T0, WT))
@@ -653,125 +736,117 @@ def rank_program(g, core, T, topo):
     dma("Y", R("IDB", p=rows(11)), R("ONE"))
     dma("G", C("AUX", PAD + T0, WT), R("IDB"))
     dma("Y", C("AUX", PAD + T0, WT, p=rows(12)), C("IO", T0, W, p=rows(12)))
-    cp(R("LB2"), C("X1", 0, 32))
-    ts(CLc(23), CLc(0), -8192.0, A.mult, 4096.0, A.add)
-    act(R("TRI"), R("TRI"), AF.Relu, bias=CLc(23), scale=8192.0)
+    ts(CLc(23), CLc(0), -2.0 ** 21, A.mult, 2.0 ** 20, A.add)
+    act(R("TRI"), R("TRI"), AF.Relu, bias=CLc(23), scale=2.0 ** 21)
+    ts(CLc(20), CLc(3), 2.0, A.mult, CLc(2), A.add)
+    ts(C("LD", 0, 2), C("TG", 0, 2), 0.5, A.mult, CLc(20), A.add)
+    ts(CLc(20), CLc(0), CLc(2), A.subtract, 0.5, A.mult)
+    ts(C("LD", 2, 4), C("TG", 0, 2), 0.5, A.mult, CLc(20), A.add)
     gfill(R("RZ2"), 1)
-    gfill(C("IO", 0, PAD), PAD - 1)
     ms(C("RZ2", 0, 512, 32), 0.0)
-    for a in range(PAD + T0, WT, L):
-        act(C("VP", a, a + L), C("IO", a, a + L), AF.Identity, bias=64.0, scale=CLc(15))
+    gfill(C("IO", 0, PAD), PAD - 1)
+    dma("Y", C("VP", PAD + T0, PAD + GB), C("IO", PAD + T0, PAD + GB))
+    act(R("PF"), C("FW", 128 * 11, 128 * 12), AF.Copy, scale=-0.5)
+    ts(CLc(24), CLc(12), 64.0, A.mult)
+    ts(CLc(24), CLc(16), 2.0 ** -17, A.mult, CLc(24), A.add)
+    act(C("PF", 0, 128, 16), C("B0", 15, 128, 16), AF.Copy, scale=CLc(24))
 
-    turn = [4, 5, 6, 0, 1]
-    held = set()
-
-    def next_bank(banks=(4, 5, 6)):
-        b = [x for x in turn if x in banks and x not in held][0]
-        turn.remove(b)
-        turn.append(b)
-        return b
-
-    def own_dist(tau, c0):
-        zx = "ZX%d" % tau
-        for c in (c0,):
-            src = "GA" if c % 2 == 0 else "VCB"
-            so = L * tau + 64 * c
-            if c not in OPT["OWNS"][tau]:
-                for a in range(0, 1024, 512):
-                    tt(C(src, a, a + 512), IND(R("VN"), C("SO", so + a // 16, so + a // 16 + 32)), C(zx, 1024 * c + a, 1024 * c + a + 512), A.max)
-                own_sum(tau, c, lambda r: C(src, r, 1024, 16))
-                continue
-            for a in range(0, 1024, PG):
-                act(C(src, a, a + PG), IND(R("VN"), C("SO", so + a // 16, so + (a + PG) // 16)), AF.Copy)
-            for a in range(0, 1024, PA):
-                b = next_bank()
-                mm(PS(b, 0, PA), R("ID"), C(src, a, a + PA), True, False)
-                mm(PS(b, 0, PA), R("NI"), C(zx, 1024 * c + a, 1024 * c + a + PA), False, True)
-                act(C("GC", a, a + PA), PS(b, 0, PA), AF.Abs)
-            o = PS(DBANK[c % 2], 384, 448)
-            for r in range(16):
-                mm(o, Wr("WP", r), CH(zx, c, r, 16), r == 0, False)
-            mm(o, R("CI"), C("ONE", 0, 64), False, False)
-            cut()
-            for r in range(16):
-                mm(o, Wr("WP", r), C("GC", r, 1024, 16), False, r == 15)
-            kn = C("KS", so, so + 64)
-            tt(kn, o, kn, A.add)
-
+    later = []
     for t in range(5):
         tau = TILE[t]
-        zx = "ZX%d" % tau
         wend = PAD + (T0 if t < 3 else GB + L * (t - 2))
         aend = PAD + (T0 if t == 0 else GB + L * t)
         own = PAD + T0 + L * t
         ld = L * (t - 1)
         gcol = PAD + GB + ld
-        H = lambda nm, h, o=0: C(nm, o + 128 * h, o + 128 * h + 128)
-        M = lambda nm, h, o=0: C(nm, o + 8 * h, o + 8 * h + 8)
+        H = lambda nm, u, o=0: C(nm, o + 16 * UNITS[u][0], o + 16 * sum(UNITS[u]))
+        M = lambda nm, u: C(nm, UNITS[u][0], sum(UNITS[u]))
         last = lambda nm: C(nm, 15, 256, 16)
         for c in range(3, -1, -1):
             so = C("SO", L * tau + 64 * c, L * tau + 64 * c + 64)
+            begin(t, "child%d" % c)
             act(CH("XA", c), IND(C("AUX", PAD, wend), so), AF.Copy)
-            tt(CH("XM", c), IND(R("VCB") if t == 0 else C("VC", PAD, wend), so), CH(zx, c), A.max)
+            maxz("XM", 1024 * c, R("VCB") if t == 0 else C("VC", PAD, wend), L * tau + 64 * c, tau, c, t == 0 and c in OPT["FIRST"][1])
+            if c == 0 and later:
+                begin(t, "lists%d" % (t in (2, 3)))
+                later.pop()(after=len(ops) - 1)
             if t < 3 and c not in OPT["OWNS"].get(t, ()):
+                begin(t, "own%d" % c)
                 o = PS(DBANK[c % 2], 0, 64)
                 for r in range(16):
                     mm(o, Wr("WA0", r), CH("XA", c, r, 16), r == 0, r == 15)
                 kn = C("KS", L * tau + 64 * c, L * tau + 64 * c + 64)
                 tt(kn, o, kn, A.add)
+            begin(t, "keys%d" % c)
             o = PS(0, 64 * c, 64 * c + 64)
             for r in range(16):
-                mm(o, Wr("WA", r), CH("XA", c, r, 16), r == 0, False)
+                mm(o, Wr("WM", r), CH("XM", c, r, 16), r == 0, False)
             cut()
             for r in range(16):
-                mm(o, Wr("WM", r), CH("XM", c, r, 16), False, False)
+                mm(o, Wr("WA", r), CH("XA", c, r, 16), False, False)
             mm(o, R("CI"), C("ONE", 0, 64), False, True)
+        begin(t, "guests")
         if t >= 1:
-            for h in (1, 0):
-                if h in OPT["GV"]:
-                    tt(H("VP", h, gcol), H("LAND", h, ld), H("VP", h, gcol), A.add)
-                else:
-                    dma("G", H("VP", h, gcol), H("LAND", h, ld), add=True)
+            for src, col0 in (("YV", own - L), ("LAND", gcol)):
+                b = next_bank()
+                mm(PS(b, 0, L), R("PF"), C("IDB", col0 - PAD - T0, col0 - PAD - T0 + L), True, False)
+                cut()
+                mm(PS(b, 0, L), R("ID"), C(src, ld, ld + L), False, True)
+                act(C("VP", col0, col0 + L), PS(b, 0, L), AF.Copy)
             tt(R("XG"), C("LAND", ld, ld + L), C("ZT", L * tau, L * tau + L), A.max)
             o = R("PS3", 16, ALL)
             for r in range(16):
                 mm(o, Wr("WN", r), C("LAND", ld + r, ld + L, 16), r == 0, False)
             cut()
             for r in range(16):
-                mm(o, Wr("WM", r), C("XG", r, L, 16), False, r == 15)
+                mm(o, Wr("WM", r), C("XG", r, L, 16), False, False)
+            mm(o, R("CI"), C("ONE", 0, 16), False, True)
             tt(R("KM"), o, C("GK", 16 * t - 16, 16 * t), A.add)
-            ts(R("GD"), R("KM"), MAGIC, A.add, MAGIC, A.subtract)
+        begin(t, "parent")
         k2, dp = PS(0, L, 2 * L), PS(1, 0, L)
         tt(k2, PS(0, 0, L), C("KS", L * tau, L * tau + L), A.min)
+        ops[-1]["key"] = "mark1"
         ts(dp, k2, MAGIC, A.add, MAGIC, A.subtract)
         scan(R("SMN"), R("RMIN"), dp, A.add, A.min)
         tt(R("NM"), R("SMN"), dp, A.not_equal)
         scan(R("SM2"), R("NM"), k2, A.mult, A.min)
-        ts(R("S1"), last("SM2"), CEN, A.add)
-        ts(R("AI"), R("S1"), 4095, A.bitwise_and)
         if t >= 1:
             scan(R("SMX"), R("RMAX"), dp, A.add, A.max)
             ts(R("S3"), last("SMX"), -1.0, A.mult)
             ts(R("S2"), R("S3"), 15, A.bitwise_and)
-            tt(R("YG"), last("SMN"), R("GD"), A.subtract)
-            tt(R("GW"), R("S2"), R("YG"), A.is_lt)
+            ts(R("GD"), last("SMX"), MAGIC, A.add, MAGIC, A.subtract)
+            tt(R("YG"), last("SMN"), R("PS3", 16, ALL), A.subtract)
+            tt(R("YG"), R("YG"), last("SMX"), A.add)
+            tt(R("GW"), R("GD"), R("YG"), A.is_lt)
             tt(R("GW"), R("GW"), C("GID", 16 * t - 16, 16 * t), A.mult)
-            tt(R("AF"), R("AI"), R("GW"), A.max)
-            par = R("AF")
+            tt(R("S1"), last("SM2"), R("GW"), A.min)
         else:
-            par = R("AI")
-        cp(R("A16"), par)
-        ops[-1]["key"] = "mark"
+            cp(R("S1"), last("SM2"))
+        begin(t, "rows")
+        ts(R("AI"), R("S1"), 4095, A.bitwise_and)
+        ts(R("A16"), R("AI"), CEN - 4096.0, A.add)
         act(C("QN", 16, 272), IND(C("QT", 0, aend - PAD), R("A16")), AF.Copy)
         for va, sc in (("NVA", -1.0), ("VAF", 1.0)):
-            for h in (1, 0):
-                act(C(va, 512 * h, 512 * h + 128), IND(C("VP", PAD, aend), M("A16", h)), AF.Copy, scale=sc)
-                for j in range(1, 4):
+            for h, (m0, nm) in enumerate(UNITS):
+                act(C(va, 512 * h, 512 * h + 16 * nm), IND(C("VP", PAD, aend), M("A16", h)), AF.Copy, scale=sc)
+                how = OPT["COPY"][va][h]
+                for w in (64, 128, 256):
+                    if w < 16 * nm or (how in "YZ" and w >= 128) or how == "N":
+                        continue
+                    o, a = C(va, 512 * h + w, 512 * h + 2 * w), C(va, 512 * h, 512 * h + w)
+                    if how in "VZ":
+                        cp(o, a)
+                    elif how in "SY":
+                        act(o, a, AF.Copy)
+                    else:
+                        asel(o, [[0, w]], A.is_ge, 0, 0, a)
+                for j in range(1, 4) if how in "YZ" else ():
                     dma("Y", C(va, 512 * h + 128 * j, 512 * h + 128 * j + 128), C(va, 512 * h, 512 * h + 128), key=(va, h, j))
         tr(C("Y", 0, 256), C("QN", 16, 272))
         tr(C("Y", 256, 544), R("QN"))
-        for h in (1, 0):
-            cp(H("QO", h), IND(R("Y"), M("LKM", h)))
+        for a, e in OPT["QO"]:
+            cp(C("QO", 16 * a, 16 * e), IND(R("Y"), C("LKM", a, e)))
+        begin(t, "put")
         if t >= 1:
             tt(R("E"), IND(R("S2"), R("LB")), R("KA"), A.is_equal)
             tt(R("E2"), IND(R("KM"), R("LB")), R("E"), A.mult)
@@ -779,14 +854,22 @@ def rank_program(g, core, T, topo):
             k3 = R("K3")
         else:
             k3 = k2
+        begin(t, "live")
         scan(R("SMX"), R("RL"), k3, A.add, A.max)
-        ts(R("U"), par, float(PAD), A.add)
+        ts(R("U"), R("AI"), PAD + CEN - 4096.0, A.add)
         tt(R("LV"), last("SMX"), C("THR", 16 * tau, 16 * tau + 16), A.is_ge)
         tt(R("U"), R("U"), R("LV"), A.mult)
         tt(R("AD"), R("U"), R("LI"), A.max)
         cp(R("AD16"), R("AD"))
         act(C("VB", tau, 768, 3), IND(C("VP", 0, aend), R("AD16")), AF.Copy)
-        ts(R("SI"), k3, CEN, A.add, TOP, A.add)
+        ops[-1]["key"] = "mark0"
+        begin(t, "once%d" % t)
+        if t == 0:
+            ts(R("SI"), k3, CEN, A.add, TOP, A.add)
+        begin(t, "best")
+        if t in (0, 3, 4):
+            act(C("YB", tau, 768, 3), IND(C("IO", 0, aend), R("AD16")), AF.Identity, bias=-float(PAD))
+        begin(t, "tables")
         if t in (1, 2):
             po = own - L
             gs = GB - T0 + ld
@@ -795,22 +878,29 @@ def rank_program(g, core, T, topo):
             dma("Y", C("AUX", po, po + L), C("AXN", 0, L))
             dma("G", C("VC", gcol, gcol + L), land)
             b = next_bank()
-            mm(PS(b, 0, L), R("M1"), land, True, False)
+            mm(PS(b, 0, L), M1, land, True, False)
             mm(PS(b, 0, L), R("P2"), C("IDB", gs, gs + L), False, True)
             act(C("AUX", gcol, gcol + L), PS(b, 0, L), AF.Copy)
+        begin(t, "send")
         if t < 4:
             hand_on(t, C("QN", 16, 272), qslot(T, t), C("QT", GB + L * t, GB + L * t + L), "aq%d" % t)
             dma("Y", C("QT", own - PAD, own - PAD + L), C("QN", 16, 272))
+        begin(t, "tile")
         if t == 0:
             zexp(2)
             stile(2)
-        for h in (1, 0):
-            ts(H("VA", h), C("NVA", 512 * h, 512 * h + 128), -1.0, A.mult, -64.0, A.add)
+        begin(t, "ends")
+        for u, (m0, nm) in enumerate(UNITS):
+            act(H("VA", u), C("NVA", 512 * u, 512 * u + 16 * nm), AF.Identity, bias=-64.0, scale=-1.0)
         ts(R("LO"), R("VA"), -2.0, A.add, 0.0, A.max)
         ts(R("HI"), R("VA"), 2.0, A.add, 63.0, A.min)
 
-        def lists():
+        def lists(t=t, tau=tau, aend=aend, after=None):
+            if t:
+                ts(R("SI"), R("K3"), CEN, A.add, TOP, A.add)
+                ops[-1]["after"] = after
             ts(R("SI2"), R("SI"), 4095, A.bitwise_and)
+            ops[-1]["after"] = after
             if t in (1, 2):
                 cp(C("SO", L * tau, L * tau + L), R("SI2"))
                 ts(R("SI"), R("SI"), 2 ** 24 - 1 - 4096, A.bitwise_and)
@@ -821,19 +911,26 @@ def rank_program(g, core, T, topo):
                 tr(C("Y", 0, 128), C("NF", 16, 144))
                 tr(C("Y", 256, 416), C("NF", 0, 160))
                 act(C("YS", tau, 384, 3), IND(R("Y"), R("LM0")), AF.Copy)
-                act(C("YB", tau, 768, 3), IND(C("IO", 0, aend), R("AD16")), AF.Identity, bias=-float(PAD))
             if t == 4:
                 dma("Y", R("ys"), R("YS"))
                 dma("Y", R("yb"), R("YB", p=rows(0)))
 
         def lowest():
-            cp(R("OX"), IND(R("AD"), R("LX")))
-            tt(R("U2"), R("LI"), R("AD"), A.subtract)
-            tt(R("X1"), IND(C("IO", 0, aend), R("OX")), R("TRI"), A.add)
-            tt(R("X2"), IND(R("AD"), R("LB2")), R("X1"), A.is_equal)
-            scan(R("X1"), R("RZ2"), R("X2"), A.mult, A.max)
-            tt(R("U2"), R("U2"), C("X1", 31, 512, 32), A.mult)
-            tt(R("U2"), R("U2"), R("AD"), A.add)
+            ts(R("ADH"), IND(R("AD"), R("LD")), -1792.0, A.add)
+            ub = next_bank([b for b in SBANK if b < 2])
+            mm(PS(ub), R("ID"), R("TRI"), True, False)
+            cut()
+            for r in range(16):
+                mm(C("PS%d" % ub, r, 512, 16), R("I128"), C("ADH", 32, 64), False, False)
+                mm(C("PS%d" % ub, r, 512, 16), C("FW", 128 * r, 128 * r + 128), C("ADH", 0, 32), False, r == 15)
+            if OPT["EQ"][t] == "V":
+                ts(R("EQ"), PS(ub), 0.0, A.is_equal, 4096.0, A.mult)
+            else:
+                act(R("EQ"), PS(ub), AF.Abs)
+                act(R("EQ"), R("EQ"), AF.Relu, bias=4096.0, scale=-4096.0)
+            scan(R("EQS"), R("RZ2"), R("EQ"), A.mult, A.max)
+            tt(R("U2"), R("AD"), C("EQS", 31, 512, 32), A.subtract)
+            tt(R("U2"), R("U2"), R("LI"), A.max)
             cp(R("O1"), R("U2"))
             if t == 4:
                 ub = next_bank()
@@ -843,130 +940,160 @@ def rank_program(g, core, T, topo):
                     cp(IND(R("AUX"), C("O1", 2 * b, 2 * b + 2)), C("AXN", L + 32 * b, L + 32 * b + 32))
                 dma("Y", R("yk"), C("AUX", PAD, WT, p=rows(12)))
 
-        raw, sized, sbank = set(), set(), {}
+        sized, picked, sbank = set(), set(), {}
 
-        def gather(h, x, u, how):
+        def gather(u, x, j, how):
             win, va, f = ("ZB", "NVA", A.add) if x == 1 else ("VB", "VAF", A.subtract)
-            o, q0 = 2048 * h + 512 * u, 128 * h + 32 * u
-            d = lambda a, e: C("D%d" % x, o + a, o + e)
+            m0 = UNITS[u][0]
+            d, q = C("D%d" % x, 256 * m0 + 512 * j, 256 * m0 + 512 * j + 512), C("QO", 16 * m0 + 32 * j, 16 * m0 + 32 * j + 32)
             if how == "T":
-                act(d(0, 512), IND(R(win), C("QO", q0, q0 + 32)), AF.Copy)
-                ub = next_bank()
-                mm(PS(ub), R("ID"), d(0, 512), True, False)
-                for k in range(4):
-                    mm(PS(ub, 128 * k, 128 * k + 128), R("ID"), C(va, 512 * h, 512 * h + 128), False, k == 3)
-                act(C("A1", o, o + 512), PS(ub), AF.Abs)
-                raw.add((h, u))
+                nl = 16 * UNITS[u][1]
+                act(d, IND(R(win), q), AF.Copy)
+                ub = next_bank(SBANK)
+                mm(PS(ub), R("ID"), d, True, False)
+                for a in range(0, 512, nl):
+                    mm(PS(ub, a, a + nl), R("ID"), C(va, 512 * u, 512 * u + nl), False, a + nl == 512)
+                act(C("A1", 256 * m0 + 512 * j, 256 * m0 + 512 * j + 512), PS(ub), AF.Abs)
+                act(R("SG", slice(16 * m0 + 32 * j, 16 * m0 + 32 * j + 32), ALL), PS(ub), AF.Sign)
+                picked.add(u)
             elif how == "D":
-                act(d(0, 512), IND(R(win), C("QO", q0, q0 + 32)), AF.Copy)
-                dma("G", d(0, 512), C(va, 512 * h, 512 * h + 512), add=True, key=("sd", h, u))
-            elif how == "v":
-                for k in range(4):
-                    tt(d(128 * k, 128 * k + 128), IND(R(win), C("QO", q0 + 8 * k, q0 + 8 * k + 8)), C(va, 512 * h, 512 * h + 128), f)
+                act(d, IND(R(win), q), AF.Copy)
+                dma("G", d, C(va, 512 * u, 512 * u + 512), add=True, key=("sd", u, j))
             else:
-                tt(d(0, 512), IND(R(win), C("QO", q0, q0 + 32)), C(va, 512 * h, 512 * h + 512), f)
+                tt(d, IND(R(win), q), C(va, 512 * u, 512 * u + 512), f)
 
-        def size(h, x, c, how):
-            d, ab, b = "D%d" % x, "A%d" % x, DBANK[h]
+        def size(u, x, c, how):
+            d, ab, b = "D%d" % x, "A%d" % x, UBANK[u]
+            ch = UNITS[u][0] // 4 + c
             o = PS(b, 128 * x - 128 + 64 * c, 128 * x - 64 + 64 * c)
-            parts = [(a, a + 512) for a in (2048 * h + 1024 * c, 2048 * h + 1024 * c + 512) if x == 2 or (h, a % 2048 // 512) not in raw]
-            if how == "S" and len(parts) == 2:
-                parts = [(parts[0][0], parts[1][1])]
-            for a, e in parts:
-                if how == "V":
-                    ts(C(ab, a, e), C(d, a, e), 0.0, A.max, 64.0, A.min)
-                else:
-                    act(C(ab, a, e), C(d, a, e), AF.Abs)
             if how == "V":
+                for a in (1024 * ch, 1024 * ch + 512):
+                    ts(C(ab, a, a + 512), C(d, a, a + 512), 0.0, A.max, 64.0, A.min)
                 for r in range(16):
-                    mm(o, Wr("WB", r), CH(d, 2 * h + c, r, 16), r == 0, False)
+                    mm(o, Wr("WB", r), CH(d, ch, r, 16), r == 0, False)
                 cut()
-            else:
-                sized.add((h, x))
+            elif how == "S":
+                act(CH(ab, ch), CH(d, ch), AF.Abs)
+                sized.add((u, x))
             for r in range(16):
-                mm(o, Wr("W2" if how == "V" else "B0", r), CH(ab, 2 * h + c, r, 16), r == 0 and how != "V", r == 15)
-            if x == 1 and c == 1:
-                act(H("D1M", h), PS(b, 0, 128), AF.Identity, bias=-0.5)
+                mm(o, Wr("W2" if how == "V" else "B0", r), CH(ab, ch, r, 16), r == 0 and how != "V", r == 15)
+            if x == 1 and c == UNITS[u][1] // 4 - 1:
+                act(H("D1M", u), PS(b, 0, 16 * UNITS[u][1]), AF.Identity, bias=-0.5)
 
-        def attract(h):
-            d2 = PS(DBANK[h], 128, 256)
-            tt(H("N1", h), H("D1M", h), d2, A.is_gt)
-            ts(H("N2", h), d2, 0.0, A.not_equal)
-            if (h, 2) in sized:
-                ts(H("N3", h), d2, 1100.0, A.is_gt)
-                tt(H("N1", h), H("N1", h), H("N3", h), A.add)
-            tt(H("NA", h), H("N1", h), H("N2", h), A.mult)
+        def early(u, c):
+            a = 16 * UNITS[u][0] + 64 * c
+            act(R("SG", slice(a, a + 64), ALL), C("D1", 16 * a, 16 * a + 1024), AF.Sign)
+            picked.add(u)
 
-        def col(ub, r, a=0, e=128):
-            return R("PS%d" % ub, slice(a, e), r % 4) if ub in (4, 5, 6) else C("PS%d" % ub, 4 * a + r % 4, 4 * e, 4)
+        def attract(u):
+            d2 = PS(UBANK[u], 128, 128 + 16 * UNITS[u][1])
+            if u in picked:
+                tt(H("N1", u), H("D1M", u), d2, A.is_le)
+                ts(H("N2", u), d2, 0.0, A.is_equal)
+                if (u, 2) in sized:
+                    ts(H("N3", u), d2, 1100.0, A.is_le)
+                    tt(H("N1", u), H("N1", u), H("N3", u), A.mult)
+                tt(H("NA", u), H("N1", u), H("N2", u), A.max)
+                return
+            tt(H("N1", u), H("D1M", u), d2, A.is_gt)
+            ts(H("N2", u), d2, 0.0, A.not_equal)
+            if (u, 2) in sized:
+                ts(H("N3", u), d2, 1100.0, A.is_gt)
+                tt(H("N1", u), H("N1", u), H("N3", u), A.add)
+            tt(H("NA", u), H("N1", u), H("N2", u), A.mult)
 
-        def ahead(h, rc):
-            ub = sbank[h, rc] = next_bank((4, 5, 6, 0, 1))
+        def col(ub, r, nr):
+            r %= nr
+            return R("PS%d" % ub, slice(r // 4, 128, nr // 4), r % 4) if ub in (4, 5, 6) else C("PS%d" % ub, r, 512, nr)
+
+        def ahead(u, rc):
+            m0, nm = UNITS[u]
+            nr = 32 // nm
+            ub = sbank[u, rc] = next_bank(SBANK)
             held.add(ub)
-            for r in range(4 * rc, 4 * rc + 4):
-                mm(col(ub, r), R("ID"), C("D1", 2048 * h + r, 2048 * h + 2048, 16), r % 4 == 0, False)
-                for u in range(4):
-                    if (h, u) in raw:
-                        mm(col(ub, r, 32 * u, 32 * u + 32), R("ID"), C("NVA", 512 * h + r, 512 * h + 512, 16), False, False)
+            for r in range(nr * rc, nr * rc + nr):
+                mm(col(ub, r, nr), R("ID"), C("D1", 256 * m0 + r, 256 * (m0 + nm), 16), r % nr == 0, False)
             cut()
 
-        def sign(h, rc, how):
-            if (h, rc) not in sbank:
-                ahead(h, rc)
-            ub = sbank[h, rc]
+        def sign(u, rc, how):
+            m0, nm = UNITS[u]
+            nr = 32 // nm
+            ub = next_bank(SBANK) if how == "M" else sbank[u, rc]
             held.discard(ub)
-            for r in range(4 * rc, 4 * rc + 4):
-                mm(col(ub, r), C("FW", 128 * r, 128 * r + 128), H("NA", h), False, r % 4 == 3)
-            sg = R("SG", slice(128 * h, 128 * h + 128), slice(4 * rc, 4 * rc + 4))
-            if how == "V":
+            for r in range(nr * rc, nr * rc + nr):
+                mm(col(ub, r, nr), C("FW", 128 * r, 128 * r + 128), H("NA", u), how == "M" and r % nr == 0, r % nr == nr - 1)
+            sg = R("SG", slice(16 * m0, 16 * (m0 + nm)), slice(nr * rc, nr * rc + nr))
+            if how == "M":
+                tt(sg, PS(ub), sg, A.mult)
+            elif how == "V":
                 ts(sg, PS(ub), -1.0, A.max, 1.0, A.min)
             else:
                 act(sg, PS(ub), AF.Sign)
 
-        def count(h):
-            b, mh = DBANK[h], slice(8 * h, 8 * h + 8)
-            for k in range(16):
-                mm(PS(b, 0, 8), R("ID"), C("NA", 128 * h + 8 * k, 128 * h + 8 * k + 8), k == 0, k == 15)
-            act(M("CN", h), PS(b, 0, 8), AF.Identity, scale=-1.0 / 128.0)
-            mm(R("PS3", mh, ALL), R("ID"), H("VA", h), True, False)
+        def sums(u, rs=ALL):
+            m0, nm = UNITS[u]
+            if nm == 8:
+                return R("PS3", slice(m0, m0 + nm), rs)
+            return PS(UBANK[u], 256, 320) if rs == ALL else C("PS%d" % UBANK[u], 256 + rs, 320, 16)
+
+        def count(u, how):
+            m0, nm = UNITS[u]
+            if how == "M":
+                mm(sums(u), R("ID"), H("VA", u), True, False)
+                cut()
+                return
+            if how == "V":
+                src, a, o = "NA", 16 * m0, 0
+                for w in (8 * nm, 4 * nm, 2 * nm, nm):
+                    tt(C("NT", o, o + w), C(src, a, a + w), C(src, a + w, a + 2 * w), A.add)
+                    src, a, o = "NT", o, o + w
+                ts(M("CN", u), C("NT", a, a + nm), -1.0 / 128.0, A.mult)
+            else:
+                for k in range(16):
+                    mm(PS(UBANK[u], 0, nm), R("ID"), C("NA", 16 * m0 + nm * k, 16 * m0 + nm * k + nm), k == 0, k == 15)
+                act(M("CN", u), PS(UBANK[u], 0, nm), AF.Identity, scale=-1.0 / 128.0)
+            mm(sums(u), R("ID"), H("VA", u), True, False)
             cut()
             for r in range(16):
-                mm(R("PS3", mh, r), C("FW", 128 * r, 128 * r + 128), M("CN", h), False, False)
+                mm(sums(u, r), C("FW", 128 * r, 128 * r + 128), M("CN", u), False, False)
             cut()
 
-        def pull(h, c):
-            mh, rc = slice(8 * h, 8 * h + 8), slice(8 * c, 8 * c + 8)
+        def pull(u, c):
+            m0, nm = UNITS[u]
+            rc = slice(8 * c, 8 * c + 8) if nm == 8 else ALL
             for k in range(16):
-                mm(R("PS3", mh, rc), R("ID"), R("SG", slice(128 * h + 8 * k, 128 * h + 8 * k + 8), rc), False, c == 1 and k == 15)
+                mm(sums(u, rc), R("NJ" if u in picked else "ID"), R("SG", slice(16 * m0 + nm * k, 16 * m0 + nm * k + nm), rc), False, c == nm // 4 - 1 and k == 15)
             cut()
 
-        def finish(h):
-            tt(H("H1", h), R("PS3", slice(8 * h, 8 * h + 8), ALL), H("HI", h), A.min)
-            tt(H("YV", h, L * t), H("H1", h), H("LO", h), A.max)
+        def finish(u):
+            m0, nm = UNITS[u]
+            tt(H("H1", u), sums(u), H("HI", u), A.min)
+            tt(H("YV", u, L * t), H("H1", u), H("LO", u), A.max)
             if t == 4:
-                dma("Y", H("yv", h, L * t), H("YV", h, L * t))
+                dma("Y", H("yv", u, L * t), H("YV", u, L * t))
                 return
-            hand_on(t, H("YV", h, L * t), nslot(T, t, h), H("LAND", h, L * t), "an%d" % (2 * t + h))
-            o = PS(DBANK[h], 256, 384)
-            mm(o, R("P2"), H("IDB", h, L * t), True, False)
+            for j, (a, e) in enumerate(SENDS):
+                if a == 16 * m0:
+                    hand_on(t, C("YV", L * t + a, L * t + e), nslot(T, t, j), C("LAND", L * t + a, L * t + e), "an%d" % (2 * t + j))
+            o = PS(UBANK[u], 320, 320 + 16 * nm)
+            mm(o, R("P2"), H("IDB", u, L * t), True, False)
             if t < 2:
-                mm(o, R("M2"), H("VA", h), False, False)
+                mm(o, M2, H("VA", u), False, False)
             cut()
-            mm(o, R("M1"), H("YV", h, L * t), False, True)
-            act(H("AXN", h), o, AF.Copy)
-            for bl in range(4 * h + 3, 4 * h - 1, -1):
+            mm(o, M1, H("YV", u, L * t), False, True)
+            act(H("AXN", u), o, AF.Copy)
+            for bl in range((m0 + nm) // 2 - 1, m0 // 2 - 1, -1):
                 cp(IND(R("VC"), C("O1", 2 * bl, 2 * bl + 2)), C("YV", L * t + 32 * bl, L * t + 32 * bl + 32))
                 cp(IND(R("AUX"), C("O1", 2 * bl, 2 * bl + 2)), C("AXN", 32 * bl, 32 * bl + 32))
 
-        steps = {"g": gather, "z": size, "a": attract, "i": ahead, "s": sign, "c": count, "p": pull, "f": finish, "l": lists, "d": lowest,
+        steps = {"e": early, "g": gather, "z": size, "a": attract, "i": ahead, "s": sign, "c": count, "p": pull, "f": finish, "l": lists if t == 4 or not OPT["LATER"] else lambda: later.append(lists), "d": lowest,
                  "o": lambda c: own_dist(t + 1, c) if t < 2 else None}
         for w in OPT["STEP4"][t].split():
-            chain["on"] = () if w[0] in "ldo" else OPT["CHAIN"]
+            begin(t, w)
             steps[w[0]](*[int(x) if x.isdigit() else x for x in w[1:]])
-        chain["on"] = ()
+        begin(t, "out")
         new = C("YV", L * t, L * t + L)
         if t < 4:
-            dma("G", C("VP", own, own + L), new, add=True)
             dma("Y", C("yv", L * t, L * t + L), new)
 
     if "seq" not in ORDER:

import numpy as np
from concourse.mybir import AluOpType, ActivationFunctionType

A = AluOpType
AF = ActivationFunctionType
TILE = [0, 1, 2, 1, 2]
HOP = [1, 4, 1, 4]
T0, L, GB, W = 1024, 256, 2304, 3328
PAD = 256
WT = PAD + W
MAGIC = 1.5 * 2.0 ** 36
BIG = 2.0 ** 26
TOP = 2.0 ** 24
KOFF = -2040.0 * 8192.0
CEN = 3700.0
CYC, CPE, WAKE, LREM, GAT, SCA = 0.00087, 0.00045, 0.3, (5.0, 1.5, 5.0, 1.5), 1.56, 3.8
PASSES, ROUNDS, BLEND, SEED, JIT = 1, 12, 0.3, 0, 0.3
MOVES, SPREAD, LATE, HEAT, SWEEPS = 2000, 0.03, 0.3, 0.1, 4
ONLY = None
LQ = 14.0
UNITS = [(8, 8), (0, 8)]
UBANK, SBANK = [2, 7], (4, 5, 6, 0, 1)
SENDS = [(128, 256), (0, 128)]
NOWAIT = False
OPT = {
    "OWNS": {0: (0,), 1: (3, 1, 0), 2: (3, 2, 1, 0)},
    "ZG": ((8, 16, "V"), (0, 8, "G")),
    "GV": [(), (1,), (), (1,), ()],
    "FIRST": ((3,), (3,)),
    "EQ": "VVVVV",
    "LATER": True,
    "COPY": {"NVA": "VVVV", "VAF": "YYYY"},
    "QO": ((8, 16), (0, 8)),
    "CHAIN": (),
    "STEP4": ["o3 o2 g110D g111D g112D g113D g010V g011V z010S g012V g013V z011S g020V g021V z020S g022V g023V z021V d i00 i01 i02 i03 "
              "z110S e10 z111S e11 g120V g121V z120S g122V g123V z121V a0 s00S c0V s01S s02S s03S p00 p01 f0 a1 c1M s10M s11M s12M s13M "
              "p10 p11 f1 l o1 o0"] * 5,
}
PG, PA = 512, 512
ORDER = {}

f32, b16, f16, i32, u16 = "float32", "bfloat16", "float16", "int32", "uint16"
SCRATCH = {}
for _n, _w, _d in [
    ("VN", 1024, b16), ("ZS", 768, b16), ("ZT", 768, b16), ("ZB", 768, b16), ("SN", 768, i32), ("NQ", 1024, i32),
    ("KC", 64, i32), ("KF", 96, f32), ("KLO", 64, b16), ("KHI", 64, b16), ("KI", 128, i32), ("BC", 48, i32), ("BCF", 96, b16), ("BCI", 96, i32),
    ("BR", 768, b16), ("KO", 64, u16), ("BO", 48, u16), ("VCB", 1024, b16),
    ("QT", W, f32), ("VP", WT, f32), ("VC", WT, f32), ("AUX", WT, f32), ("IO", WT, f32), ("VB", 768, f32),
    ("IDB", 2304, b16), ("ILO", 144, b16), ("IHI", 144, b16), ("GA", 1024, b16), ("GC", 1024, b16),
    ("D1", 4096, b16), ("D2", 4096, b16), ("A1", 4096, b16), ("A2", 4096, b16), ("FW", 2048, b16), ("ZX0", 4096, b16), ("ZX1", 4096, b16),
    ("B0", 144, b16), ("WM", 144, b16), ("WN", 144, b16), ("WP", 144, b16), ("WA", 144, b16), ("WA0", 144, b16), ("W2", 144, b16), ("WB", 144, b16), ("BF", 144, b16),
    ("ID", 128, b16), ("NI", 128, b16), ("CI", 128, b16), ("MX", 132, b16), ("NJ", 128, b16), ("P2", 128, b16), ("ONE", 144, b16),
    ("PI", 8, i32), ("CL", 26, f32), ("PF", 128, b16), ("TI", 16, i32), ("TF", 16, f32), ("TG", 16, f32), ("TH", 16, f32),
    ("LMK", 16, u16), ("LM0", 8, u16), ("LKM", 16, u16), ("LK", 4, u16), ("LB", 16, u16), ("LD", 4, u16), ("REV", 8, u16), ("LI", 16, f32),
    ("TRI", 512, b16), ("RMAX", 256, b16), ("RMIN", 256, b16), ("RL", 256, b16), ("EQ", 512, b16), ("KA", 256, f32),
    ("ADH", 64, f16), ("EQS", 512, b16), ("RZ2", 512, b16), ("I128", 128, b16), ("NT", 128, b16),
    ("THR", 48, f32), ("NF", 288, f32), ("QN", 288, f32), ("Y", 544, f32), ("KS", 768, f32), ("SO", 768, u16), ("QO", 256, u16),
    ("SMN", 256, f32), ("SMX", 256, f32), ("SM2", 256, f32), ("NM", 256, b16), ("E", 256, f32), ("E2", 256, f32), ("K3", 256, f32),
    ("S1", 16, i32), ("S2", 16, i32), ("S3", 16, i32), ("AI", 16, i32), ("A16", 16, u16), ("KM", 16, f32), ("LV", 16, f32), ("U", 16, f32), ("U2", 16, f32),
    ("GD", 16, f32), ("YG", 16, f32), ("GW", 16, f32), ("AF", 16, f32), ("GID", 64, f32), ("GK", 64, f32),
    ("AD", 16, f32), ("AD16", 16, u16), ("O1", 16, u16), ("SI", 256, i32), ("SI2", 256, i32),
    ("XG", 256, b16), ("LAND", 1024, b16), ("NVA", 2048, b16), ("VAF", 2048, f32), ("VA", 256, b16),
    ("D1M", 256, f32), ("N1", 256, b16), ("N2", 256, b16), ("N3", 256, b16), ("NA", 256, b16), ("CN", 16, b16), ("H1", 256, b16), ("LO", 256, b16), ("HI", 256, b16),
    ("YV", 1280, b16), ("AXN", 512, f32), ("YS", 384, f32), ("YB", 768, f32),
]:
    SCRATCH[_n] = ("sbuf", [128, _w], _d)
ALIAS = {"XM": "A1", "XA": "A2", "XS": "D2", "KD": "GC"}
PART = {}
for _grp in (("KLO", "KHI", "ILO", "IHI"), ("U", "U2", "LV", "GD", "YG", "GW", "AF", "GID", "GK"), ("N1", "N2", "N3", "H1", "LO", "HI", "NM"),
             ("S1", "S3", "AI"), ("WM", "WN", "WP", "WA", "WA0", "W2", "WB"), ("TF", "TG", "TH", "LI"), ("LMK", "LM0", "LKM", "LK", "LB", "LD", "REV"),
             ("NI", "CI"), ("RMAX", "RMIN", "RL")):
    _o = 0
    for _n in _grp:
        _where, _s, _d = SCRATCH.pop(_n)
        PART[_n] = ("X" + _grp[0], _o, _s[1])
        _o += _s[1]
    SCRATCH["X" + _grp[0]] = ("sbuf", [128, _o], _d)
SCRATCH["ZG"] = ("sbuf", [128, 16, 256], b16)
SCRATCH["ZG2"] = ("sbuf", [128, 16, 256], b16)
SCRATCH["SG"] = ("sbuf", [128, 256, 16], b16)
for _j in range(8):
    SCRATCH["PS%d" % _j] = ("psum", [128, 32, 16] if _j == 3 else [128, 128, 4] if _j in (4, 5, 6) else [128, 512], f32)
DBANK = (7, 2)
NDMA = 128
SEMAPHORES = ["cV", "cS", "cT", "cG"] + ["d%d" % _j for _j in range(NDMA)] + ["aq%d" % _j for _j in range(4)] + ["an%d" % _j for _j in range(8)] + ["fwd"]
MASKS = {}


def bits(shape, idx):
    key = (tuple(shape), repr(idx))
    if key not in MASKS:
        n = int(np.prod(shape))
        m = np.zeros(n, bool)
        m[np.arange(n).reshape(shape)[idx].reshape(-1)] = True
        MASKS[key] = int.from_bytes(np.packbits(m, bitorder="little").tobytes(), "little")
    return MASKS[key]


def relay_of(T, topo, src, dst):
    c = [x for x in topo.cores_of(src) if T.rank_of(x) is None and topo.may_write(x, dst)]
    c.sort(key=lambda x: topo.die(x) != topo.die(src))
    return c[0]


def routes(T, topo):
    n = len(T.cores)
    out = []
    for t in range(4):
        for r in range(n):
            s, d = T.cores[r], T.cores[(r + HOP[t]) % n]
            out.append((t, s, None if topo.may_write(s, d) else relay_of(T, topo, s, d), d))
    return out


def qslot(T, t):
    return T["QT"][:, GB + L * t:GB + L * t + L]


def nslot(T, t, j):
    return T["LAND"][:, L * t + SENDS[j][0]:L * t + SENDS[j][1]]


def relay_program(g, core, T, topo):
    sent = 0
    for t, s, via, d in routes(T, topo):
        if via != core:
            continue
        n_in = len(topo.engines(s, core))
        rid, pid = topo.addr(d, core)
        for sem, ap in (("aq%d" % t, qslot(T, t)), ("an%d" % (2 * t), nslot(T, t, 0)), ("an%d" % (2 * t + 1), nslot(T, t, 1))):
            g.wait_ge(T.sem[sem], n_in)
            g.remote_dma(ap, ap, T.sem[sem], T.sem["fwd"], pid, rid, topo.mask(core, d))
            sent += len(topo.engines(core, d))
    if sent:
        g.wait_ge(T.sem["fwd"], sent)


def place(ops, order, edges, first, fixed=None, near=()):
    line = {}
    start = list(fixed) if fixed else [0.0] * len(ops)
    floor = min([fixed[i] for i in near], default=0.0)
    for i in sorted(near, key=lambda i: fixed[i]):
        if ops[i]["q"]:
            line.setdefault(ops[i]["q"], []).append((fixed[i], fixed[i] + ops[i]["cost"], i))
    end = [s + o["cost"] for s, o in zip(start, ops)]
    for i in order:
        o = ops[i]
        t = first[i] if first[i] > floor else floor
        for j, d in edges[i]:
            if end[j] + d > t:
                t = end[j] + d
        c = o["cost"]
        if o["q"]:
            ln = line.setdefault(o["q"], [])
            k = m = len(ln)
            while k > 0 and ln[k - 1][0] >= t:
                k -= 1
            if k > 0 and ln[k - 1][1] > t:
                t = ln[k - 1][1]
            while k < m and t + c > ln[k][0] + 1e-9:
                t = max(t, ln[k][1])
                k += 1
            ln.insert(k, (t, t + c, i))
        start[i] = t
        end[i] = t + c
    return start, {q: [e[2] for e in ln] for q, ln in line.items()}


def plan_calls(ops):
    n = len(ops)
    acc = {}
    bank = {}
    pred = []
    for i, o in enumerate(ops):
        q = o["q"]
        need = {}
        if o["ext"]:
            need[o["sent"]] = False
        if o["after"] is not None:
            need[o["after"]] = False
        for regs, w in ((o["rd"], False), (o["wr"], True)):
            for name, cm, pm in regs:
                for j, cm2, pm2, w2 in acc.get(name, []):
                    if j == i or not (cm & cm2 and pm & pm2) or not (w or w2):
                        continue
                    same = ops[j]["q"] == q and not ops[j]["dma"] and not o["dma"]
                    free = same and (q == "T" or (NOWAIT and o["sct"] == name and ops[j]["sct"] == name))
                    need[j] = need.get(j, False) or not free
        for name in {r[0] for r in o["rd"] + o["wr"] if r[0].startswith("PS")}:
            user, run, before = bank.setdefault(name, [q, [], []])
            if user != q:
                bank[name] = [q, [], run]
                before, run = run, bank[name][1]
            for j in before:
                need[j] = True
            if q == "T" and run:
                need.setdefault(run[-1], False)
            run.append(i)
        for regs, w in ((o["rd"], False), (o["wr"], True)):
            for name, cm, pm in regs:
                lst = acc.setdefault(name, [])
                if w:
                    lst[:] = [e for e in lst if (e[1] & ~cm) or (e[2] & ~pm) or e[0] == i or (NOWAIT and ops[e[0]]["sct"] == name and o["sct"] == name)]
                lst.append((i, cm, pm, w))
        pred.append(need)
    fwd = [[(j, ops[j]["lat"] + (WAKE if s else 0.0)) for j, s in pred[i].items()] for i in range(n)]
    bwd = [[] for _ in range(n)]
    for i in range(n):
        for j, d in fwd[i]:
            bwd[j].append((i, d))
    level = [0.0] * n
    for i in range(n - 1, -1, -1):
        level[i] = ops[i]["cost"] + max([level[j] + d for j, d in bwd[i]] + [ops[i]["lat"]])
    zero = [0.0] * n
    lats = [o["lat"] for o in ops]
    best_end, seq = None, None
    for _ in range(ROUNDS):
        start, sq = place(ops, sorted(range(n), key=lambda i: (-level[i], i)), fwd, zero)
        first = (start, sq)
        for p in range(PASSES + 1):
            end = max(start[i] + ops[i]["cost"] + lats[i] for i in range(n))
            if best_end is None or end < best_end:
                best_end, seq, first, best_start = end, sq, (start, sq), start
            if p < PASSES:
                back, _s = place(ops, sorted(range(n), key=lambda i: (-(start[i] + ops[i]["cost"]), -i)), bwd, lats)
                start, sq = place(ops, sorted(range(n), key=lambda i: (-(back[i] + ops[i]["cost"]), i)), fwd, zero)
        nxt = {a: b for ln in first[1].values() for a, b in zip(ln, ln[1:])}
        true = [0.0] * n
        for i in sorted(range(n), key=lambda i: (-first[0][i], -i)):
            true[i] = ops[i]["cost"] + max([true[j] + d for j, d in bwd[i]] + [lats[i], true[nxt[i]] if i in nxt else 0.0])
        level = [(1 - BLEND) * a + BLEND * b for a, b in zip(level, true)]
        if _ % 3 == 2:
            jit = np.random.default_rng(SEED + _).uniform(1 - JIT, 1 + JIT, n).tolist()
            for i in range(n - 1, -1, -1):
                level[i] = ops[i]["cost"] * jit[i] + max([level[j] + d for j, d in bwd[i]] + [lats[i], 0.98 * true[i]])
    rng = np.random.default_rng(SEED)
    start = best_start
    done = lambda st, i: st[i] + ops[i]["cost"] + lats[i]
    tags = {ops[i]["tag"]: i for i in range(n)}
    for sweep, w in [(s, w) for s in range(SWEEPS) for w in ONLY or range(6)]:
        marks = [i for i in range(n) if ops[i]["key"] == "mark%d" % (sweep % 2)] + [None]
        lo = start[marks[w - 1]] if w else -1.0
        hi = start[marks[w]] + 3.0 if marks[w] is not None else 1e9
        free = [i for i in range(n) if lo < start[i] <= hi]
        near = [i for i in range(n) if lo - 8.0 < start[i] <= lo]
        some = [i for i in free if ops[i]["q"] in ("V", "S", "T", "G")]
        inside = set(free)

        def score(st):
            if marks[w] is None:
                return max(done(st, i) for i in free) + SPREAD * sum(st[i] for i in free) / len(free)
            m = st[marks[w]]
            return m + SPREAD * sum(st[i] for i in free) / len(free) + LATE * sum(ops[i]["cost"] for i in some if st[i] > m)

        def held_up(st, sq):
            before = {b: a for ln in sq.values() for a, b in zip(ln, ln[1:])}
            i = marks[w] if marks[w] is not None else max(free, key=lambda i: done(st, i))
            out = []
            while i in inside:
                j = max(fwd[i], key=lambda e: st[e[0]] + ops[e[0]]["cost"] + e[1], default=None)
                if j is not None and st[j[0]] + ops[j[0]]["cost"] + j[1] >= st[i] - 1e-9:
                    i = j[0]
                elif i in before:
                    if before[i] in inside:
                        out.append((before[i], i))
                    i = before[i]
                else:
                    break
            return out, before

        cur, cur_seq = place(ops, sorted(free, key=lambda i: (start[i], i)), fwd, zero, start, near)
        now = score(cur)
        for w2 in range(1, 5) if w else ():
            key = {}
            for i in free:
                rd, tag = ops[i]["tag"]
                j = tags.get((rd - w + w2, tag))
                key[i] = start[i] - lo if j is None else start[j] - start[marks[w2 - 1]]
                key[i] = max([key[i]] + [key[a] + 1e-5 for a, d in fwd[i] if a in inside])
            st, sq = place(ops, sorted(free, key=key.get), fwd, zero, start, near)
            if score(st) < now:
                cur, cur_seq, now = st, sq, score(st)
        best = now
        keep = cur
        pairs, before = held_up(cur, cur_seq)
        for _ in range(MOVES):
            key = {i: cur[i] + 1e-7 * i for i in free}
            u = rng.random()
            if u < 0.3 or not pairs:
                i = some[int(rng.integers(0, len(some)))]
                sign = -1 if rng.random() < 0.5 else 1
                key[i] += sign * float(rng.uniform(0.2, 5.0))
            else:
                j, i = pairs[int(rng.integers(0, len(pairs)))]
                if u < 0.65:
                    for _s in range(int(rng.integers(0, 4))):
                        if before.get(j) in inside:
                            j = before[j]
                    sign, key[i] = -1, key[j] - 1e-3
                else:
                    sign, key[j], i = 1, key[i] + float(rng.uniform(1e-3, 3.0)), j
            edges = fwd if sign < 0 else bwd
            todo = [i]
            while todo:
                a = todo.pop()
                for b, d in edges[a]:
                    if b in inside and sign * (key[a] - key[b]) >= 0:
                        key[b] = key[a] + sign * 1e-5
                        todo.append(b)
            st, sq = place(ops, sorted(free, key=key.get), fwd, zero, start, near)
            s = score(st)
            if s <= now - HEAT * 0.03 ** (_ / MOVES) * np.log(1.0 - rng.random()):
                now, cur = s, st
                pairs, before = held_up(st, sq)
                if s < best:
                    best, keep = s, st
        order = sorted(range(n), key=lambda i: (0, keep[i], i) if start[i] <= hi else (1, start[i], i))
        st, sq = place(ops, order, fwd, zero)
        if sweep == 0 or max(done(st, i) for i in range(n)) <= max(done(start, i) for i in range(n)):
            start, seq = st, sq
    best_end = max(start[i] + ops[i]["cost"] + lats[i] for i in range(n))
    ORDER["end"] = best_end
    ORDER["dbg"] = (ops, start, fwd, seq, marks)
    pos = {}
    for q in seq:
        for k, i in enumerate(seq[q]):
            pos[i] = k
    wait = [[] for _ in range(n)]
    for q in seq:
        seen = {}
        for i in seq[q]:
            best = {}
            for j, s in pred[i].items():
                if s:
                    key = ("x", j) if (ops[j]["dma"] or ops[j]["ext"]) else ops[j]["q"]
                    if key not in best or pos.get(j, 0) > pos.get(best[key], 0):
                        best[key] = j
            for key, j in best.items():
                if seen.get(key, -1) < pos.get(j, 0):
                    seen[key] = pos.get(j, 0)
                    wait[i].append(j)
    return seq, wait


def rank_program(g, core, T, topo):
    if T.rank_of(core) is None:
        relay_program(g, core, T, topo)
        return
    ops = []
    part = [-9, "", 0]
    chain = {"on": ()}
    Q = {"V": g.vector, "S": g.scalar, "T": g.tensor, "G": g, "Y": g.sync}
    ALL = slice(None)

    def R(name, *idx, p=ALL):
        name = ALIAS.get(name, name)
        if name in PART:
            name, o, w = PART[name]
            s = idx[0] if idx else slice(0, w)
            idx = (slice(o + s.start, o + s.stop, s.step),)
        if name not in SCRATCH:
            return {"ap": T[name][(p,) + idx] if idx else T[name][p], "reg": [], "n": 0, "w": 0, "ps": False}
        where, shape, d = SCRATCH[name]
        if not idx:
            idx = tuple(slice(0, n) for n in shape[1:])
        ap = T[name][(p,) + idx]
        cm = bits(shape[1:], idx)
        return {"ap": ap, "reg": [(name, cm, bits([128], p))], "n": cm.bit_count(), "w": 2 if d in (b16, f16, u16) else 4, "ps": where == "psum"}

    def C(name, a, b, s=None, p=ALL):
        return R(name, slice(a, b, s), p=p)

    def IND(win, off):
        return {"ap": win["ap"].indirect(off["ap"]), "reg": win["reg"], "off": off["reg"], "n": 16 * off["n"], "w": 4, "ps": False}

    def op(q, fn, outs, ins, dma=0, ext=None, two=False, key=None, sent=None):
        rd, wr = [], []
        ins = [x for x in ins if isinstance(x, dict)]
        for x in ins:
            rd += x["reg"] + x.get("off", [])
        for x in outs:
            wr += x["reg"]
            rd += x.get("off", [])
        n = outs[0]["n"] if outs else 0
        lat = 0.0
        sct = None
        if ext:
            cost, lat = 0.001, LREM[key] + (LQ if ext[0].startswith("aq") else 0.0)
        elif dma:
            by = 128 * max([x["n"] * x["w"] for x in outs + ins]) * (2 if two else 1)
            cost, lat = (1.0 if q == "G" else 0.15), 2.2 + by / (2e5 if dma > 0 else 4e4)
        elif q == "T":
            cost = max(64, ins[1]["n"]) * CPE * (1 if ins[1]["w"] == 2 else 4)
        elif q == "G":
            cost = 0.15 + 2 * n * CYC
        elif "off" in outs[0]:
            cost = 0.05 + n * SCA * CYC
            sct = outs[0]["reg"][0][0]
        elif any("off" in x for x in ins):
            cost = 0.06 + n * GAT * CYC
        elif q == "S":
            cost = 0.08 + n * CYC
        else:
            f = 0.5 if all(x["w"] == 2 for x in outs + ins if x["n"] > 1) else 1.0
            if two and not any(x["ps"] for x in ins):
                f *= 2
            cost = max(0.066, n * f * CYC)
        ops.append({"q": q, "fn": fn, "rd": rd, "wr": wr, "dma": dma, "ext": ext, "inc": False, "cost": cost, "lat": lat, "key": key, "sct": sct,
                    "tag": (part[0], (part[1], len(ops) - part[2])), "sent": sent, "after": chain.get(q) if q in chain["on"] and not (dma or sct) else None})
        if q in chain["on"] and not (dma or sct):
            chain[q] = len(ops) - 1

    def begin(t, name):
        part[:] = [t, name, len(ops)]
        cut()

    def a_(x):
        return x["ap"] if isinstance(x, dict) else x

    def tt(o, a, b, f):
        op("V", lambda e: e.tensor_tensor(o["ap"], a["ap"], b["ap"], f), [o], [a, b], two=True)

    def ts(o, a, s1, f1, s2=None, f2=None):
        if s2 is None:
            op("V", lambda e: e.tensor_scalar(o["ap"], a["ap"], a_(s1), None, f1), [o], [a, s1])
        else:
            op("V", lambda e: e.tensor_scalar(o["ap"], a["ap"], a_(s1), a_(s2), f1, f2), [o], [a, s1, s2])

    def cp(o, a):
        op("V", lambda e: e.tensor_copy(o["ap"], a["ap"]), [o], [a])

    def ms(o, c):
        op("V", lambda e: e.memset(o["ap"], c), [o], [])

    def scan(o, a, b, f1, f2):
        op("V", lambda e: e.tensor_tensor_scan(o["ap"], a["ap"], b["ap"], 0.0, f1, f2), [o], [a, b])

    def tr(o, a):
        op("V", lambda e: e.transpose(o["ap"], a["ap"]), [o], [a])

    def act(o, a, f, bias=None, scale=None):
        kw = {}
        if bias is not None:
            kw["bias"] = a_(bias)
        if scale is not None:
            kw["scale"] = a_(scale)
        op("S", lambda e: e.activation(o["ap"], a["ap"], f, **kw), [o], [a, bias, scale])

    run = [None]

    def mm(o, l, r, st, sp):
        op("T", lambda e: e.matmul(o["ap"], l["ap"], r["ap"], st, sp), [o], [l, r])
        bank = o["reg"][0][0]
        if run[0] == (len(ops) - 2, bank):
            new, old = ops.pop(), ops[-1]
            if "T" in chain["on"]:
                chain["T"] = len(ops) - 1
            f0, f1 = old["fn"], new["fn"]
            old["fn"] = lambda e: (f0(e), f1(e))[1]
            old["rd"] += new["rd"]
            old["wr"] += new["wr"]
            old["cost"] += new["cost"]
        run[0] = (len(ops) - 1, bank)

    def cut():
        run[0] = None

    def iota(o, pat, base, cm, isint=False):
        if isint:
            op("G", lambda e: e.iota(o["ap"], pat, base, cm), [o], [])
        else:
            op("G", lambda e: e.iota(o["ap"], pat, base, cm, allow_small_or_imprecise_dtypes=True), [o], [])

    def gfill(o, c):
        iota(o, [[0, o["n"]]], c, 0)

    def asel(o, pat, f, base, cm, a=None):
        a = a or o
        op("G", lambda e: e.affine_select(o["ap"], a["ap"], pat, f, 0.0, base, cm), [o], [a])

    def dma(q, o, a, add=False, key=None):
        if add:
            op(q, lambda e: e.dma_start(o["ap"], a["ap"], accum_op=A.add), [o], [a, o], dma=16, key=key, two=True)
        else:
            op(q, lambda e: e.dma_start(o["ap"], a["ap"]), [o], [a], dma=16, key=key)

    def hand_on(t, src, dst_ap, landed, sem):
        for t2, s, via, d in routes(T, topo):
            if t2 == t and s == core:
                to = d if via is None else via
                rid, pid = topo.addr(to, core)
                mask = topo.mask(core, to)
                op("G", lambda e, ls: e.remote_dma(dst_ap, src["ap"], T.sem[sem], ls, pid, rid, mask), [], [src],
                   dma=-len(topo.engines(core, to)))
        sent = len(ops) - 1
        for t2, s, via, d in routes(T, topo):
            if t2 == t and d == core:
                op(None, None, [landed], [], ext=(sem, len(topo.engines(s if via is None else via, core))), sent=sent, key=t)

    def Wr(name, r):
        return C(name, 15 - r, 143 - r)

    def PS(b, a=0, e=512):
        return R("PS%d" % b, slice(a // 4, e // 4), ALL) if b in (4, 5, 6) else C("PS%d" % b, a, e)

    rows = lambda x: slice(x, 128, 16)
    CLc = lambda j: C("CL", j, j + 1)
    PIc = lambda j: C("PI", j, j + 1)
    CH = lambda nm, c, r=0, s=None: C(nm, 1024 * c + r, 1024 * c + 1024, s)

    dma("Y", R("ZS"), R("zs"))
    dma("S", R("SN"), R("sn"))
    dma("Y", R("KC"), R("kid"))
    dma("Y", R("VN"), R("vn"))
    dma("Y", R("KD"), R("vn"))
    dma("Y", R("BC"), R("bst"))
    dma("Y", R("BR"), R("zs"))
    dma("Y", R("NQ"), R("nq"))

    iota(PIc(0), [[1, 1]], 0, 1, True)
    iota(R("TF"), [[0, 8], [1, 2]], 0, 0)
    iota(R("TG"), [[16, 16]], 0, 0)
    iota(R("TI"), [[1, 16]], 0, 0, True)
    ms(R("B0"), 0.0)
    ms(R("ID"), 1.0)
    ms(C("B0", 15, 144, 16), 1.0)
    ts(PIc(1), PIc(0), 15, A.bitwise_and)
    ts(PIc(2), PIc(0), 4, A.arith_shift_right, 1, A.bitwise_and)
    ts(PIc(3), PIc(0), 1, A.bitwise_and)
    ts(PIc(4), PIc(0), 2, A.arith_shift_right, 3, A.bitwise_and)
    ts(PIc(5), PIc(0), 3, A.bitwise_and)
    ts(PIc(6), PIc(0), 7, A.bitwise_and)
    ts(PIc(7), PIc(0), 3, A.arith_shift_right, 1, A.bitwise_and)
    ms(C("NF", 0, 16), 0.0)
    ms(C("NF", 272, 288), 0.0)
    ms(R("KF"), 0.0)
    cp(C("CL", 0, 7), C("PI", 1, 8))
    asel(R("B0"), [[-1, 144]], A.is_ge, 15, 1)
    asel(R("B0"), [[1, 144]], A.is_ge, 0, -1)
    ts(C("TH", 8, 12), C("TG", 0, 4), 1.0 / 16.0, A.mult, CLc(3), A.is_equal)
    act(R("MX"), C("B0", 0, 132), AF.Copy, scale=0.0)
    for j in range(4):
        act(C("MX", 4 + j, 132, 16), C("B0", 15, 128, 16), AF.Copy, scale=C("TH", 8 + j, 9 + j))
    M1, M2 = C("MX", 4, 132), C("MX", 0, 128)
    asel(R("ID"), [[-1, 128]], A.is_equal, 0, 1)
    ms(R("ONE"), 1.0)
    ts(R("TF"), R("TF"), CLc(1), A.not_equal, 272.0, A.mult)
    ts(R("LI"), R("TG"), CLc(0), A.add)
    ts(CLc(7), CLc(2), CLc(1), A.not_equal, 272.0, A.mult)
    ts(CLc(8), CLc(4), 16.0, A.mult, CLc(3), A.add)
    tt(R("TF"), R("TF"), R("TG"), A.add)
    ts(CLc(8), CLc(8), CLc(7), A.add)
    ts(CLc(9), CLc(5), 16.0, A.mult, CLc(6), A.add)
    ts(R("LMK"), R("TF"), CLc(0), A.subtract, 15.0, A.add)
    ts(R("LK"), C("TG", 0, 4), 0.25, A.mult, CLc(8), A.add)
    ts(CLc(9), CLc(9), CLc(7), A.add)
    for u, (m0, nm) in enumerate(UNITS):
        ts(C("TH", u, u + 1), CLc(9 if nm == 8 else 8), 16.0 * m0, A.add)
        ts(C("LKM", m0, m0 + nm), C("TG", 0, nm), 1.0 / nm, A.mult, C("TH", u, u + 1), A.add)
    cp(R("LB"), R("TI"))
    ts(CLc(10), CLc(0), 8.0, A.is_equal)
    ts(CLc(11), CLc(0), 9.0, A.is_equal)
    ts(CLc(12), CLc(0), 11.0, A.is_equal)
    ts(CLc(13), CLc(0), 4.0, A.is_lt, -8192.0, A.mult)
    ts(CLc(14), CLc(0), 8.0, A.is_lt, -8192.0, A.mult)
    ts(CLc(15), CLc(0), 0.0, A.is_equal, 2.0 ** -17, A.mult)
    ts(CLc(16), CLc(11), 16.0, A.mult, CLc(10), A.add)
    ts(CLc(17), CLc(10), CLc(11), A.add, CLc(12), A.add)
    ts(CLc(18), CLc(12), 4096.0 - CEN, A.mult, CLc(16), A.add)
    ts(CLc(21), CLc(14), CLc(13), A.subtract)
    ts(CLc(19), CLc(18), CLc(13), A.add)
    for nm, src, f in (("WM", "B0", 16384.0), ("WN", "B0", -8192.0), ("WP", "B0", 8192.0), ("CI", "ID", KOFF), ("NI", "ID", -1.0), ("NJ", "ID", -1.0 / 128.0),
                       ("WA", "B0", CLc(19)), ("WA0", "B0", CLc(21)), ("W2", "B0", 2.0), ("WB", "B0", -1.0), ("P2", "ID", CLc(17))):
        act(R(nm), R(src), AF.Copy, scale=f)
    act(C("P2", 12, 128, 16), C("B0", 15, 128, 16), AF.Copy, scale=CLc(16))
    act(R("BF"), R("B0"), AF.Copy, scale=CLc(16))

    def stile(tau):
        cp(C("NF", 16, 272), C("SN", tau, 768, 3))
        tr(C("Y", 0, 256), C("NF", 16, 272))
        tr(C("Y", 256, 544), R("NF"))
        if tau:
            act(C("KS", L * tau, L * tau + L), IND(R("Y"), R("LMK")), AF.Identity, bias=-CEN)
            ts(C("SO", L * tau, L * tau + L), C("KS", L * tau, L * tau + L), CEN, A.add)
        else:
            cp(C("SO", 0, L), IND(R("Y"), R("LMK")))
            act(C("KS", 0, L), IND(R("Y"), R("LMK")), AF.Identity, bias=-CEN)

    def zexp(tau, m0=0, m1=16, q="G"):
        zg = "ZG2" if tau == 1 else "ZG"

        def f(o, a, n):
            if q == "G":
                asel(o, [[0, n]], A.is_ge, 0, 0, a)
            elif q == "V":
                cp(o, a)
            else:
                act(o, a, AF.Copy)
        ms_ = slice(m0, m1)
        f(R(zg, ms_, slice(0, 16)), C("ZS", tau + 48 * m0, 48 * m1, 3), 16 * (m1 - m0))
        for w in (16, 32, 64, 128):
            f(R(zg, ms_, slice(w, 2 * w)), R(zg, ms_, slice(0, w)), w * (m1 - m0))
        for a in range(m0, m1, 4):
            dma("Y", C("ZX1" if tau == 1 else "ZX0", L * a, L * a + 4 * L), R(zg, slice(a, a + 4), ALL), key=("zx", tau % 2, a))

    def maxz(out, o, win, so, tau, c, first=False):
        if first:
            for m in range(3, -1, -1):
                tt(C(out, o + L * m, o + L * m + L), IND(win, C("SO", so + 16 * m, so + 16 * m + 16)), R("ZG", 4 * c + m, ALL), A.max)
        else:
            tt(C(out, o, o + 1024), IND(win, C("SO", so, so + 64)), CH("ZX1" if tau == 1 else "ZX0", c), A.max)

    def ZX(tau, c, a=0, e=1024, r=None):
        return R("ZG2" if tau == 1 else "ZG", slice(4 * c + a // L, 4 * c + e // L), ALL if r is None else slice(r, L, 16))

    for tau in range(3):
        act(C("ZT", L * tau, L * tau + L), C("ZS", tau, 768, 3), AF.Copy)
    for m0, m1, q in OPT["ZG"]:
        zexp(0, m0, m1, q)
    zexp(1)
    cp(C("KF", 16, 80), R("KC"))
    tr(C("Y", 0, 64), C("KF", 16, 80))
    tr(C("Y", 256, 352), R("KF"))
    ms(C("Y", 64, 256), 0.0)
    cp(R("KO"), IND(C("Y", 0, 352), R("LK")))
    ts(C("KI", 0, 64), R("KC"), 15, A.bitwise_and)
    ts(C("KI", 64, 128), R("KC"), 4, A.arith_shift_right)
    cp(C("XKLO", 0, 128), R("KI"))
    dma("Y", R("KD", p=rows(8)), R("KLO"))
    dma("Y", R("KD", p=rows(9)), R("KHI"))
    dma("Y", R("KD", p=rows(11)), C("ONE", 0, 64))
    stile(0)
    act(R("VCB"), IND(R("VN"), R("KO")), AF.Copy)
    for hf in range(2):
        cols = lambda nm, o=0: C(nm, o + 512 * hf, o + 512 * hf + 512)
        mm(PS(4 + hf), M2, cols("VN"), True, False)
        mm(PS(4 + hf), R("P2"), cols("KD"), False, False)
        mm(PS(4 + hf), M1, cols("VCB"), False, True)
        act(cols("AUX", PAD), PS(4 + hf), AF.Copy)
    act(R("ZB"), R("ZS"), AF.Identity, bias=64.0)
    iota(R("KA"), [[0, 16], [-1, 16]], 15, 0)
    for a, b in ((PAD, PAD + T0), (PAD + T0, PAD + GB), (PAD + GB, WT)):
        iota(C("IO", a, b), [[1, b - a]], a, 0)
    ts(CLc(25), CLc(15), -float(PAD), A.mult, 64.0, A.add)
    act(C("VP", PAD, PAD + T0), C("IO", PAD, PAD + T0), AF.Identity, bias=CLc(25), scale=CLc(15))
    dma("G", C("VP", PAD, PAD + T0), R("vn"), add=True)
    dma("G", C("VC", PAD, PAD + T0), R("VCB"))

    def own_sum(tau, c, src):
        o = PS(DBANK[c % 2], 384, 448)
        for r in range(16):
            mm(o, Wr("WM", r), src(r), r == 0, False)
        mm(o, R("CI"), C("ONE", 0, 64), False, True)
        kn = C("KS", L * tau + 64 * c, L * tau + 64 * c + 64)
        tt(kn, o, kn, A.add)

    turn = [4, 5, 6, 0, 1]
    held = set()

    def next_bank(banks=(4, 5, 6)):
        b = [x for x in turn if x in banks and x not in held][0]
        turn.remove(b)
        turn.append(b)
        return b

    def own_dist(tau, c):
        src, s0, ab, a0 = ("XS", 1024 * c, "D1", 1024 * c) if tau == 0 else ("GA" if c % 2 == 0 else "VCB", 0, "GC", 0)
        so = L * tau + 64 * c
        if c not in OPT["OWNS"][tau]:
            maxz(src, s0, R("VN"), so, tau, c, tau == 0 and c in OPT["FIRST"][0])
            own_sum(tau, c, lambda r: C(src, s0 + r, s0 + 1024, 16))
            return
        for a in range(0, 1024, PG):
            act(C(src, s0 + a, s0 + a + PG), IND(R("VN"), C("SO", so + a // 16, so + (a + PG) // 16)), AF.Copy)
        for a in range(0, 1024, PA):
            b = next_bank()
            mm(PS(b, 0, PA), R("ID"), C(src, s0 + a, s0 + a + PA), True, False)
            mm(PS(b, 0, PA), R("NI"), ZX(tau, c, a, a + PA), False, True)
            act(C(ab, a0 + a, a0 + a + PA), PS(b, 0, PA), AF.Abs)
        o = PS(DBANK[c % 2], 384, 448)
        for r in range(16):
            mm(o, Wr("WP", r), ZX(tau, c, r=r), r == 0, False)
        mm(o, R("CI"), C("ONE", 0, 64), False, False)
        cut()
        for r in range(16):
            mm(o, Wr("WP", r), C(ab, a0 + r, a0 + 1024, 16), False, r == 15)
        kn = C("KS", so, so + 64)
        tt(kn, o, kn, A.add)

    for c in range(3, -1, -1):
        own_dist(0, c)
    ts(R("BC"), R("BC"), float(PAD), A.add)
    ts(C("BCI", 0, 48), R("BC"), 15, A.bitwise_and)
    ts(C("BCI", 48, 96), R("BC"), 4, A.arith_shift_right)
    cp(R("BCF"), R("BCI"))
    dma("Y", R("BR", p=rows(8)), C("BCF", 0, 48))
    dma("Y", R("BR", p=rows(9)), C("BCF", 48, 96))
    ms(R("RMIN"), 1.0)
    ms(C("RMIN", 0, 256, 16), BIG)
    act(R("RMAX"), R("RMIN"), AF.Copy, scale=-1.0)
    act(R("RL"), R("RMIN"), AF.Identity, bias=1.0, scale=-1.0)
    gfill(C("VP", 0, PAD), 1024)
    ms(C("QN", 0, 16), 0.0)
    ms(C("QN", 272, 288), 0.0)
    for hf in range(2):
        cp(C("QT", 512 * hf, 512 * hf + 512), C("NQ", 512 * hf, 512 * hf + 512))
    stile(1)
    ts(R("LM0"), C("TF", 0, 8), CLc(0), A.add)
    ts(R("REV"), C("TG", 0, 8), CLc(0), A.subtract, 15.0, A.add)
    iota(R("GID"), [[L, 4], [16, 16]], GB, 0)
    act(R("GID"), R("GID"), AF.Identity, bias=CLc(0))
    act(R("GK"), R("GID"), AF.Identity, bias=4096.0 - CEN)
    act(R("GID"), R("GID"), AF.Identity, bias=4096.0 - CEN - TOP)
    iota(R("TRI"), [[0, 8], [-16, 2], [1, 32]], 0, 0)
    act(R("I128"), R("ID"), AF.Copy, scale=128.0)
    for a in range(0, 16, 4):
        b = next_bank()
        for r in range(a, a + 4):
            mm(PS(b, 128 * (r - a), 128 * (r - a) + 128), Wr("WB", r), R("I128"), r == a, r == a + 3)
        act(C("FW", 128 * a, 128 * a + 512), PS(b), AF.Copy)
    iota(R("ILO"), [[1, 144]], 0, 0)
    ts(CLc(22), CLc(0), 9.0, A.mult, T0 / 16.0, A.add)
    act(R("IHI"), R("ONE"), AF.Copy, scale=CLc(22))
    dma("Y", R("IDB"), R("ZG", slice(7, 16), ALL))
    dma("Y", R("IDB", p=rows(8)), R("ILO"))
    dma("Y", C("QT", T0, GB), C("IO", T0, GB))
    dma("Y", C("VC", PAD + T0, WT), C("IO", PAD + T0, WT))
    for r in range(16):
        mm(PS(6, 0, 48), Wr("BF", r), C("BR", r, 768, 16), r == 0, r == 15)
    for r in range(16):
        mm(PS(7, 0, 48), Wr("B0", r), C("ZT", r, 768, 16), r == 0, r == 15)
    act(R("THR"), PS(7, 0, 48), AF.Identity, bias=200.0 * 8192.0 + KOFF - 4096.0, scale=8192.0)
    cp(R("BO"), PS(6, 0, 48))
    act(R("VB"), IND(C("VP", 0, PAD + T0), R("BO")), AF.Copy)
    dma("Y", R("IDB", p=rows(9)), R("IHI"))
    dma("Y", R("IDB", p=rows(11)), R("ONE"))
    dma("G", C("AUX", PAD + T0, WT), R("IDB"))
    dma("Y", C("AUX", PAD + T0, WT, p=rows(12)), C("IO", T0, W, p=rows(12)))
    ts(CLc(23), CLc(0), -2.0 ** 21, A.mult, 2.0 ** 20, A.add)
    act(R("TRI"), R("TRI"), AF.Relu, bias=CLc(23), scale=2.0 ** 21)
    ts(CLc(20), CLc(3), 2.0, A.mult, CLc(2), A.add)
    ts(C("LD", 0, 2), C("TG", 0, 2), 0.5, A.mult, CLc(20), A.add)
    ts(CLc(20), CLc(0), CLc(2), A.subtract, 0.5, A.mult)
    ts(C("LD", 2, 4), C("TG", 0, 2), 0.5, A.mult, CLc(20), A.add)
    gfill(R("RZ2"), 1)
    ms(C("RZ2", 0, 512, 32), 0.0)
    gfill(C("IO", 0, PAD), PAD - 1)
    dma("Y", C("VP", PAD + T0, PAD + GB), C("IO", PAD + T0, PAD + GB))
    act(R("PF"), C("FW", 128 * 11, 128 * 12), AF.Copy, scale=-0.5)
    ts(CLc(24), CLc(12), 64.0, A.mult)
    ts(CLc(24), CLc(16), 2.0 ** -17, A.mult, CLc(24), A.add)
    act(C("PF", 0, 128, 16), C("B0", 15, 128, 16), AF.Copy, scale=CLc(24))

    later = []
    for t in range(5):
        tau = TILE[t]
        wend = PAD + (T0 if t < 3 else GB + L * (t - 2))
        aend = PAD + (T0 if t == 0 else GB + L * t)
        own = PAD + T0 + L * t
        ld = L * (t - 1)
        gcol = PAD + GB + ld
        H = lambda nm, u, o=0: C(nm, o + 16 * UNITS[u][0], o + 16 * sum(UNITS[u]))
        M = lambda nm, u: C(nm, UNITS[u][0], sum(UNITS[u]))
        last = lambda nm: C(nm, 15, 256, 16)
        for c in range(3, -1, -1):
            so = C("SO", L * tau + 64 * c, L * tau + 64 * c + 64)
            begin(t, "child%d" % c)
            act(CH("XA", c), IND(C("AUX", PAD, wend), so), AF.Copy)
            maxz("XM", 1024 * c, R("VCB") if t == 0 else C("VC", PAD, wend), L * tau + 64 * c, tau, c, t == 0 and c in OPT["FIRST"][1])
            if c == 0 and later:
                begin(t, "lists%d" % (t in (2, 3)))
                later.pop()(after=len(ops) - 1)
            if t < 3 and c not in OPT["OWNS"].get(t, ()):
                begin(t, "own%d" % c)
                o = PS(DBANK[c % 2], 0, 64)
                for r in range(16):
                    mm(o, Wr("WA0", r), CH("XA", c, r, 16), r == 0, r == 15)
                kn = C("KS", L * tau + 64 * c, L * tau + 64 * c + 64)
                tt(kn, o, kn, A.add)
            begin(t, "keys%d" % c)
            o = PS(0, 64 * c, 64 * c + 64)
            for r in range(16):
                mm(o, Wr("WM", r), CH("XM", c, r, 16), r == 0, False)
            cut()
            for r in range(16):
                mm(o, Wr("WA", r), CH("XA", c, r, 16), False, False)
            mm(o, R("CI"), C("ONE", 0, 64), False, True)
        begin(t, "guests")
        if t >= 1:
            for src, col0 in (("YV", own - L), ("LAND", gcol)):
                b = next_bank()
                mm(PS(b, 0, L), R("PF"), C("IDB", col0 - PAD - T0, col0 - PAD - T0 + L), True, False)
                cut()
                mm(PS(b, 0, L), R("ID"), C(src, ld, ld + L), False, True)
                act(C("VP", col0, col0 + L), PS(b, 0, L), AF.Copy)
            tt(R("XG"), C("LAND", ld, ld + L), C("ZT", L * tau, L * tau + L), A.max)
            o = R("PS3", 16, ALL)
            for r in range(16):
                mm(o, Wr("WN", r), C("LAND", ld + r, ld + L, 16), r == 0, False)
            cut()
            for r in range(16):
                mm(o, Wr("WM", r), C("XG", r, L, 16), False, False)
            mm(o, R("CI"), C("ONE", 0, 16), False, True)
            tt(R("KM"), o, C("GK", 16 * t - 16, 16 * t), A.add)
        begin(t, "parent")
        k2, dp = PS(0, L, 2 * L), PS(1, 0, L)
        tt(k2, PS(0, 0, L), C("KS", L * tau, L * tau + L), A.min)
        ops[-1]["key"] = "mark1"
        ts(dp, k2, MAGIC, A.add, MAGIC, A.subtract)
        scan(R("SMN"), R("RMIN"), dp, A.add, A.min)
        tt(R("NM"), R("SMN"), dp, A.not_equal)
        scan(R("SM2"), R("NM"), k2, A.mult, A.min)
        if t >= 1:
            scan(R("SMX"), R("RMAX"), dp, A.add, A.max)
            ts(R("S3"), last("SMX"), -1.0, A.mult)
            ts(R("S2"), R("S3"), 15, A.bitwise_and)
            ts(R("GD"), last("SMX"), MAGIC, A.add, MAGIC, A.subtract)
            tt(R("YG"), last("SMN"), R("PS3", 16, ALL), A.subtract)
            tt(R("YG"), R("YG"), last("SMX"), A.add)
            tt(R("GW"), R("GD"), R("YG"), A.is_lt)
            tt(R("GW"), R("GW"), C("GID", 16 * t - 16, 16 * t), A.mult)
            tt(R("S1"), last("SM2"), R("GW"), A.min)
        else:
            cp(R("S1"), last("SM2"))
        begin(t, "rows")
        ts(R("AI"), R("S1"), 4095, A.bitwise_and)
        ts(R("A16"), R("AI"), CEN - 4096.0, A.add)
        act(C("QN", 16, 272), IND(C("QT", 0, aend - PAD), R("A16")), AF.Copy)
        for va, sc in (("NVA", -1.0), ("VAF", 1.0)):
            for h, (m0, nm) in enumerate(UNITS):
                act(C(va, 512 * h, 512 * h + 16 * nm), IND(C("VP", PAD, aend), M("A16", h)), AF.Copy, scale=sc)
                how = OPT["COPY"][va][h]
                for w in (64, 128, 256):
                    if w < 16 * nm or (how in "YZ" and w >= 128) or how == "N":
                        continue
                    o, a = C(va, 512 * h + w, 512 * h + 2 * w), C(va, 512 * h, 512 * h + w)
                    if how in "VZ":
                        cp(o, a)
                    elif how in "SY":
                        act(o, a, AF.Copy)
                    else:
                        asel(o, [[0, w]], A.is_ge, 0, 0, a)
                for j in range(1, 4) if how in "YZ" else ():
                    dma("Y", C(va, 512 * h + 128 * j, 512 * h + 128 * j + 128), C(va, 512 * h, 512 * h + 128), key=(va, h, j))
        tr(C("Y", 0, 256), C("QN", 16, 272))
        tr(C("Y", 256, 544), R("QN"))
        for a, e in OPT["QO"]:
            cp(C("QO", 16 * a, 16 * e), IND(R("Y"), C("LKM", a, e)))
        begin(t, "put")
        if t >= 1:
            tt(R("E"), IND(R("S2"), R("LB")), R("KA"), A.is_equal)
            tt(R("E2"), IND(R("KM"), R("LB")), R("E"), A.mult)
            tt(R("K3"), k2, R("E2"), A.min)
            k3 = R("K3")
        else:
            k3 = k2
        begin(t, "live")
        scan(R("SMX"), R("RL"), k3, A.add, A.max)
        ts(R("U"), R("AI"), PAD + CEN - 4096.0, A.add)
        tt(R("LV"), last("SMX"), C("THR", 16 * tau, 16 * tau + 16), A.is_ge)
        tt(R("U"), R("U"), R("LV"), A.mult)
        tt(R("AD"), R("U"), R("LI"), A.max)
        cp(R("AD16"), R("AD"))
        act(C("VB", tau, 768, 3), IND(C("VP", 0, aend), R("AD16")), AF.Copy)
        ops[-1]["key"] = "mark0"
        begin(t, "once%d" % t)
        if t == 0:
            ts(R("SI"), k3, CEN, A.add, TOP, A.add)
        begin(t, "best")
        if t in (0, 3, 4):
            act(C("YB", tau, 768, 3), IND(C("IO", 0, aend), R("AD16")), AF.Identity, bias=-float(PAD))
        begin(t, "tables")
        if t in (1, 2):
            po = own - L
            gs = GB - T0 + ld
            land = C("LAND", ld, ld + L)
            dma("G", C("VC", po, po + L), C("YV", L * (t - 1), L * t))
            dma("Y", C("AUX", po, po + L), C("AXN", 0, L))
            dma("G", C("VC", gcol, gcol + L), land)
            b = next_bank()
            mm(PS(b, 0, L), M1, land, True, False)
            mm(PS(b, 0, L), R("P2"), C("IDB", gs, gs + L), False, True)
            act(C("AUX", gcol, gcol + L), PS(b, 0, L), AF.Copy)
        begin(t, "send")
        if t < 4:
            hand_on(t, C("QN", 16, 272), qslot(T, t), C("QT", GB + L * t, GB + L * t + L), "aq%d" % t)
            dma("Y", C("QT", own - PAD, own - PAD + L), C("QN", 16, 272))
        begin(t, "tile")
        if t == 0:
            zexp(2)
            stile(2)
        begin(t, "ends")
        for u, (m0, nm) in enumerate(UNITS):
            act(H("VA", u), C("NVA", 512 * u, 512 * u + 16 * nm), AF.Identity, bias=-64.0, scale=-1.0)
        ts(R("LO"), R("VA"), -2.0, A.add, 0.0, A.max)
        ts(R("HI"), R("VA"), 2.0, A.add, 63.0, A.min)

        def lists(t=t, tau=tau, aend=aend, after=None):
            if t:
                ts(R("SI"), R("K3"), CEN, A.add, TOP, A.add)
                ops[-1]["after"] = after
            ts(R("SI2"), R("SI"), 4095, A.bitwise_and)
            ops[-1]["after"] = after
            if t in (1, 2):
                cp(C("SO", L * tau, L * tau + L), R("SI2"))
                ts(R("SI"), R("SI"), 2 ** 24 - 1 - 4096, A.bitwise_and)
                ts(C("KS", L * tau, L * tau + L), R("SI"), -TOP, A.add, -CEN, A.add)
            else:
                ts(C("E", 0, 128), IND(C("SI2", 128, 256), R("REV")), 4096.0, A.mult)
                tt(C("NF", 16, 144), IND(C("SI2", 0, 128), R("REV")), C("E", 0, 128), A.add)
                tr(C("Y", 0, 128), C("NF", 16, 144))
                tr(C("Y", 256, 416), C("NF", 0, 160))
                act(C("YS", tau, 384, 3), IND(R("Y"), R("LM0")), AF.Copy)
            if t == 4:
                dma("Y", R("ys"), R("YS"))
                dma("Y", R("yb"), R("YB", p=rows(0)))

        def lowest():
            ts(R("ADH"), IND(R("AD"), R("LD")), -1792.0, A.add)
            ub = next_bank([b for b in SBANK if b < 2])
            mm(PS(ub), R("ID"), R("TRI"), True, False)
            cut()
            for r in range(16):
                mm(C("PS%d" % ub, r, 512, 16), R("I128"), C("ADH", 32, 64), False, False)
                mm(C("PS%d" % ub, r, 512, 16), C("FW", 128 * r, 128 * r + 128), C("ADH", 0, 32), False, r == 15)
            if OPT["EQ"][t] == "V":
                ts(R("EQ"), PS(ub), 0.0, A.is_equal, 4096.0, A.mult)
            else:
                act(R("EQ"), PS(ub), AF.Abs)
                act(R("EQ"), R("EQ"), AF.Relu, bias=4096.0, scale=-4096.0)
            scan(R("EQS"), R("RZ2"), R("EQ"), A.mult, A.max)
            tt(R("U2"), R("AD"), C("EQS", 31, 512, 32), A.subtract)
            tt(R("U2"), R("U2"), R("LI"), A.max)
            cp(R("O1"), R("U2"))
            if t == 4:
                ub = next_bank()
                mm(PS(ub, 0, L), R("P2"), C("IDB", L * t, L * t + L), True, True)
                act(C("AXN", L, 2 * L), PS(ub, 0, L), AF.Copy)
                for b in range(7, -1, -1):
                    cp(IND(R("AUX"), C("O1", 2 * b, 2 * b + 2)), C("AXN", L + 32 * b, L + 32 * b + 32))
                dma("Y", R("yk"), C("AUX", PAD, WT, p=rows(12)))

        sized, picked, sbank = set(), set(), {}

        def gather(u, x, j, how):
            win, va, f = ("ZB", "NVA", A.add) if x == 1 else ("VB", "VAF", A.subtract)
            m0 = UNITS[u][0]
            d, q = C("D%d" % x, 256 * m0 + 512 * j, 256 * m0 + 512 * j + 512), C("QO", 16 * m0 + 32 * j, 16 * m0 + 32 * j + 32)
            if how == "T":
                nl = 16 * UNITS[u][1]
                act(d, IND(R(win), q), AF.Copy)
                ub = next_bank(SBANK)
                mm(PS(ub), R("ID"), d, True, False)
                for a in range(0, 512, nl):
                    mm(PS(ub, a, a + nl), R("ID"), C(va, 512 * u, 512 * u + nl), False, a + nl == 512)
                act(C("A1", 256 * m0 + 512 * j, 256 * m0 + 512 * j + 512), PS(ub), AF.Abs)
                act(R("SG", slice(16 * m0 + 32 * j, 16 * m0 + 32 * j + 32), ALL), PS(ub), AF.Sign)
                picked.add(u)
            elif how == "D":
                act(d, IND(R(win), q), AF.Copy)
                dma("G", d, C(va, 512 * u, 512 * u + 512), add=True, key=("sd", u, j))
            else:
                tt(d, IND(R(win), q), C(va, 512 * u, 512 * u + 512), f)

        def size(u, x, c, how):
            d, ab, b = "D%d" % x, "A%d" % x, UBANK[u]
            ch = UNITS[u][0] // 4 + c
            o = PS(b, 128 * x - 128 + 64 * c, 128 * x - 64 + 64 * c)
            if how == "V":
                for a in (1024 * ch, 1024 * ch + 512):
                    ts(C(ab, a, a + 512), C(d, a, a + 512), 0.0, A.max, 64.0, A.min)
                for r in range(16):
                    mm(o, Wr("WB", r), CH(d, ch, r, 16), r == 0, False)
                cut()
            elif how == "S":
                act(CH(ab, ch), CH(d, ch), AF.Abs)
                sized.add((u, x))
            for r in range(16):
                mm(o, Wr("W2" if how == "V" else "B0", r), CH(ab, ch, r, 16), r == 0 and how != "V", r == 15)
            if x == 1 and c == UNITS[u][1] // 4 - 1:
                act(H("D1M", u), PS(b, 0, 16 * UNITS[u][1]), AF.Identity, bias=-0.5)

        def early(u, c):
            a = 16 * UNITS[u][0] + 64 * c
            act(R("SG", slice(a, a + 64), ALL), C("D1", 16 * a, 16 * a + 1024), AF.Sign)
            picked.add(u)

        def attract(u):
            d2 = PS(UBANK[u], 128, 128 + 16 * UNITS[u][1])
            if u in picked:
                tt(H("N1", u), H("D1M", u), d2, A.is_le)
                ts(H("N2", u), d2, 0.0, A.is_equal)
                if (u, 2) in sized:
                    ts(H("N3", u), d2, 1100.0, A.is_le)
                    tt(H("N1", u), H("N1", u), H("N3", u), A.mult)
                tt(H("NA", u), H("N1", u), H("N2", u), A.max)
                return
            tt(H("N1", u), H("D1M", u), d2, A.is_gt)
            ts(H("N2", u), d2, 0.0, A.not_equal)
            if (u, 2) in sized:
                ts(H("N3", u), d2, 1100.0, A.is_gt)
                tt(H("N1", u), H("N1", u), H("N3", u), A.add)
            tt(H("NA", u), H("N1", u), H("N2", u), A.mult)

        def col(ub, r, nr):
            r %= nr
            return R("PS%d" % ub, slice(r // 4, 128, nr // 4), r % 4) if ub in (4, 5, 6) else C("PS%d" % ub, r, 512, nr)

        def ahead(u, rc):
            m0, nm = UNITS[u]
            nr = 32 // nm
            ub = sbank[u, rc] = next_bank(SBANK)
            held.add(ub)
            for r in range(nr * rc, nr * rc + nr):
                mm(col(ub, r, nr), R("ID"), C("D1", 256 * m0 + r, 256 * (m0 + nm), 16), r % nr == 0, False)
            cut()

        def sign(u, rc, how):
            m0, nm = UNITS[u]
            nr = 32 // nm
            ub = next_bank(SBANK) if how == "M" else sbank[u, rc]
            held.discard(ub)
            for r in range(nr * rc, nr * rc + nr):
                mm(col(ub, r, nr), C("FW", 128 * r, 128 * r + 128), H("NA", u), how == "M" and r % nr == 0, r % nr == nr - 1)
            sg = R("SG", slice(16 * m0, 16 * (m0 + nm)), slice(nr * rc, nr * rc + nr))
            if how == "M":
                tt(sg, PS(ub), sg, A.mult)
            elif how == "V":
                ts(sg, PS(ub), -1.0, A.max, 1.0, A.min)
            else:
                act(sg, PS(ub), AF.Sign)

        def sums(u, rs=ALL):
            m0, nm = UNITS[u]
            if nm == 8:
                return R("PS3", slice(m0, m0 + nm), rs)
            return PS(UBANK[u], 256, 320) if rs == ALL else C("PS%d" % UBANK[u], 256 + rs, 320, 16)

        def count(u, how):
            m0, nm = UNITS[u]
            if how == "M":
                mm(sums(u), R("ID"), H("VA", u), True, False)
                cut()
                return
            if how == "V":
                src, a, o = "NA", 16 * m0, 0
                for w in (8 * nm, 4 * nm, 2 * nm, nm):
                    tt(C("NT", o, o + w), C(src, a, a + w), C(src, a + w, a + 2 * w), A.add)
                    src, a, o = "NT", o, o + w
                ts(M("CN", u), C("NT", a, a + nm), -1.0 / 128.0, A.mult)
            else:
                for k in range(16):
                    mm(PS(UBANK[u], 0, nm), R("ID"), C("NA", 16 * m0 + nm * k, 16 * m0 + nm * k + nm), k == 0, k == 15)
                act(M("CN", u), PS(UBANK[u], 0, nm), AF.Identity, scale=-1.0 / 128.0)
            mm(sums(u), R("ID"), H("VA", u), True, False)
            cut()
            for r in range(16):
                mm(sums(u, r), C("FW", 128 * r, 128 * r + 128), M("CN", u), False, False)
            cut()

        def pull(u, c):
            m0, nm = UNITS[u]
            rc = slice(8 * c, 8 * c + 8) if nm == 8 else ALL
            for k in range(16):
                mm(sums(u, rc), R("NJ" if u in picked else "ID"), R("SG", slice(16 * m0 + nm * k, 16 * m0 + nm * k + nm), rc), False, c == nm // 4 - 1 and k == 15)
            cut()

        def finish(u):
            m0, nm = UNITS[u]
            tt(H("H1", u), sums(u), H("HI", u), A.min)
            tt(H("YV", u, L * t), H("H1", u), H("LO", u), A.max)
            if t == 4:
                dma("Y", H("yv", u, L * t), H("YV", u, L * t))
                return
            for j, (a, e) in enumerate(SENDS):
                if a == 16 * m0:
                    hand_on(t, C("YV", L * t + a, L * t + e), nslot(T, t, j), C("LAND", L * t + a, L * t + e), "an%d" % (2 * t + j))
            o = PS(UBANK[u], 320, 320 + 16 * nm)
            mm(o, R("P2"), H("IDB", u, L * t), True, False)
            if t < 2:
                mm(o, M2, H("VA", u), False, False)
            cut()
            mm(o, M1, H("YV", u, L * t), False, True)
            act(H("AXN", u), o, AF.Copy)
            for bl in range((m0 + nm) // 2 - 1, m0 // 2 - 1, -1):
                cp(IND(R("VC"), C("O1", 2 * bl, 2 * bl + 2)), C("YV", L * t + 32 * bl, L * t + 32 * bl + 32))
                cp(IND(R("AUX"), C("O1", 2 * bl, 2 * bl + 2)), C("AXN", 32 * bl, 32 * bl + 32))

        steps = {"e": early, "g": gather, "z": size, "a": attract, "i": ahead, "s": sign, "c": count, "p": pull, "f": finish, "l": lists if t == 4 or not OPT["LATER"] else lambda: later.append(lists), "d": lowest,
                 "o": lambda c: own_dist(t + 1, c) if t < 2 else None}
        for w in OPT["STEP4"][t].split():
            begin(t, w)
            steps[w[0]](*[int(x) if x.isdigit() else x for x in w[1:]])
        begin(t, "out")
        new = C("YV", L * t, L * t + L)
        if t < 4:
            dma("Y", C("yv", L * t, L * t + L), new)

    if "seq" not in ORDER:
        ORDER["seq"], ORDER["wait"] = plan_calls(ops)
    sems = {}
    for i, o in enumerate(ops):
        for j in ORDER["wait"][i]:
            ops[j]["inc"] = True
        if o["dma"]:
            s = sems.setdefault(o["key"] or i, ["d%d" % len(sems), 0])
            s[1] += abs(o["dma"])
            o["sem"] = (s[0], s[1])
        elif o["ext"]:
            o["sem"] = o["ext"]
    for q in Q:
        cnt = 0
        for i in ORDER["seq"][q]:
            if ops[i]["inc"] and not ops[i]["dma"]:
                cnt += 1
                ops[i]["sem"] = ("c" + q, cnt)
    for q in Q:
        for i in ORDER["seq"][q]:
            o = ops[i]
            for j in ORDER["wait"][i]:
                Q[q].wait_ge(T.sem[ops[j]["sem"][0]], ops[j]["sem"][1])
            if o["dma"] < 0:
                o["fn"](Q[q], T.sem[o["sem"][0]])
            elif o["dma"]:
                o["fn"](Q[q]).then_inc(T.sem[o["sem"][0]], 16)
            else:
                ins = o["fn"](Q[q])
                if o["inc"]:
                    ins.then_inc(T.sem["c" + q], 1)
    for o in ops:
        if (o["dma"] or o["ext"]) and not o["inc"]:
            g.sync.wait_ge(T.sem[o["sem"][0]], o["sem"][1])
